import numpy as np
import ml_dtypes


def mxq(x, axis, fmt="e4m3"):
    dtype, down = {"e4m3": (ml_dtypes.float8_e4m3fn, 7), "e5m2": (ml_dtypes.float8_e5m2, 14)}[fmt]
    v = np.moveaxis(np.asarray(x, np.float32).astype(ml_dtypes.bfloat16).astype(np.float64), axis, -1)
    blocks = v.reshape(v.shape[:-1] + (-1, 32))
    amax = np.abs(blocks).max(-1, keepdims=True)
    byte = np.maximum(np.where(amax > 0, np.frexp(amax)[1] - 1 + 127, 0) - down, 1)
    scale = np.exp2(byte - 127.0)
    codes = (blocks / scale).astype(np.float32).astype(dtype).astype(np.float64)
    return np.moveaxis((codes * scale).reshape(v.shape), -1, axis)


WIDE = False


def mx_kscale(k):
    if not WIDE:
        return np.ones(k)
    levels = np.array([30, -30])
    if k % 512:
        return np.exp2(np.random.permutation(np.resize(levels, k // 32))).repeat(32)
    a = np.empty((k // 512, 16))
    for p in range(k // 512):
        a[p, :8] = np.random.permutation(np.resize(levels, 8))
        for g in range(8):
            far = levels[np.abs(levels - a[p, g]) >= 10]
            a[p, g + 8] = far[np.random.randint(len(far))]
    return np.exp2(a.ravel()).repeat(32)


def f64(x):
    return np.asarray(x).astype(np.float64)


def striped(idx):
    return np.tile(idx.reshape(-1, 16).T, (8, 1)).astype(np.uint16)


def unstriped(offs):
    return offs[:16].T.reshape(-1).astype(np.int64)


E2M1 = np.array([0.0, 0.5, 1.0, 1.5, 2.0, 3.0, 4.0, 6.0, -0.0, -0.5, -1.0, -1.5, -2.0, -3.0, -4.0, -6.0])


def pack_weight(w, fmt):
    k, n = w.shape
    w = f64(np.asarray(w, np.float32).astype(ml_dtypes.bfloat16)).reshape(k // 32, 32, n)
    amax = np.abs(w).max(1)
    if fmt == "e4m3":
        byte = np.frexp(amax)[1] - 1 + 127 - 7
    else:
        mant, ex = np.frexp(amax / 6.0)
        byte = np.where(mant > 0.5, ex, ex - 1) + 127
    byte = np.clip(np.where(amax > 0, byte, 1), 1, 254)
    scaled = (w * np.exp2(127.0 - byte)[:, None, :]).reshape(k, n).astype(np.float32)
    by_word = np.ascontiguousarray(scaled.reshape(k // 512, 128, 4, n).transpose(0, 1, 3, 2))
    if fmt == "e4m3":
        words = by_word.astype(ml_dtypes.float8_e4m3fn).view(np.uint8)
    else:
        c = by_word.astype(ml_dtypes.float4_e2m1fn).view(np.uint8) & 0xF
        words = (c[..., 0::2] | (c[..., 1::2] << 4)).reshape(k // 512, 128, 2 * n)
    return np.ascontiguousarray(words), np.ascontiguousarray(byte.astype(np.uint8).reshape(k // 512, 16, n))


def unpack_weight(words, scales, fmt):
    g, _, n = scales.shape
    words = np.ascontiguousarray(words).reshape(g, 128, n, -1)
    if fmt == "e4m3":
        vals = words.view(ml_dtypes.float8_e4m3fn).astype(np.float64)
    else:
        nib = np.empty((g, 128, n, 4), np.uint8)
        nib[..., 0::2] = words & 0xF
        nib[..., 1::2] = words >> 4
        vals = E2M1[nib]
    vals = vals * np.repeat(np.exp2(scales.astype(np.float64) - 127.0), 8, axis=1)[..., None]
    return vals.transpose(0, 1, 3, 2).reshape(g * 512, n)


def relu(v):
    return np.maximum(v, 0.0)


def d_relu(v):
    return (v > 0).astype(np.float64)


K, T, E, C, H, N = 256, 1024, 4, 512, 1024, 512


def by_expert(wq, xq):
    return np.concatenate([wq[e].T @ xq[:, e * C:(e + 1) * C] for e in range(E)], axis=1)


def setup_inputs():
    n = np.random.standard_normal
    s = mx_kscale(N)[:, None]
    u = mx_kscale(H)
    first = np.random.permutation(np.repeat(np.arange(E), T // E))
    second = (first + 1 + np.random.permutation(np.repeat(np.arange(E - 1), -(-T // (E - 1)))[:T])) % E
    while np.bincount(second, minlength=E).max() != T // E:
        load = np.bincount(second, minlength=E); hi, lo = int(load.argmax()), int(load.argmin())
        t = np.flatnonzero((second == hi) & (first != lo))[0]; second[t] = lo
    slot_token = np.empty(E * C, np.int64); pos = np.empty((2, T), np.int64); fill = np.zeros(E, np.int64)
    place = np.stack([np.random.permutation(C) for _ in range(E)])
    for r, deal in enumerate((first, second)):
        for t in np.random.permutation(T):
            e = deal[t]; j = e * C + place[e, fill[e]]; fill[e] += 1; slot_token[j] = t; pos[r, t] = j
    g = np.random.uniform(0.2, 0.8, T)
    w_slot = np.empty(E * C); w_slot[pos[0]] = g; w_slot[pos[1]] = 1.0 - g
    w2 = [pack_weight(m, "e2m1") for m in n((E, N, H)) / np.sqrt(N) / s[None] * u[None, None, :]]
    w1 = [pack_weight(m, "e2m1") for m in n((E, H, K)) / np.sqrt(H) / u[None, :, None]]
    w3 = [pack_weight(m, "e2m1") for m in n((E, H, K)) / np.sqrt(H) / u[None, :, None]]
    return {
        "dyT": (n((N, T)) * s).astype(np.float32),
        "a1": n((H, E * C)).astype(np.float32),
        "a3": n((H, E * C)).astype(np.float32),
        "w2_words": np.stack([m[0] for m in w2]),
        "w2_scales": np.stack([m[1] for m in w2]),
        "w1_words": np.stack([m[0] for m in w1]),
        "w1_scales": np.stack([m[1] for m in w1]),
        "w3_words": np.stack([m[0] for m in w3]),
        "w3_scales": np.stack([m[1] for m in w3]),
        "gate": np.tile(w_slot, (N, 1)).astype(np.float32),
        "offs": striped(slot_token),
        "pos1": striped(pos[0]),
        "pos2": striped(pos[1]),
    }


def reference(dyT, a1, a3, w2_words, w2_scales, w1_words, w1_scales, w3_words, w3_scales, gate, offs, pos1, pos2):
    idx = unstriped(offs)
    w2 = np.stack([unpack_weight(w2_words[e], w2_scales[e], "e2m1") for e in range(E)])
    w1 = np.stack([unpack_weight(w1_words[e], w1_scales[e], "e2m1") for e in range(E)])
    w3 = np.stack([unpack_weight(w3_words[e], w3_scales[e], "e2m1") for e in range(E)])
    gq = mxq(f64(gate) * f64(dyT)[:, idx], 0, "e5m2")
    dh = by_expert(w2, gq)
    da1 = dh * f64(a3) * d_relu(f64(a1))
    da3 = dh * relu(f64(a1))
    dx = by_expert(w1, mxq(da1, 0, "e5m2")) + by_expert(w3, mxq(da3, 0, "e5m2"))
    return dx[:, unstriped(pos1)] + dx[:, unstriped(pos2)]

@@ -1,0 +1,256 @@
+from contextlib import ExitStack
+
+import concourse.mybir as mybir
+from concourse.masks import make_identity
+
+K, T, E, C, H, N = 256, 1024, 4, 512, 1024, 512
+S = E * C
+P = 128
+X4 = 4
+NG = H // 512
+SB = C // P
+KB = K // P
+
+F32 = mybir.dt.float32
+BF16 = mybir.dt.bfloat16
+U32 = mybir.dt.uint32
+I32 = mybir.dt.int32
+U16 = mybir.dt.uint16
+U8 = mybir.dt.uint8
+E5M2 = mybir.dt.float8_e5m2_x4
+E2M1 = mybir.dt.float4_e2m1fn_x4
+ALU = mybir.AluOpType
+ACT = mybir.ActivationFunctionType
+
+FLOPS = 2 * S * N * H + 2 * 2 * S * H * K
+BYTES = 4 * (N * T + 2 * H * S + S + K * T) + E * (N * H + 2 * H * K) // 2 + E * (N * H + 2 * H * K) // 32 + 2 * 128 * 256
+
+
+def by_lines(planes):
+    return planes.rearrange("p t (c i) -> p c t i", i=4)
+
+
+def interleaved(flat):
+    return flat.rearrange("p (c i t) -> p c t i", i=4, t=X4)
+
+
+def tile_moe_bdx_glu_relu_kernel(
+    tc, dyT, a1, a3, w2_words, w2_scales, w1_words, w1_scales, w3_words, w3_scales, gate, offs, pos1, pos2, out
+):
+    nc = tc.nc
+    with ExitStack() as ctx:
+        held = ctx.enter_context(tc.tile_pool(name="held", bufs=1))
+        saved = ctx.enter_context(tc.tile_pool(name="saved", bufs=4))
+        ring = ctx.enter_context(tc.tile_pool(name="ring", bufs=2))
+        turn = ctx.enter_context(tc.tile_pool(name="turn", bufs=8))
+        mid = ctx.enter_context(tc.tile_pool(name="mid", bufs=3))
+        pa = ctx.enter_context(tc.psum_pool(name="pa", bufs=3))
+        pb = ctx.enter_context(tc.psum_pool(name="pb", bufs=3))
+        pc = ctx.enter_context(tc.psum_pool(name="pc", bufs=1))
+
+        offs_sb = held.tile([P, S // 16], U16, name="offs_sb")
+        pos1_sb = held.tile([P, T // 16], U16, name="pos1_sb")
+        pos2_sb = held.tile([P, T // 16], U16, name="pos2_sb")
+        w2_sc = held.tile([P, E, H], U8, name="w2_sc", align_bytes=64)
+        w1_sc = held.tile([P, E * NG, K], U8, name="w1_sc", align_bytes=64)
+        w3_sc = held.tile([P, E * NG, K], U8, name="w3_sc", align_bytes=64)
+        ident = held.tile([P, P], F32, name="ident")
+        for plane in (w2_sc, w1_sc, w3_sc):
+            nc.vector.memset(plane[:].rearrange("p e i -> p (e i)").bitcast(I32), 0)
+        make_identity(nc, ident[:])
+
+        nc.sync.dma_start(offs_sb[:], offs)
+        dy_rows = dyT.rearrange("(p t) s -> t p s", t=X4)
+        dy = []
+        gates = []
+
+        def load_gate(e):
+            gate_e = held.tile([P, C], F32, name=f"gate{e}")
+            nc.sync.dma_start(gate_e[:], gate[0:P, C * e : C * (e + 1)])
+            gates.append(gate_e)
+
+        for t in range(X4):
+            dy_t = held.tile([P, T], F32, name=f"dy{t}")
+            nc.sync.dma_start(dy_t[:], dy_rows[t])
+            dy.append(dy_t)
+            if t == 0:
+                load_gate(0)
+
+        w2_w = []
+
+        def load_w2(e):
+            w = held.tile([P, 2 * H], U8, name=f"w2_{e}", align_bytes=64)
+            nc.sync.dma_start(w[:].bitcast(I32), w2_words[e, 0].bitcast(I32))
+            w2_w.append(w)
+
+        def load_scales(queue, plane, scales):
+            by_row = scales.bitcast(I32).rearrange("e s f i -> f (e s) i")
+            for q in range(4):
+                queue.dma_start(plane[32 * q : 32 * q + 4].bitcast(I32), by_row[4 * q : 4 * q + 4])
+
+        a_tiles = {}
+
+        def load_a(which, e, g):
+            rows = slice(512 * g, 512 * g + 512)
+            cols = slice(C * e, C * e + C)
+            tile_a = saved.tile([P, X4, C], F32, name=f"a{which}_t")
+            nc.sync.dma_start(tile_a[:], (a1 if which == 1 else a3)[rows, cols].rearrange("(p t) s -> p t s", t=X4))
+            a_tiles[which, e, g] = tile_a
+
+        load_scales(nc.sync, w2_sc, w2_scales)
+        load_w2(0)
+        load_a(1, 0, 0)
+        load_gate(1)
+        load_a(1, 0, 1)
+        load_a(3, 0, 0)
+        load_w2(1)
+        load_a(3, 0, 1)
+        load_scales(nc.sync, w1_sc, w1_scales)
+        load_scales(nc.sync, w3_sc, w3_scales)
+        load_gate(2)
+        load_gate(3)
+        w1_w = held.tile([P, E * NG, 2 * K], U8, name="w1_w", align_bytes=64)
+        nc.sync.dma_start(w1_w[:].bitcast(I32), w1_words.bitcast(I32).rearrange("e s p k -> p (e s) k"))
+        w3_w = held.tile([P, E * NG, 2 * K], U8, name="w3_w", align_bytes=64)
+        nc.sync.dma_start(w3_w[:].bitcast(I32), w3_words.bitcast(I32).rearrange("e s p k -> p (e s) k"))
+        for g in range(NG):
+            load_a(1, 1, g)
+            load_a(3, 1, g)
+        load_w2(2)
+        load_w2(3)
+        nc.sync.dma_start(pos1_sb[:], pos1)
+        nc.sync.dma_start(pos2_sb[:], pos2)
+
+        dx = [held.tile([P, S], F32, name=f"dx{kb}") for kb in range(KB)]
+
+        g_planes = {}
+        g_codes = {}
+        turned_in = {}
+        steps_1 = {}
+
+        def gather(e):
+            g4 = ring.tile([P, X4, C], F32, name="g4")
+            for t in range(X4):
+                nc.vector.tensor_tensor(
+                    g4[:, t, :], dy[t][:].indirect(offs_sb[:, (C // 16) * e : (C // 16) * (e + 1)]), gates[e][:], ALU.mult
+                )
+            g_planes[e] = g4
+
+        def quantise_g(e, step):
+            words = ring.tile([P, C], U32, name="g_words", align_bytes=64)
+            scales = ring.tile([P, C], U8, name="g_scales", align_bytes=64)
+            for s in range(0, C, step):
+                gb = mid.tile([P, X4 * 256], BF16, name="gb", align_bytes=64, bufs=2)
+                run = gb[:, : X4 * step]
+                nc.scalar.copy(interleaved(run), by_lines(g_planes[e][:, :, s : s + step]))
+                nc.vector.quantize_mx(out=words[:, s : s + step].bitcast(E5M2), scales=scales[:, s : s + step], in_=run)
+            g_codes[e] = (words, scales)
+
+        order = [(g, s) for g in range(NG) for s in range(SB)]
+
+        def first_product(e):
+            words, scales = g_codes[e]
+            for g, s in order:
+                bank = pa.tile([P, 512], F32, name="dh_bank")
+                nc.tensor.matmul_mx(
+                    out=bank[:],
+                    lhsT=words[:, P * s : P * s + P].bitcast(E5M2),
+                    lhsT_scale=scales[:, P * s : P * s + P],
+                    rhs=w2_w[e][:, 1024 * g : 1024 * g + 1024].bitcast(E2M1),
+                    rhs_scale=w2_sc[:, e, 512 * g : 512 * g + 512],
+                    start=True,
+                    stop=True,
+                )
+                dht = turn.tile([P, X4, P], F32, name="dht")
+                nc.scalar.copy(dht[:], bank[:].rearrange("p (m t) -> p t m", t=X4))
+                turned_in[e, g, s] = dht
+                kept = a_tiles[1, e, g][:, :, P * s : P * (s + 1)]
+                nc.scalar.activation(kept, kept, ACT.Relu)
+                if s == SB - 1:
+                    steps_1[e, g] = ring.tile([P, X4 * C], BF16, name="mask", bufs=3, align_bytes=64)
+                    nc.scalar.activation(interleaved(steps_1[e, g][:]), by_lines(a_tiles[1, e, g][:]), ACT.Sign)
+
+        def hidden(e, between):
+            d1 = [ring.tile([P, X4 * C], BF16, name=f"d1_{g}", align_bytes=64, bufs=1) for g in range(NG)]
+            d3 = [ring.tile([P, X4 * C], BF16, name=f"d3_{g}", align_bytes=64, bufs=1) for g in range(NG)]
+            for n, (g, s) in enumerate(order):
+                cols = slice(P * s, P * s + P)
+                run = slice(X4 * P * s, X4 * P * (s + 1))
+                dht = turned_in[e, g, s]
+                bank = pb.tile([P, X4, P], F32, name="turned")
+                for t in range(X4):
+                    nc.tensor.transpose(bank[:, t, :], dht[:, t, :], ident[:])
+                for d, which in ((d3, 1), (d1, 3)):
+                    nc.vector.tensor_tensor(
+                        interleaved(d[g][:, run]), by_lines(bank[:]), by_lines(a_tiles[which, e, g][:, :, cols]), ALU.mult
+                    )
+                between(n, d1, d3)
+
+        codes = {}
+
+        def close_half(e, g, d1, d3):
+            nc.vector.tensor_tensor(d1[g][:], d1[g][:], steps_1[e, g][:], ALU.mult)
+            quantise_hidden(3, e, g, d3[g])
+            quantise_hidden(1, e, g, d1[g])
+
+        def quantise_hidden(which, e, g, d):
+            words = ring.tile([P, C], U32, name=f"d_words{which}{g}", align_bytes=64)
+            scales = ring.tile([P, C], U8, name=f"d_scales{which}{g}", align_bytes=64)
+            nc.vector.quantize_mx(out=words[:].bitcast(E5M2), scales=scales[:], in_=d[:])
+            codes[which, e, g] = (words, scales)
+
+        def second_product(e):
+            for kb in range(KB):
+                bank = pc.tile([P, C], F32, name=f"dx_bank{kb}")
+                passes = [(which, g) for g in range(NG) for which in (3, 1)]
+                for n, (which, g) in enumerate(passes):
+                    w, sc = (w1_w, w1_sc) if which == 1 else (w3_w, w3_sc)
+                    words, scales = codes[which, e, g]
+                    nc.tensor.matmul_mx(
+                        out=bank[:],
+                        lhsT=w[:, NG * e + g, 2 * P * kb : 2 * P * (kb + 1)].bitcast(E2M1),
+                        lhsT_scale=sc[:, NG * e + g, P * kb : P * (kb + 1)],
+                        rhs=words[:].bitcast(E5M2),
+                        rhs_scale=scales[:],
+                        start=(n == 0),
+                        stop=(n == len(passes) - 1),
+                    )
+                nc.scalar.copy(dx[kb][:, C * e : C * (e + 1)], bank[:])
+
+        gather(0)
+        quantise_g(0, 128)
+        first_product(0)
+        gather(1)
+        for e in range(E):
+
+            def between(n, d1, d3):
+                if n == 1 and e + 1 < E:
+                    quantise_g(e + 1, 256)
+                    first_product(e + 1)
+                if n == 4:
+                    close_half(e, 0, d1, d3)
+                if n == 7:
+                    close_half(e, 1, d1, d3)
+
+            hidden(e, between)
+            if e + 2 < E:
+                for g in range(NG):
+                    load_a(1, e + 2, g)
+                    load_a(3, e + 2, g)
+                gather(e + 2)
+            second_product(e)
+
+        for kb in range(KB):
+            half = T // (kb + 1)
+            picks = ring.tile([P, X4, C], F32, name="g4")
+            flat = picks[:].rearrange("p t c -> p (t c)")
+            first, second = flat[:, 0:T], flat[:, T : 2 * T]
+            total = ring.tile([P, T], F32, name="total", bufs=1)
+            for h in range(0, T, half):
+                span = slice(h, h + half)
+                lists = slice(h // 16, (h + half) // 16)
+                nc.vector.tensor_copy(first[:, span], dx[kb][:].indirect(pos1_sb[:, lists]))
+                nc.vector.tensor_copy(second[:, span], dx[kb][:].indirect(pos2_sb[:, lists]))
+                engine = nc.gpsimd if kb == 0 else nc.vector
+                engine.tensor_tensor(total[:, span], first[:, span], second[:, span], ALU.add)
+                nc.sync.dma_start(out[P * kb : P * (kb + 1), span], total[:, span])

@@ -40,13 +40,24 @@ def tile_moe_bdx_glu_relu_kernel(
     nc = tc.nc
     with ExitStack() as ctx:
         held = ctx.enter_context(tc.tile_pool(name="held", bufs=1))
-        saved = ctx.enter_context(tc.tile_pool(name="saved", bufs=4))
-        ring = ctx.enter_context(tc.tile_pool(name="ring", bufs=2))
-        turn = ctx.enter_context(tc.tile_pool(name="turn", bufs=8))
-        mid = ctx.enter_context(tc.tile_pool(name="mid", bufs=3))
-        pa = ctx.enter_context(tc.psum_pool(name="pa", bufs=3))
-        pb = ctx.enter_context(tc.psum_pool(name="pb", bufs=3))
+        arena = ctx.enter_context(tc.tile_pool(name="arena", bufs=1))
+        turn = ctx.enter_context(tc.tile_pool(name="turn", bufs=6))
+        pa = ctx.enter_context(tc.psum_pool(name="pa", bufs=2))
+        pb = ctx.enter_context(tc.psum_pool(name="pb", bufs=4))
         pc = ctx.enter_context(tc.psum_pool(name="pc", bufs=1))
+
+        def placed(shape, dtype, name, kib):
+            return arena.tile(shape, dtype, name=name, offset=1024 * kib, align_bytes=64)
+
+        HALF = C // 2
+        DY = 0
+        X0 = 16
+        SLOT = [20 + 8 * ((n - 3) % 6) for n in range(6)]
+        RAW3 = [68 + 8 * n for n in range(4)]
+        GATE3, D1, D3, GB_A, GB_B, GB_C, X1 = 104, 108, 116, 124, 100, 128, 132
+        DX = 148
+        STEP = [138 + 2 * n for n in range(5)]
+        CLOSING = (X0, X1, RAW3[0], RAW3[0] + 2)
 
         offs_sb = held.tile([P, S // 16], U16, name="offs_sb")
         pos1_sb = held.tile([P, T // 16], U16, name="pos1_sb")
@@ -59,198 +70,335 @@ def tile_moe_bdx_glu_relu_kernel(
             nc.vector.memset(plane[:].rearrange("p e i -> p (e i)").bitcast(I32), 0)
         make_identity(nc, ident[:])
 
-        nc.sync.dma_start(offs_sb[:], offs)
         dy_rows = dyT.rearrange("(p t) s -> t p s", t=X4)
         dy = []
-        gates = []
-
-        def load_gate(e):
-            gate_e = held.tile([P, C], F32, name=f"gate{e}")
-            nc.sync.dma_start(gate_e[:], gate[0:P, C * e : C * (e + 1)])
-            gates.append(gate_e)
-
-        for t in range(X4):
-            dy_t = held.tile([P, T], F32, name=f"dy{t}")
-            nc.sync.dma_start(dy_t[:], dy_rows[t])
-            dy.append(dy_t)
-            if t == 0:
-                load_gate(0)
-
-        w2_w = []
-
-        def load_w2(e):
-            w = held.tile([P, 2 * H], U8, name=f"w2_{e}", align_bytes=64)
-            nc.sync.dma_start(w[:].bitcast(I32), w2_words[e, 0].bitcast(I32))
-            w2_w.append(w)
-
-        def load_scales(queue, plane, scales):
-            by_row = scales.bitcast(I32).rearrange("e s f i -> f (e s) i")
-            for q in range(4):
-                queue.dma_start(plane[32 * q : 32 * q + 4].bitcast(I32), by_row[4 * q : 4 * q + 4])
-
+        gates = {}
+        w2_w = {}
         a_tiles = {}
 
-        def load_a(which, e, g):
-            rows = slice(512 * g, 512 * g + 512)
-            cols = slice(C * e, C * e + C)
-            tile_a = saved.tile([P, X4, C], F32, name=f"a{which}_t")
-            nc.sync.dma_start(tile_a[:], (a1 if which == 1 else a3)[rows, cols].rearrange("(p t) s -> p t s", t=X4))
-            a_tiles[which, e, g] = tile_a
+        def load_gate(e):
+            if e == E - 1:
+                gates[e] = placed([P, C], F32, f"gate{e}", GATE3)
+            else:
+                gates[e] = held.tile([P, C], F32, name=f"gate{e}")
+            nc.sync.dma_start(gates[e][:], gate[0:P, C * e : C * (e + 1)])
 
-        load_scales(nc.sync, w2_sc, w2_scales)
+        def load_w2(e):
+            w2_w[e] = held.tile([P, 2 * H], U8, name=f"w2_{e}", align_bytes=64)
+            nc.sync.dma_start(w2_w[e][:].bitcast(I32), w2_words[e, 0].bitcast(I32))
+
+        def load_scales(plane, scales, lo, hi):
+            by_row = scales.bitcast(I32).rearrange("e s f i -> f (e s) i")
+            for q in range(4):
+                nc.sync.dma_start(plane[32 * q : 32 * q + 4, lo:hi].bitcast(I32), by_row[4 * q : 4 * q + 4, lo:hi])
+
+        a1_home = {(0, 0): 2, (0, 1): 3, (1, 0): 4, (1, 1): 1, (2, 0): 5, (2, 1): 0, (3, 0): 2, (3, 1): 4}
+        a3_home = {(0, 0): 0, (0, 1): 1, (1, 0): 2, (1, 1): 3, (2, 0): 1, (2, 1): 2, (3, 0): 3, (3, 1): 1}
+
+        def load_a(which, e, g, h=None):
+            if not h:
+                home = SLOT[a1_home[e, g]] if which == 1 else RAW3[a3_home[e, g]]
+                a_tiles[which, e, g] = placed([P, X4, C], F32, f"a{which}_{e}{g}", home)
+            lo, hi = (0, C) if h is None else (HALF * h, HALF * (h + 1))
+            saved = (a1 if which == 1 else a3)[512 * g : 512 * (g + 1), C * e + lo : C * e + hi]
+            nc.sync.dma_start(a_tiles[which, e, g][:, :, lo:hi], saved.rearrange("(p t) s -> p t s", t=X4))
+
+        def load_dy(t):
+            dy_t = placed([P, T], F32, f"dy{t}", DY + 4 * t)
+            nc.sync.dma_start(dy_t[:], dy_rows[t])
+            dy.append(dy_t)
+
+        nc.sync.dma_start(offs_sb[:], offs)
+        load_dy(0)
+        for e in range(3):
+            load_gate(e)
+        load_a(1, 0, 0, 0)
+        load_dy(1)
+        load_a(1, 0, 0, 1)
+        load_a(1, 0, 1, 0)
+        load_dy(2)
+        load_a(1, 0, 1, 1)
+        load_a(1, 1, 0, 0)
+        load_dy(3)
+        load_scales(w2_sc, w2_scales, 0, 1)
         load_w2(0)
-        load_a(1, 0, 0)
-        load_gate(1)
-        load_a(1, 0, 1)
         load_a(3, 0, 0)
-        load_w2(1)
+        load_a(1, 1, 0, 1)
         load_a(3, 0, 1)
-        load_scales(nc.sync, w1_sc, w1_scales)
-        load_scales(nc.sync, w3_sc, w3_scales)
-        load_gate(2)
-        load_gate(3)
+        load_a(3, 1, 0)
         w1_w = held.tile([P, E * NG, 2 * K], U8, name="w1_w", align_bytes=64)
-        nc.sync.dma_start(w1_w[:].bitcast(I32), w1_words.bitcast(I32).rearrange("e s p k -> p (e s) k"))
         w3_w = held.tile([P, E * NG, 2 * K], U8, name="w3_w", align_bytes=64)
-        nc.sync.dma_start(w3_w[:].bitcast(I32), w3_words.bitcast(I32).rearrange("e s p k -> p (e s) k"))
-        for g in range(NG):
-            load_a(1, 1, g)
-            load_a(3, 1, g)
-        load_w2(2)
-        load_w2(3)
-        nc.sync.dma_start(pos1_sb[:], pos1)
-        nc.sync.dma_start(pos2_sb[:], pos2)
 
-        dx = [held.tile([P, S], F32, name=f"dx{kb}") for kb in range(KB)]
+        dx = []
 
         g_planes = {}
+        g_bf16 = {}
         g_codes = {}
         turned_in = {}
-        steps_1 = {}
+        steps = {}
+        masked = {}
+        masked_home = {(0, 0, 0): X0, (0, 0, 1): X1}
+        d_tiles = {}
+        codes = {}
+        dx_banks = {}
 
         def gather(e):
-            g4 = ring.tile([P, X4, C], F32, name="g4")
+            g4 = placed([P, X4, C], F32, f"g4_{e}", (SLOT[0], DX, DX + 8, X0 + 3)[e])
             for t in range(X4):
                 nc.vector.tensor_tensor(
                     g4[:, t, :], dy[t][:].indirect(offs_sb[:, (C // 16) * e : (C // 16) * (e + 1)]), gates[e][:], ALU.mult
                 )
             g_planes[e] = g4
 
-        def quantise_g(e, step):
-            words = ring.tile([P, C], U32, name="g_words", align_bytes=64)
-            scales = ring.tile([P, C], U8, name="g_scales", align_bytes=64)
-            for s in range(0, C, step):
-                gb = mid.tile([P, X4 * 256], BF16, name="gb", align_bytes=64, bufs=2)
-                run = gb[:, : X4 * step]
-                nc.scalar.copy(interleaved(run), by_lines(g_planes[e][:, :, s : s + step]))
-                nc.vector.quantize_mx(out=words[:, s : s + step].bitcast(E5M2), scales=scales[:, s : s + step], in_=run)
-            g_codes[e] = (words, scales)
+        def weave_g(e, first, count):
+            if first == 0:
+                g_bf16[e] = placed([P, X4 * C], BF16, f"gb{e}", (GB_A, GB_B, GB_A, GB_C)[e])
+            run = g_bf16[e][:, X4 * first : X4 * (first + count)]
+            nc.scalar.copy(interleaved(run), by_lines(g_planes[e][:, :, first : first + count]))
 
-        order = [(g, s) for g in range(NG) for s in range(SB)]
-
-        def first_product(e):
+        def quantise_g(e, first, count):
+            if first == 0:
+                if e == 0:
+                    scales = held.tile([P, C], U8, name="g_scales0", align_bytes=64)
+                else:
+                    scales = placed([P, C], U8, f"g_scales{e}", {1: X0 + 1, 2: X0 + 2, 3: X1 + 1}[e])
+                g_codes[e] = (held.tile([P, C], U32, name="g_words", align_bytes=64, bufs=3), scales)
             words, scales = g_codes[e]
-            for g, s in order:
-                bank = pa.tile([P, 512], F32, name="dh_bank")
-                nc.tensor.matmul_mx(
-                    out=bank[:],
-                    lhsT=words[:, P * s : P * s + P].bitcast(E5M2),
-                    lhsT_scale=scales[:, P * s : P * s + P],
-                    rhs=w2_w[e][:, 1024 * g : 1024 * g + 1024].bitcast(E2M1),
-                    rhs_scale=w2_sc[:, e, 512 * g : 512 * g + 512],
-                    start=True,
-                    stop=True,
+            cols = slice(first, first + count)
+            run = g_bf16[e][:, X4 * first : X4 * (first + count)]
+            nc.vector.quantize_mx(out=words[:, cols].bitcast(E5M2), scales=scales[:, cols], in_=run)
+
+        def first_product(e, n):
+            g, s = divmod(n, SB)
+            words, scales = g_codes[e]
+            bank = pa.tile([P, 512], F32, name="dh_bank")
+            nc.tensor.matmul_mx(
+                out=bank[:],
+                lhsT=words[:, P * s : P * s + P].bitcast(E5M2),
+                lhsT_scale=scales[:, P * s : P * s + P],
+                rhs=w2_w[e][:, 1024 * g : 1024 * g + 1024].bitcast(E2M1),
+                rhs_scale=w2_sc[:, e, 512 * g : 512 * g + 512],
+                start=True,
+                stop=True,
+            )
+            dht = turn.tile([P, X4, P], F32, name="dht")
+            nc.scalar.copy(dht[:], bank[:].rearrange("p (m t) -> p t m", t=X4))
+            turned_in[e, n] = dht
+
+        def relu_a1(e, g, h):
+            kept = a_tiles[1, e, g][:, :, HALF * h : HALF * (h + 1)]
+            nc.scalar.activation(kept, kept, ACT.Relu)
+
+        def step_a1(e, g, h):
+            relu_a1(e, g, h)
+            if g == 1 and e in (2,3,):
+                return
+            home = GB_C if (e, g, h) == (1, 1, 1) else STEP[(4 * e + 2 * g + h) % len(STEP)]
+            steps[e, g, h] = placed([P, X4, HALF], BF16, f"step{e}{g}{h}", home)[:]
+            nc.scalar.activation(steps[e, g, h], a_tiles[1, e, g][:, :, HALF * h : HALF * (h + 1)], ACT.Sign)
+
+        def step_on_vector(e):
+            both = placed([P, X4, C], BF16, f"step{e}", CLOSING[e - 1] + 2)
+            nc.vector.tensor_scalar(both[:], a_tiles[1, e, 1][:], 0.0, None, ALU.is_gt)
+            for h in range(2):
+                steps[e, 1, h] = both[:, :, HALF * h : HALF * (h + 1)]
+
+        def mask_a3(e, g, h):
+            cols = slice(HALF * h, HALF * (h + 1))
+            if (g, h) == (1, 0):
+                masked_home[e, g, h] = (RAW3[0], GATE3, D1, DY)[e]
+            elif (g, h) == (1, 1):
+                masked_home[e, g, h] = masked_home[e, 0, 0]
+            elif e > 0:
+                masked_home[e, g, h] = masked_home[e - 1, h, 1 - h]
+            masked[e, g, h] = placed([P, X4, HALF], F32, f"a3m{e}{g}{h}", masked_home[e, g, h])
+            if (e, g) == (0, 0):
+                nc.vector.scalar_tensor_tensor(
+                    masked[e, g, h][:], a_tiles[1, e, g][:, :, cols], 0.0, a_tiles[3, e, g][:, :, cols], ALU.is_gt, ALU.mult
                 )
-                dht = turn.tile([P, X4, P], F32, name="dht")
-                nc.scalar.copy(dht[:], bank[:].rearrange("p (m t) -> p t m", t=X4))
-                turned_in[e, g, s] = dht
-                kept = a_tiles[1, e, g][:, :, P * s : P * (s + 1)]
-                nc.scalar.activation(kept, kept, ACT.Relu)
-                if s == SB - 1:
-                    steps_1[e, g] = ring.tile([P, X4 * C], BF16, name="mask", bufs=3, align_bytes=64)
-                    nc.scalar.activation(interleaved(steps_1[e, g][:]), by_lines(a_tiles[1, e, g][:]), ACT.Sign)
+            else:
+                nc.gpsimd.tensor_tensor(masked[e, g, h][:], a_tiles[3, e, g][:, :, cols], steps[e, g, h], ALU.mult)
 
-        def hidden(e, between):
-            d1 = [ring.tile([P, X4 * C], BF16, name=f"d1_{g}", align_bytes=64, bufs=1) for g in range(NG)]
-            d3 = [ring.tile([P, X4 * C], BF16, name=f"d3_{g}", align_bytes=64, bufs=1) for g in range(NG)]
-            for n, (g, s) in enumerate(order):
-                cols = slice(P * s, P * s + P)
-                run = slice(X4 * P * s, X4 * P * (s + 1))
-                dht = turned_in[e, g, s]
-                bank = pb.tile([P, X4, P], F32, name="turned")
-                for t in range(X4):
-                    nc.tensor.transpose(bank[:, t, :], dht[:, t, :], ident[:])
-                for d, which in ((d3, 1), (d1, 3)):
-                    nc.vector.tensor_tensor(
-                        interleaved(d[g][:, run]), by_lines(bank[:]), by_lines(a_tiles[which, e, g][:, :, cols]), ALU.mult
-                    )
-                between(n, d1, d3)
+        def hidden(e, n):
+            g, s = divmod(n, SB)
+            if n == 0:
+                d_tiles[1, e] = placed([P, NG * X4 * C], BF16, f"d1_{e}", (D1, D1, DY, DY + 8)[e])
+                d_tiles[3, e] = placed([P, NG * X4 * C], BF16, f"d3_{e}", D3)
+            run = slice(X4 * P * n, X4 * P * (n + 1))
+            bank = pb.tile([P, X4, P], F32, name="turned")
+            for t in range(X4):
+                nc.tensor.transpose(bank[:, t, :], turned_in[e, n][:, t, :], ident[:])
+            h, r = divmod(s, 2)
+            nc.vector.tensor_tensor(
+                interleaved(d_tiles[3, e][:, run]),
+                by_lines(bank[:]),
+                by_lines(a_tiles[1, e, g][:, :, P * s : P * (s + 1)]),
+                ALU.mult,
+            )
+            nc.vector.tensor_tensor(
+                interleaved(d_tiles[1, e][:, run]),
+                by_lines(bank[:]),
+                by_lines(masked[e, g, h][:, :, P * r : P * (r + 1)]),
+                ALU.mult,
+            )
 
-        codes = {}
-
-        def close_half(e, g, d1, d3):
-            nc.vector.tensor_tensor(d1[g][:], d1[g][:], steps_1[e, g][:], ALU.mult)
-            quantise_hidden(3, e, g, d3[g])
-            quantise_hidden(1, e, g, d1[g])
-
-        def quantise_hidden(which, e, g, d):
-            words = ring.tile([P, C], U32, name=f"d_words{which}{g}", align_bytes=64)
-            scales = ring.tile([P, C], U8, name=f"d_scales{which}{g}", align_bytes=64)
-            nc.vector.quantize_mx(out=words[:].bitcast(E5M2), scales=scales[:], in_=d[:])
-            codes[which, e, g] = (words, scales)
+        def quantise_d(which, e, first, count):
+            if first == 0:
+                if e == E - 1 or which == 3:
+                    scales = placed([P, NG * C], U8, f"d_scales{which}{e}", CLOSING[e] + (which == 1))
+                else:
+                    scales = held.tile([P, NG * C], U8, name="d_scales1", align_bytes=64, bufs=2)
+                codes[which, e] = (held.tile([P, NG * C], U32, name=f"d_words{which}", align_bytes=64, bufs=2), scales)
+            words, scales = codes[which, e]
+            cols = slice(C * first, C * (first + count))
+            run = d_tiles[which, e][:, X4 * C * first : X4 * C * (first + count)]
+            nc.vector.quantize_mx(out=words[:, cols].bitcast(E5M2), scales=scales[:, cols], in_=run)
 
         def second_product(e):
-            for kb in range(KB):
-                bank = pc.tile([P, C], F32, name=f"dx_bank{kb}")
-                passes = [(which, g) for g in range(NG) for which in (3, 1)]
-                for n, (which, g) in enumerate(passes):
-                    w, sc = (w1_w, w1_sc) if which == 1 else (w3_w, w3_sc)
-                    words, scales = codes[which, e, g]
+            banks = [pc.tile([P, C], F32, name=f"dx_bank{kb}") for kb in range(KB)]
+            passes = [(which, g) for g in range(NG) for which in (3, 1)]
+            for n, (which, g) in enumerate(passes):
+                w, sc = (w1_w, w1_sc) if which == 1 else (w3_w, w3_sc)
+                words, scales = codes[which, e]
+                for kb in range(KB):
                     nc.tensor.matmul_mx(
-                        out=bank[:],
+                        out=banks[kb][:],
                         lhsT=w[:, NG * e + g, 2 * P * kb : 2 * P * (kb + 1)].bitcast(E2M1),
                         lhsT_scale=sc[:, NG * e + g, P * kb : P * (kb + 1)],
-                        rhs=words[:].bitcast(E5M2),
-                        rhs_scale=scales[:],
+                        rhs=words[:, C * g : C * (g + 1)].bitcast(E5M2),
+                        rhs_scale=scales[:, C * g : C * (g + 1)],
                         start=(n == 0),
                         stop=(n == len(passes) - 1),
                     )
-                nc.scalar.copy(dx[kb][:, C * e : C * (e + 1)], bank[:])
+            dx_banks[e] = banks
 
-        gather(0)
-        quantise_g(0, 128)
-        first_product(0)
-        gather(1)
+        def keep_dx(e):
+            for kb in range(KB):
+                if e == 0:
+                    dx.append(placed([P, S], F32, f"dx{kb}", DX + 8 * kb))
+                nc.scalar.copy(dx[kb][:, C * e : C * (e + 1)], dx_banks[e][kb][:])
+
+        relu_a1(0, 0, 0)
+        relu_a1(0, 0, 1)
+        step_a1(0, 1, 0)
+        step_a1(0, 1, 1)
+        for e in range(3):
+            gather(e)
+        for h in range(2):
+            weave_g(0, HALF * h, HALF)
+            quantise_g(0, HALF * h, HALF)
+        load_a(1, 1, 1)
+        load_w2(1)
+        load_scales(w2_sc, w2_scales, 1, E)
+        load_gate(3)
+        load_a(1, 2, 0)
+        load_a(3, 1, 1)
+        load_a(1, 2, 1)
+        for n in range(4):
+            first_product(0, n)
+        for h in range(2):
+            mask_a3(0, 0, h)
+        step_a1(1, 0, 0)
+        for n in range(4, 8):
+            first_product(0, n)
+
         for e in range(E):
-
-            def between(n, d1, d3):
-                if n == 1 and e + 1 < E:
-                    quantise_g(e + 1, 256)
-                    first_product(e + 1)
-                if n == 4:
-                    close_half(e, 0, d1, d3)
-                if n == 7:
-                    close_half(e, 1, d1, d3)
-
-            hidden(e, between)
-            if e + 2 < E:
-                for g in range(NG):
-                    load_a(1, e + 2, g)
-                    load_a(3, e + 2, g)
-                gather(e + 2)
-            second_product(e)
+            last = e == E - 1
+            mask_a3(e, 1, 0)
+            hidden(e, 0)
+            hidden(e, 1)
+            if e > 1:
+                step_a1(e, 1, 1)
+            mask_a3(e, 1, 1)
+            if e > 1:
+                first_product(e, 4)
+            if e in (1, 2):
+                step_a1(e + 1, 0, 0)
+            if e > 1:
+                first_product(e, 5)
+            hidden(e, 2)
+            hidden(e, 3)
+            if not last:
+                mask_a3(e + 1, 0, 0)
+            if e > 1:
+                first_product(e, 6)
+            if not last:
+                step_a1(e + 1, 0, 1)
+            if e > 1:
+                first_product(e, 7)
+            if last:
+                keep_dx(1)
+                second_product(2)
+                keep_dx(2)
+            hidden(e, 4)
+            if last:
+                quantise_d(3, e, 0, 1)
+                quantise_d(1, e, 0, 1)
+            hidden(e, 5)
+            if not last:
+                mask_a3(e + 1, 0, 1)
+            if e == 0:
+                weave_g(1, 0, C)
+                weave_g(2, 0, C)
+            if e == 1:
+                weave_g(3, 0, C)
+            if e in (1, 2):
+                first_product(e + 1, 0)
+                step_a1(e + 1, 1, 0)
+                for n in range(1, 4):
+                    first_product(e + 1, n)
+            if e == 2:
+                keep_dx(0)
+                second_product(1)
+            hidden(e, 6)
+            hidden(e, 7)
+            if e == 0:
+                load_a(3, 2, 0)
+                load_w2(2)
+                load_a(1, 3, 0)
+                load_a(3, 2, 1)
+                load_w2(3)
+                load_scales(w1_sc, w1_scales, 0, E * NG)
+                load_scales(w3_sc, w3_scales, 0, E * NG)
+                nc.sync.dma_start(w1_w[:].bitcast(I32), w1_words.bitcast(I32).rearrange("e s p k -> p (e s) k"))
+                nc.sync.dma_start(w3_w[:].bitcast(I32), w3_words.bitcast(I32).rearrange("e s p k -> p (e s) k"))
+                nc.sync.dma_start(pos1_sb[:], pos1)
+                nc.sync.dma_start(pos2_sb[:], pos2)
+                quantise_g(1, 0, C)
+            if e == 1:
+                load_a(1, 3, 1)
+                load_a(3, 3, 0)
+                load_a(3, 3, 1)
+                quantise_g(3, 0, C)
+            if last:
+                quantise_d(3, e, 1, 1)
+                quantise_d(1, e, 1, 1)
+            else:
+                if e + 1 in (2,3,):
+                    step_on_vector(e + 1)
+                quantise_d(3, e, 0, NG)
+                quantise_d(1, e, 0, NG)
+            if e == 0:
+                quantise_g(2, 0, C)
+                gather(3)
+                step_a1(1, 1, 0)
+                for n in range(4):
+                    first_product(1, n)
+                step_a1(1, 1, 1)
+                for n in range(4, 8):
+                    first_product(1, n)
+                second_product(0)
+        second_product(E - 1)
+        keep_dx(E - 1)
 
         for kb in range(KB):
-            half = T // (kb + 1)
-            picks = ring.tile([P, X4, C], F32, name="g4")
-            flat = picks[:].rearrange("p t c -> p (t c)")
-            first, second = flat[:, 0:T], flat[:, T : 2 * T]
-            total = ring.tile([P, T], F32, name="total", bufs=1)
-            for h in range(0, T, half):
-                span = slice(h, h + half)
-                lists = slice(h // 16, (h + half) // 16)
-                nc.vector.tensor_copy(first[:, span], dx[kb][:].indirect(pos1_sb[:, lists]))
-                nc.vector.tensor_copy(second[:, span], dx[kb][:].indirect(pos2_sb[:, lists]))
-                engine = nc.gpsimd if kb == 0 else nc.vector
-                engine.tensor_tensor(total[:, span], first[:, span], second[:, span], ALU.add)
-                nc.sync.dma_start(out[P * kb : P * (kb + 1), span], total[:, span])
+            first = placed([P, T], F32, f"first{kb}", SLOT[1] + 4 * kb)
+            total = placed([P, T], F32, f"total{kb}", SLOT[5] + 4 * kb)
+            spans = [(0, 512), (512, 1024)]
+            for lo, hi in spans:
+                nc.vector.tensor_copy(first[:, lo:hi], dx[kb][:].indirect(pos1_sb[:, lo // 16 : hi // 16]))
+            for lo, hi in spans:
+                nc.vector.tensor_tensor(
+                    total[:, lo:hi], dx[kb][:].indirect(pos2_sb[:, lo // 16 : hi // 16]), first[:, lo:hi], ALU.add
+                )
+                nc.sync.dma_start(out[P * kb : P * (kb + 1), lo:hi], total[:, lo:hi])

@@ -57,7 +57,7 @@ def tile_moe_bdx_glu_relu_kernel(
         GATE3, D1, D3, GB_A, GB_B, GB_C, X1 = 104, 108, 116, 124, 100, 128, 132
         DX = 148
         STEP = [138 + 2 * n for n in range(5)]
-        CLOSING = (X0, X1, RAW3[0], RAW3[0] + 2)
+        CLOSING = (X0, X1, RAW3[0], DY)
 
         offs_sb = held.tile([P, S // 16], U16, name="offs_sb")
         pos1_sb = held.tile([P, T // 16], U16, name="pos1_sb")
@@ -87,10 +87,10 @@ def tile_moe_bdx_glu_relu_kernel(
             w2_w[e] = held.tile([P, 2 * H], U8, name=f"w2_{e}", align_bytes=64)
             nc.sync.dma_start(w2_w[e][:].bitcast(I32), w2_words[e, 0].bitcast(I32))
 
-        def load_scales(plane, scales, lo, hi):
+        def load_scales(plane, scales):
             by_row = scales.bitcast(I32).rearrange("e s f i -> f (e s) i")
             for q in range(4):
-                nc.sync.dma_start(plane[32 * q : 32 * q + 4, lo:hi].bitcast(I32), by_row[4 * q : 4 * q + 4, lo:hi])
+                nc.gpsimd.dma_start(plane[32 * q : 32 * q + 4].bitcast(I32), by_row[4 * q : 4 * q + 4])
 
         a1_home = {(0, 0): 2, (0, 1): 3, (1, 0): 4, (1, 1): 1, (2, 0): 5, (2, 1): 0, (3, 0): 2, (3, 1): 4}
         a3_home = {(0, 0): 0, (0, 1): 1, (1, 0): 2, (1, 1): 3, (2, 0): 1, (2, 1): 2, (3, 0): 3, (3, 1): 1}
@@ -103,11 +103,19 @@ def tile_moe_bdx_glu_relu_kernel(
             saved = (a1 if which == 1 else a3)[512 * g : 512 * (g + 1), C * e + lo : C * e + hi]
             nc.sync.dma_start(a_tiles[which, e, g][:, :, lo:hi], saved.rearrange("(p t) s -> p t s", t=X4))
 
+        def load_w13(pair):
+            lo, hi = E * pair, E * (pair + 1)
+            for tile_w, words in ((w3_w, w3_words), (w1_w, w1_words)):
+                by_pass = words.bitcast(I32).rearrange("e s p k -> p (e s) k")
+                nc.sync.dma_start(tile_w[:, lo:hi].bitcast(I32), by_pass[:, lo:hi])
+
         def load_dy(t):
             dy_t = placed([P, T], F32, f"dy{t}", DY + 4 * t)
             nc.sync.dma_start(dy_t[:], dy_rows[t])
             dy.append(dy_t)
 
+        for plane, scales in ((w2_sc, w2_scales), (w3_sc, w3_scales), (w1_sc, w1_scales)):
+            load_scales(plane, scales)
         nc.sync.dma_start(offs_sb[:], offs)
         load_dy(0)
         for e in range(3):
@@ -115,12 +123,11 @@ def tile_moe_bdx_glu_relu_kernel(
         load_a(1, 0, 0, 0)
         load_dy(1)
         load_a(1, 0, 0, 1)
-        load_a(1, 0, 1, 0)
         load_dy(2)
+        load_a(1, 0, 1, 0)
         load_a(1, 0, 1, 1)
-        load_a(1, 1, 0, 0)
         load_dy(3)
-        load_scales(w2_sc, w2_scales, 0, 1)
+        load_a(1, 1, 0, 0)
         load_w2(0)
         load_a(3, 0, 0)
         load_a(1, 1, 0, 1)
@@ -152,7 +159,7 @@ def tile_moe_bdx_glu_relu_kernel(
 
         def weave_g(e, first, count):
             if first == 0:
-                g_bf16[e] = placed([P, X4 * C], BF16, f"gb{e}", (GB_A, GB_B, GB_A, GB_C)[e])
+                g_bf16[e] = placed([P, X4 * C], BF16, f"gb{e}", (GB_A, GB_B, GB_C, GB_A)[e])
             run = g_bf16[e][:, X4 * first : X4 * (first + count)]
             nc.scalar.copy(interleaved(run), by_lines(g_planes[e][:, :, first : first + count]))
 
@@ -191,9 +198,9 @@ def tile_moe_bdx_glu_relu_kernel(
 
         def step_a1(e, g, h):
             relu_a1(e, g, h)
-            if g == 1 and e in (2,3,):
+            if g == 1 and e in ():
                 return
-            home = GB_C if (e, g, h) == (1, 1, 1) else STEP[(4 * e + 2 * g + h) % len(STEP)]
+            home = {(0, 1, 0): GB_B, (0, 1, 1): GB_C, (1, 1, 1): GB_A}.get((e, g, h), STEP[(4 * e + 2 * g + h) % len(STEP)])
             steps[e, g, h] = placed([P, X4, HALF], BF16, f"step{e}{g}{h}", home)[:]
             nc.scalar.activation(steps[e, g, h], a_tiles[1, e, g][:, :, HALF * h : HALF * (h + 1)], ACT.Sign)
 
@@ -243,32 +250,35 @@ def tile_moe_bdx_glu_relu_kernel(
             )
 
         def quantise_d(which, e, first, count):
-            if first == 0:
-                if e == E - 1 or which == 3:
-                    scales = placed([P, NG * C], U8, f"d_scales{which}{e}", CLOSING[e] + (which == 1))
-                else:
-                    scales = held.tile([P, NG * C], U8, name="d_scales1", align_bytes=64, bufs=2)
-                codes[which, e] = (held.tile([P, NG * C], U32, name=f"d_words{which}", align_bytes=64, bufs=2), scales)
-            words, scales = codes[which, e]
-            cols = slice(C * first, C * (first + count))
+            cols = C * count
+            if e == E - 1:
+                scales = placed([P, cols], U8, f"d_scales{which}{e}{first}", CLOSING[e] + 2 * first + (which == 1))
+            elif which == 3:
+                scales = placed([P, cols], U8, f"d_scales{which}{e}", CLOSING[e])
+            else:
+                scales = held.tile([P, cols], U8, name="d_scales1", align_bytes=64, bufs=2)
+            words = held.tile([P, cols], U32, name=f"d_words{which}", align_bytes=64, bufs=2)
             run = d_tiles[which, e][:, X4 * C * first : X4 * C * (first + count)]
-            nc.vector.quantize_mx(out=words[:, cols].bitcast(E5M2), scales=scales[:, cols], in_=run)
+            nc.vector.quantize_mx(out=words[:].bitcast(E5M2), scales=scales[:], in_=run)
+            for g in range(count):
+                codes[which, e, first + g] = (words[:, C * g : C * (g + 1)], scales[:, C * g : C * (g + 1)])
 
         def second_product(e):
             banks = [pc.tile([P, C], F32, name=f"dx_bank{kb}") for kb in range(KB)]
-            passes = [(which, g) for g in range(NG) for which in (3, 1)]
-            for n, (which, g) in enumerate(passes):
-                w, sc = (w1_w, w1_sc) if which == 1 else (w3_w, w3_sc)
-                words, scales = codes[which, e]
+            for n in range(2 * NG):
+                g = n // 2
                 for kb in range(KB):
+                    which = (3, 1)[n % 2]
+                    w, sc = (w1_w, w1_sc) if which == 1 else (w3_w, w3_sc)
+                    words, scales = codes[which, e, g]
                     nc.tensor.matmul_mx(
                         out=banks[kb][:],
                         lhsT=w[:, NG * e + g, 2 * P * kb : 2 * P * (kb + 1)].bitcast(E2M1),
                         lhsT_scale=sc[:, NG * e + g, P * kb : P * (kb + 1)],
-                        rhs=words[:, C * g : C * (g + 1)].bitcast(E5M2),
-                        rhs_scale=scales[:, C * g : C * (g + 1)],
+                        rhs=words.bitcast(E5M2),
+                        rhs_scale=scales,
                         start=(n == 0),
-                        stop=(n == len(passes) - 1),
+                        stop=(n == 2 * NG - 1),
                     )
             dx_banks[e] = banks
 
@@ -284,12 +294,11 @@ def tile_moe_bdx_glu_relu_kernel(
         step_a1(0, 1, 1)
         for e in range(3):
             gather(e)
-        for h in range(2):
-            weave_g(0, HALF * h, HALF)
-            quantise_g(0, HALF * h, HALF)
+        for first, count in ((0, P), (P, P), (HALF, HALF)):
+            weave_g(0, first, count)
+            quantise_g(0, first, count)
         load_a(1, 1, 1)
         load_w2(1)
-        load_scales(w2_sc, w2_scales, 1, E)
         load_gate(3)
         load_a(1, 2, 0)
         load_a(3, 1, 1)
@@ -327,54 +336,52 @@ def tile_moe_bdx_glu_relu_kernel(
             if e > 1:
                 first_product(e, 7)
             if last:
-                keep_dx(1)
                 second_product(2)
                 keep_dx(2)
             hidden(e, 4)
+            hidden(e, 5)
             if last:
                 quantise_d(3, e, 0, 1)
                 quantise_d(1, e, 0, 1)
-            hidden(e, 5)
             if not last:
                 mask_a3(e + 1, 0, 1)
             if e == 0:
-                weave_g(1, 0, C)
-                weave_g(2, 0, C)
+                for n in range(4):
+                    weave_g(1 + n // 2, HALF * (n % 2), HALF)
             if e == 1:
-                weave_g(3, 0, C)
+                weave_g(3, 0, HALF)
+                weave_g(3, HALF, HALF)
             if e in (1, 2):
                 first_product(e + 1, 0)
                 step_a1(e + 1, 1, 0)
                 for n in range(1, 4):
                     first_product(e + 1, n)
-            if e == 2:
-                keep_dx(0)
-                second_product(1)
+            if e in (1, 2):
+                second_product(e - 1)
+                keep_dx(e - 1)
             hidden(e, 6)
             hidden(e, 7)
             if e == 0:
                 load_a(3, 2, 0)
                 load_w2(2)
-                load_a(1, 3, 0)
+                load_w13(0)
                 load_a(3, 2, 1)
+                load_a(1, 3, 0)
                 load_w2(3)
-                load_scales(w1_sc, w1_scales, 0, E * NG)
-                load_scales(w3_sc, w3_scales, 0, E * NG)
-                nc.sync.dma_start(w1_w[:].bitcast(I32), w1_words.bitcast(I32).rearrange("e s p k -> p (e s) k"))
-                nc.sync.dma_start(w3_w[:].bitcast(I32), w3_words.bitcast(I32).rearrange("e s p k -> p (e s) k"))
                 nc.sync.dma_start(pos1_sb[:], pos1)
                 nc.sync.dma_start(pos2_sb[:], pos2)
                 quantise_g(1, 0, C)
             if e == 1:
-                load_a(1, 3, 1)
                 load_a(3, 3, 0)
+                load_a(1, 3, 1)
+                load_w13(1)
                 load_a(3, 3, 1)
                 quantise_g(3, 0, C)
             if last:
                 quantise_d(3, e, 1, 1)
                 quantise_d(1, e, 1, 1)
             else:
-                if e + 1 in (2,3,):
+                if e + 1 in ():
                     step_on_vector(e + 1)
                 quantise_d(3, e, 0, NG)
                 quantise_d(1, e, 0, NG)
@@ -387,7 +394,6 @@ def tile_moe_bdx_glu_relu_kernel(
                 step_a1(1, 1, 1)
                 for n in range(4, 8):
                     first_product(1, n)
-                second_product(0)
         second_product(E - 1)
         keep_dx(E - 1)
 

@@ -87,10 +87,10 @@ def tile_moe_bdx_glu_relu_kernel(
             w2_w[e] = held.tile([P, 2 * H], U8, name=f"w2_{e}", align_bytes=64)
             nc.sync.dma_start(w2_w[e][:].bitcast(I32), w2_words[e, 0].bitcast(I32))
 
-        def load_scales(plane, scales):
+        def load_scales(queue, plane, scales, lo, hi):
             by_row = scales.bitcast(I32).rearrange("e s f i -> f (e s) i")
             for q in range(4):
-                nc.gpsimd.dma_start(plane[32 * q : 32 * q + 4].bitcast(I32), by_row[4 * q : 4 * q + 4])
+                queue.dma_start(plane[32 * q : 32 * q + 4, lo:hi].bitcast(I32), by_row[4 * q : 4 * q + 4, lo:hi])
 
         a1_home = {(0, 0): 2, (0, 1): 3, (1, 0): 4, (1, 1): 1, (2, 0): 5, (2, 1): 0, (3, 0): 2, (3, 1): 4}
         a3_home = {(0, 0): 0, (0, 1): 1, (1, 0): 2, (1, 1): 3, (2, 0): 1, (2, 1): 2, (3, 0): 3, (3, 1): 1}
@@ -105,7 +105,8 @@ def tile_moe_bdx_glu_relu_kernel(
 
         def load_w13(pair):
             lo, hi = E * pair, E * (pair + 1)
-            for tile_w, words in ((w3_w, w3_words), (w1_w, w1_words)):
+            for tile_w, words, plane, scales in ((w3_w, w3_words, w3_sc, w3_scales), (w1_w, w1_words, w1_sc, w1_scales)):
+                load_scales(nc.sync, plane, scales, lo, hi)
                 by_pass = words.bitcast(I32).rearrange("e s p k -> p (e s) k")
                 nc.sync.dma_start(tile_w[:, lo:hi].bitcast(I32), by_pass[:, lo:hi])
 
@@ -114,8 +115,7 @@ def tile_moe_bdx_glu_relu_kernel(
             nc.sync.dma_start(dy_t[:], dy_rows[t])
             dy.append(dy_t)
 
-        for plane, scales in ((w2_sc, w2_scales), (w3_sc, w3_scales), (w1_sc, w1_scales)):
-            load_scales(plane, scales)
+        load_scales(nc.gpsimd, w2_sc, w2_scales, 0, E)
         nc.sync.dma_start(offs_sb[:], offs)
         load_dy(0)
         for e in range(3):
@@ -197,9 +197,9 @@ def tile_moe_bdx_glu_relu_kernel(
             nc.scalar.activation(kept, kept, ACT.Relu)
 
         def step_a1(e, g, h):
-            relu_a1(e, g, h)
-            if g == 1 and e in ():
+            if g == 1 and e in (2,3,):
                 return
+            relu_a1(e, g, h)
             home = {(0, 1, 0): GB_B, (0, 1, 1): GB_C, (1, 1, 1): GB_A}.get((e, g, h), STEP[(4 * e + 2 * g + h) % len(STEP)])
             steps[e, g, h] = placed([P, X4, HALF], BF16, f"step{e}{g}{h}", home)[:]
             nc.scalar.activation(steps[e, g, h], a_tiles[1, e, g][:, :, HALF * h : HALF * (h + 1)], ACT.Sign)
@@ -294,7 +294,7 @@ def tile_moe_bdx_glu_relu_kernel(
         step_a1(0, 1, 1)
         for e in range(3):
             gather(e)
-        for first, count in ((0, P), (P, P), (HALF, HALF)):
+        for first, count in ((0, HALF), (HALF, HALF)):
             weave_g(0, first, count)
             quantise_g(0, first, count)
         load_a(1, 1, 1)
@@ -329,10 +329,14 @@ def tile_moe_bdx_glu_relu_kernel(
             hidden(e, 3)
             if not last:
                 mask_a3(e + 1, 0, 0)
+            if e in (2,3,):
+                relu_a1(e, 1, 0)
             if e > 1:
                 first_product(e, 6)
             if not last:
                 step_a1(e + 1, 0, 1)
+            if e in (2,3,):
+                relu_a1(e, 1, 1)
             if e > 1:
                 first_product(e, 7)
             if last:
@@ -374,14 +378,14 @@ def tile_moe_bdx_glu_relu_kernel(
             if e == 1:
                 load_a(3, 3, 0)
                 load_a(1, 3, 1)
-                load_w13(1)
                 load_a(3, 3, 1)
+                load_w13(1)
                 quantise_g(3, 0, C)
             if last:
                 quantise_d(3, e, 1, 1)
                 quantise_d(1, e, 1, 1)
             else:
-                if e + 1 in ():
+                if e + 1 in (2,3,):
                     step_on_vector(e + 1)
                 quantise_d(3, e, 0, NG)
                 quantise_d(1, e, 0, NG)
@@ -400,10 +404,9 @@ def tile_moe_bdx_glu_relu_kernel(
         for kb in range(KB):
             first = placed([P, T], F32, f"first{kb}", SLOT[1] + 4 * kb)
             total = placed([P, T], F32, f"total{kb}", SLOT[5] + 4 * kb)
-            spans = [(0, 512), (512, 1024)]
-            for lo, hi in spans:
+            for lo, hi in ((0, 512), (512, T)):
                 nc.vector.tensor_copy(first[:, lo:hi], dx[kb][:].indirect(pos1_sb[:, lo // 16 : hi // 16]))
-            for lo, hi in spans:
+            for lo, hi in ((0, 512), (512, T)) if kb == 0 else ((0, 512), (512, T - P), (T - P, T)):
                 nc.vector.tensor_tensor(
                     total[:, lo:hi], dx[kb][:].indirect(pos2_sb[:, lo // 16 : hi // 16]), first[:, lo:hi], ALU.add
                 )

@@ -41,23 +41,23 @@ def tile_moe_bdx_glu_relu_kernel(
     with ExitStack() as ctx:
         held = ctx.enter_context(tc.tile_pool(name="held", bufs=1))
         arena = ctx.enter_context(tc.tile_pool(name="arena", bufs=1))
-        turn = ctx.enter_context(tc.tile_pool(name="turn", bufs=6))
-        pa = ctx.enter_context(tc.psum_pool(name="pa", bufs=2))
+        turn = ctx.enter_context(tc.tile_pool(name="turn", bufs=4))
+        pa = ctx.enter_context(tc.psum_pool(name="pa", bufs=3))
         pb = ctx.enter_context(tc.psum_pool(name="pb", bufs=4))
         pc = ctx.enter_context(tc.psum_pool(name="pc", bufs=1))
 
         def placed(shape, dtype, name, kib):
-            return arena.tile(shape, dtype, name=name, offset=1024 * kib, align_bytes=64)
+            return arena.tile(shape, dtype, name=name, offset=int(1024 * kib), align_bytes=64)
 
         HALF = C // 2
         DY = 0
-        X0 = 16
-        SLOT = [20 + 8 * ((n - 3) % 6) for n in range(6)]
-        RAW3 = [68 + 8 * n for n in range(4)]
-        GATE3, D1, D3, GB_A, GB_B, GB_C, X1 = 104, 108, 116, 124, 100, 128, 132
-        DX = 148
-        STEP = [138 + 2 * n for n in range(5)]
-        CLOSING = (X0, X1, RAW3[0], DY)
+        X0 = 19
+        SLOT = [23 + 8 * ((n - 3) % 6) for n in range(6)]
+        RAW3 = [71 + 8 * n for n in range(4)]
+        GATE3, D1, D3, GB_A, GB_B, GB_C, X1 = 103, 107, 115, 123, 127, 131, 138
+        DX = 156
+        STEP = [146 + 2 * n for n in range(5)]
+        CLOSING = (X0 + 1, X1 + 1, X0 - 3, DY)
 
         offs_sb = held.tile([P, S // 16], U16, name="offs_sb")
         pos1_sb = held.tile([P, T // 16], U16, name="pos1_sb")
@@ -118,8 +118,9 @@ def tile_moe_bdx_glu_relu_kernel(
         load_scales(nc.gpsimd, w2_sc, w2_scales, 0, E)
         nc.sync.dma_start(offs_sb[:], offs)
         load_dy(0)
-        for e in range(3):
-            load_gate(e)
+        load_gate(0)
+        load_gate(1)
+        load_gate(2)
         load_a(1, 0, 0, 0)
         load_dy(1)
         load_a(1, 0, 0, 1)
@@ -147,7 +148,6 @@ def tile_moe_bdx_glu_relu_kernel(
         masked_home = {(0, 0, 0): X0, (0, 0, 1): X1}
         d_tiles = {}
         codes = {}
-        dx_banks = {}
 
         def gather(e):
             g4 = placed([P, X4, C], F32, f"g4_{e}", (SLOT[0], DX, DX + 8, X0 + 3)[e])
@@ -168,7 +168,7 @@ def tile_moe_bdx_glu_relu_kernel(
                 if e == 0:
                     scales = held.tile([P, C], U8, name="g_scales0", align_bytes=64)
                 else:
-                    scales = placed([P, C], U8, f"g_scales{e}", {1: X0 + 1, 2: X0 + 2, 3: X1 + 1}[e])
+                    scales = placed([P, C], U8, f"g_scales{e}", {1: X0 + 2, 2: X0 + 2.5, 3: X1 + 2}[e])
                 g_codes[e] = (held.tile([P, C], U32, name="g_words", align_bytes=64, bufs=3), scales)
             words, scales = g_codes[e]
             cols = slice(first, first + count)
@@ -190,14 +190,17 @@ def tile_moe_bdx_glu_relu_kernel(
             )
             dht = turn.tile([P, X4, P], F32, name="dht")
             nc.scalar.copy(dht[:], bank[:].rearrange("p (m t) -> p t m", t=X4))
-            turned_in[e, n] = dht
+            turned = pb.tile([P, X4, P], F32, name="turned")
+            for t in range(X4):
+                nc.tensor.transpose(turned[:, t, :], dht[:, t, :], ident[:])
+            turned_in[e, n] = turned
 
         def relu_a1(e, g, h):
             kept = a_tiles[1, e, g][:, :, HALF * h : HALF * (h + 1)]
             nc.scalar.activation(kept, kept, ACT.Relu)
 
         def step_a1(e, g, h):
-            if g == 1 and e in (2,3,):
+            if g == 1 and e in ():
                 return
             relu_a1(e, g, h)
             home = {(0, 1, 0): GB_B, (0, 1, 1): GB_C, (1, 1, 1): GB_A}.get((e, g, h), STEP[(4 * e + 2 * g + h) % len(STEP)])
@@ -205,7 +208,7 @@ def tile_moe_bdx_glu_relu_kernel(
             nc.scalar.activation(steps[e, g, h], a_tiles[1, e, g][:, :, HALF * h : HALF * (h + 1)], ACT.Sign)
 
         def step_on_vector(e):
-            both = placed([P, X4, C], BF16, f"step{e}", CLOSING[e - 1] + 2)
+            both = placed([P, X4, C], BF16, f"step{e}", X1 + 3)
             nc.vector.tensor_scalar(both[:], a_tiles[1, e, 1][:], 0.0, None, ALU.is_gt)
             for h in range(2):
                 steps[e, 1, h] = both[:, :, HALF * h : HALF * (h + 1)]
@@ -216,10 +219,12 @@ def tile_moe_bdx_glu_relu_kernel(
                 masked_home[e, g, h] = (RAW3[0], GATE3, D1, DY)[e]
             elif (g, h) == (1, 1):
                 masked_home[e, g, h] = masked_home[e, 0, 0]
+            elif e > 0 and h == 0:
+                masked_home[e, g, h] = masked_home[e - 1, 0, 1]
             elif e > 0:
-                masked_home[e, g, h] = masked_home[e - 1, h, 1 - h]
+                masked_home[e, g, h] = (X0 - 3, X1 - 3, X0)[e - 1]
             masked[e, g, h] = placed([P, X4, HALF], F32, f"a3m{e}{g}{h}", masked_home[e, g, h])
-            if (e, g) == (0, 0):
+            if (e, g) == (0, 0) or (g, h) == (0, 1):
                 nc.vector.scalar_tensor_tensor(
                     masked[e, g, h][:], a_tiles[1, e, g][:, :, cols], 0.0, a_tiles[3, e, g][:, :, cols], ALU.is_gt, ALU.mult
                 )
@@ -232,22 +237,16 @@ def tile_moe_bdx_glu_relu_kernel(
                 d_tiles[1, e] = placed([P, NG * X4 * C], BF16, f"d1_{e}", (D1, D1, DY, DY + 8)[e])
                 d_tiles[3, e] = placed([P, NG * X4 * C], BF16, f"d3_{e}", D3)
             run = slice(X4 * P * n, X4 * P * (n + 1))
-            bank = pb.tile([P, X4, P], F32, name="turned")
-            for t in range(X4):
-                nc.tensor.transpose(bank[:, t, :], turned_in[e, n][:, t, :], ident[:])
+            bank = turned_in[e, n]
             h, r = divmod(s, 2)
-            nc.vector.tensor_tensor(
-                interleaved(d_tiles[3, e][:, run]),
-                by_lines(bank[:]),
-                by_lines(a_tiles[1, e, g][:, :, P * s : P * (s + 1)]),
-                ALU.mult,
-            )
-            nc.vector.tensor_tensor(
-                interleaved(d_tiles[1, e][:, run]),
-                by_lines(bank[:]),
-                by_lines(masked[e, g, h][:, :, P * r : P * (r + 1)]),
-                ALU.mult,
-            )
+            factors = {
+                3: a_tiles[1, e, g][:, :, P * s : P * (s + 1)],
+                1: masked[e, g, h][:, :, P * r : P * (r + 1)],
+            }
+            for which in (1, 3) if n == NG * SB - 1 else (3, 1):
+                nc.vector.tensor_tensor(
+                    interleaved(d_tiles[which, e][:, run]), by_lines(bank[:]), by_lines(factors[which]), ALU.mult
+                )
 
         def quantise_d(which, e, first, count):
             cols = C * count
@@ -263,30 +262,24 @@ def tile_moe_bdx_glu_relu_kernel(
             for g in range(count):
                 codes[which, e, first + g] = (words[:, C * g : C * (g + 1)], scales[:, C * g : C * (g + 1)])
 
-        def second_product(e):
-            banks = [pc.tile([P, C], F32, name=f"dx_bank{kb}") for kb in range(KB)]
-            for n in range(2 * NG):
-                g = n // 2
-                for kb in range(KB):
-                    which = (3, 1)[n % 2]
-                    w, sc = (w1_w, w1_sc) if which == 1 else (w3_w, w3_sc)
-                    words, scales = codes[which, e, g]
-                    nc.tensor.matmul_mx(
-                        out=banks[kb][:],
-                        lhsT=w[:, NG * e + g, 2 * P * kb : 2 * P * (kb + 1)].bitcast(E2M1),
-                        lhsT_scale=sc[:, NG * e + g, P * kb : P * (kb + 1)],
-                        rhs=words.bitcast(E5M2),
-                        rhs_scale=scales,
-                        start=(n == 0),
-                        stop=(n == 2 * NG - 1),
-                    )
-            dx_banks[e] = banks
-
-        def keep_dx(e):
-            for kb in range(KB):
-                if e == 0:
-                    dx.append(placed([P, S], F32, f"dx{kb}", DX + 8 * kb))
-                nc.scalar.copy(dx[kb][:, C * e : C * (e + 1)], dx_banks[e][kb][:])
+        def second_product(e, kb):
+            bank = pc.tile([P, C], F32, name="dx_bank")
+            passes = [(which, g) for g in range(NG) for which in (1, 3)]
+            for n, (which, g) in enumerate(passes):
+                w, sc = (w1_w, w1_sc) if which == 1 else (w3_w, w3_sc)
+                words, scales = codes[which, e, g]
+                nc.tensor.matmul_mx(
+                    out=bank[:],
+                    lhsT=w[:, NG * e + g, 2 * P * kb : 2 * P * (kb + 1)].bitcast(E2M1),
+                    lhsT_scale=sc[:, NG * e + g, P * kb : P * (kb + 1)],
+                    rhs=words.bitcast(E5M2),
+                    rhs_scale=scales,
+                    start=(n == 0),
+                    stop=(n == len(passes) - 1),
+                )
+            if e == 0:
+                dx.append(placed([P, S], F32, f"dx{kb}", DX + 8 * kb))
+            nc.scalar.copy(dx[kb][:, C * e : C * (e + 1)], bank[:])
 
         relu_a1(0, 0, 0)
         relu_a1(0, 0, 1)
@@ -329,26 +322,24 @@ def tile_moe_bdx_glu_relu_kernel(
             hidden(e, 3)
             if not last:
                 mask_a3(e + 1, 0, 0)
-            if e in (2,3,):
+            if e in ():
                 relu_a1(e, 1, 0)
             if e > 1:
                 first_product(e, 6)
             if not last:
-                step_a1(e + 1, 0, 1)
-            if e in (2,3,):
+                relu_a1(e + 1, 0, 1)
+            if e in ():
                 relu_a1(e, 1, 1)
             if e > 1:
                 first_product(e, 7)
             if last:
-                second_product(2)
-                keep_dx(2)
+                for kb in range(KB):
+                    second_product(2, kb)
             hidden(e, 4)
             hidden(e, 5)
             if last:
                 quantise_d(3, e, 0, 1)
                 quantise_d(1, e, 0, 1)
-            if not last:
-                mask_a3(e + 1, 0, 1)
             if e == 0:
                 for n in range(4):
                     weave_g(1 + n // 2, HALF * (n % 2), HALF)
@@ -361,8 +352,8 @@ def tile_moe_bdx_glu_relu_kernel(
                 for n in range(1, 4):
                     first_product(e + 1, n)
             if e in (1, 2):
-                second_product(e - 1)
-                keep_dx(e - 1)
+                for kb in range(KB):
+                    second_product(e - 1, kb)
             hidden(e, 6)
             hidden(e, 7)
             if e == 0:
@@ -382,11 +373,12 @@ def tile_moe_bdx_glu_relu_kernel(
                 load_w13(1)
                 quantise_g(3, 0, C)
             if last:
-                quantise_d(3, e, 1, 1)
                 quantise_d(1, e, 1, 1)
+                quantise_d(3, e, 1, 1)
             else:
-                if e + 1 in (2,3,):
+                if e + 1 in ():
                     step_on_vector(e + 1)
+                mask_a3(e + 1, 0, 1)
                 quantise_d(3, e, 0, NG)
                 quantise_d(1, e, 0, NG)
             if e == 0:
@@ -398,8 +390,8 @@ def tile_moe_bdx_glu_relu_kernel(
                 step_a1(1, 1, 1)
                 for n in range(4, 8):
                     first_product(1, n)
-        second_product(E - 1)
-        keep_dx(E - 1)
+        for kb in range(KB):
+            second_product(E - 1, kb)
 
         for kb in range(KB):
             first = placed([P, T], F32, f"first{kb}", SLOT[1] + 4 * kb)

@@ -54,10 +54,10 @@ def tile_moe_bdx_glu_relu_kernel(
         X0 = 19
         SLOT = [23 + 8 * ((n - 3) % 6) for n in range(6)]
         RAW3 = [71 + 8 * n for n in range(4)]
-        GATE3, D1, D3, GB_A, GB_B, GB_C, X1 = 103, 107, 115, 123, 127, 131, 138
+        GATE3, D1, D3, GB_A, GB_B, GB_C, X1 = 105, 107, 115, 123, 127, 131, 138
         DX = 156
         STEP = [146 + 2 * n for n in range(5)]
-        CLOSING = (X0 + 1, X1 + 1, X0 - 3, DY)
+        CLOSING = (X0 + 1, X1 + 1, X0 - 3, DY + 8)
 
         offs_sb = held.tile([P, S // 16], U16, name="offs_sb")
         pos1_sb = held.tile([P, T // 16], U16, name="pos1_sb")
@@ -159,7 +159,7 @@ def tile_moe_bdx_glu_relu_kernel(
 
         def weave_g(e, first, count):
             if first == 0:
-                g_bf16[e] = placed([P, X4 * C], BF16, f"gb{e}", (GB_A, GB_B, GB_C, GB_A)[e])
+                g_bf16[e] = placed([P, X4 * C], BF16, f"gb{e}", (X1, GB_B, GB_C, GB_A)[e])
             run = g_bf16[e][:, X4 * first : X4 * (first + count)]
             nc.scalar.copy(interleaved(run), by_lines(g_planes[e][:, :, first : first + count]))
 
@@ -216,7 +216,7 @@ def tile_moe_bdx_glu_relu_kernel(
         def mask_a3(e, g, h):
             cols = slice(HALF * h, HALF * (h + 1))
             if (g, h) == (1, 0):
-                masked_home[e, g, h] = (RAW3[0], GATE3, D1, DY)[e]
+                masked_home[e, g, h] = (RAW3[0], GATE3, DY, DY + 8)[e]
             elif (g, h) == (1, 1):
                 masked_home[e, g, h] = masked_home[e, 0, 0]
             elif e > 0 and h == 0:
@@ -234,7 +234,7 @@ def tile_moe_bdx_glu_relu_kernel(
         def hidden(e, n):
             g, s = divmod(n, SB)
             if n == 0:
-                d_tiles[1, e] = placed([P, NG * X4 * C], BF16, f"d1_{e}", (D1, D1, DY, DY + 8)[e])
+                d_tiles[1, e] = placed([P, NG * X4 * C], BF16, f"d1_{e}", (D1, DY, DY + 8, D1)[e])
                 d_tiles[3, e] = placed([P, NG * X4 * C], BF16, f"d3_{e}", D3)
             run = slice(X4 * P * n, X4 * P * (n + 1))
             bank = turned_in[e, n]
@@ -256,7 +256,10 @@ def tile_moe_bdx_glu_relu_kernel(
                 scales = placed([P, cols], U8, f"d_scales{which}{e}", CLOSING[e])
             else:
                 scales = held.tile([P, cols], U8, name="d_scales1", align_bytes=64, bufs=2)
-            words = held.tile([P, cols], U32, name=f"d_words{which}", align_bytes=64, bufs=2)
+            if which == 1 and e < 2:
+                words = placed([P, cols], U32, f"d_words1{e}", (GB_C, GB_A)[e])
+            else:
+                words = held.tile([P, cols], U32, name=f"d_words{which}", align_bytes=64, bufs=2)
             run = d_tiles[which, e][:, X4 * C * first : X4 * C * (first + count)]
             nc.vector.quantize_mx(out=words[:].bitcast(E5M2), scales=scales[:], in_=run)
             for g in range(count):
@@ -326,8 +329,6 @@ def tile_moe_bdx_glu_relu_kernel(
                 relu_a1(e, 1, 0)
             if e > 1:
                 first_product(e, 6)
-            if not last:
-                relu_a1(e + 1, 0, 1)
             if e in ():
                 relu_a1(e, 1, 1)
             if e > 1:
@@ -379,10 +380,12 @@ def tile_moe_bdx_glu_relu_kernel(
                 if e + 1 in ():
                     step_on_vector(e + 1)
                 mask_a3(e + 1, 0, 1)
+                relu_a1(e + 1, 0, 1)
                 quantise_d(3, e, 0, NG)
+                if e == 0:
+                    quantise_g(2, 0, C)
                 quantise_d(1, e, 0, NG)
             if e == 0:
-                quantise_g(2, 0, C)
                 gather(3)
                 step_a1(1, 1, 0)
                 for n in range(4):

@@ -9,7 +9,11 @@ P = 128
 X4 = 4
 NG = H // 512
 SB = C // P
+STEPS = NG * SB
 KB = K // P
+HALF = C // 2
+LAST = E - 1
+STEP_ON_VECTOR = 2
 
 F32 = mybir.dt.float32
 BF16 = mybir.dt.bfloat16
@@ -25,13 +29,31 @@ ACT = mybir.ActivationFunctionType
 FLOPS = 2 * S * N * H + 2 * 2 * S * H * K
 BYTES = 4 * (N * T + 2 * H * S + S + K * T) + E * (N * H + 2 * H * K) // 2 + E * (N * H + 2 * H * K) // 32 + 2 * 128 * 256
 
+DY = 0
+MASKED_A = 19
+A1 = (47, 55, 63, 23, 31, 39)
+A3 = (71, 79, 87, 95)
+GATE_LAST = 105
+DA1, DA3 = 107, 115
+WOVEN_A, WOVEN_B, WOVEN_C = 123, 127, 131
+MASKED_B = 138
+STEP_RING = (146, 148, 150, 152, 154)
+DX = 156
+
+A1_PLACE = {(0, 0): 2, (0, 1): 3, (1, 0): 4, (1, 1): 1, (2, 0): 5, (2, 1): 0, (3, 0): 2, (3, 1): 4}
+A3_PLACE = {(0, 0): 0, (0, 1): 1, (1, 0): 2, (1, 1): 3, (2, 0): 1, (2, 1): 2, (3, 0): 3, (3, 1): 1}
+
 
 def by_lines(planes):
     return planes.rearrange("p t (c i) -> p c t i", i=4)
 
 
-def interleaved(flat):
+def woven(flat):
     return flat.rearrange("p (c i t) -> p c t i", i=4, t=X4)
+
+
+def quarter(h):
+    return slice(HALF * h, HALF * (h + 1))
 
 
 def tile_moe_bdx_glu_relu_kernel(
@@ -41,23 +63,13 @@ def tile_moe_bdx_glu_relu_kernel(
     with ExitStack() as ctx:
         held = ctx.enter_context(tc.tile_pool(name="held", bufs=1))
         arena = ctx.enter_context(tc.tile_pool(name="arena", bufs=1))
-        turn = ctx.enter_context(tc.tile_pool(name="turn", bufs=4))
-        pa = ctx.enter_context(tc.psum_pool(name="pa", bufs=3))
-        pb = ctx.enter_context(tc.psum_pool(name="pb", bufs=4))
-        pc = ctx.enter_context(tc.psum_pool(name="pc", bufs=1))
+        unturned = ctx.enter_context(tc.tile_pool(name="unturned", bufs=4))
+        dh_banks = ctx.enter_context(tc.psum_pool(name="dh_banks", bufs=3))
+        turned_banks = ctx.enter_context(tc.psum_pool(name="turned_banks", bufs=4))
+        dx_banks = ctx.enter_context(tc.psum_pool(name="dx_banks", bufs=1))
 
         def placed(shape, dtype, name, kib):
             return arena.tile(shape, dtype, name=name, offset=int(1024 * kib), align_bytes=64)
-
-        HALF = C // 2
-        DY = 0
-        X0 = 19
-        SLOT = [23 + 8 * ((n - 3) % 6) for n in range(6)]
-        RAW3 = [71 + 8 * n for n in range(4)]
-        GATE3, D1, D3, GB_A, GB_B, GB_C, X1 = 105, 107, 115, 123, 127, 131, 138
-        DX = 156
-        STEP = [146 + 2 * n for n in range(5)]
-        CLOSING = (X0 + 1, X1 + 1, X0 - 3, DY + 8)
 
         offs_sb = held.tile([P, S // 16], U16, name="offs_sb")
         pos1_sb = held.tile([P, T // 16], U16, name="pos1_sb")
@@ -66,19 +78,23 @@ def tile_moe_bdx_glu_relu_kernel(
         w1_sc = held.tile([P, E * NG, K], U8, name="w1_sc", align_bytes=64)
         w3_sc = held.tile([P, E * NG, K], U8, name="w3_sc", align_bytes=64)
         ident = held.tile([P, P], F32, name="ident")
-        for plane in (w2_sc, w1_sc, w3_sc):
-            nc.vector.memset(plane[:].rearrange("p e i -> p (e i)").bitcast(I32), 0)
+        for scale_tile in (w2_sc, w1_sc, w3_sc):
+            nc.vector.memset(scale_tile[:].rearrange("p e i -> p (e i)").bitcast(I32), 0)
         make_identity(nc, ident[:])
 
-        dy_rows = dyT.rearrange("(p t) s -> t p s", t=X4)
-        dy = []
-        gates = {}
-        w2_w = {}
-        a_tiles = {}
+        dy, dx = [], []
+        gates, w2_w, saved = {}, {}, {}
+        g_planes, g_woven, g_codes = {}, {}, {}
+        dh_turned, steps, masked, da, da_codes = {}, {}, {}, {}, {}
+        masked_place = {(0, 0, 0): MASKED_A, (0, 0, 1): MASKED_B}
+
+        def load_dy(t):
+            dy.append(placed([P, T], F32, f"dy{t}", DY + 4 * t))
+            nc.sync.dma_start(dy[t][:], dyT.rearrange("(p t) s -> t p s", t=X4)[t])
 
         def load_gate(e):
-            if e == E - 1:
-                gates[e] = placed([P, C], F32, f"gate{e}", GATE3)
+            if e == LAST:
+                gates[e] = placed([P, C], F32, f"gate{e}", GATE_LAST)
             else:
                 gates[e] = held.tile([P, C], F32, name=f"gate{e}")
             nc.sync.dma_start(gates[e][:], gate[0:P, C * e : C * (e + 1)])
@@ -87,322 +103,287 @@ def tile_moe_bdx_glu_relu_kernel(
             w2_w[e] = held.tile([P, 2 * H], U8, name=f"w2_{e}", align_bytes=64)
             nc.sync.dma_start(w2_w[e][:].bitcast(I32), w2_words[e, 0].bitcast(I32))
 
-        def load_scales(queue, plane, scales, lo, hi):
+        def load_scales(queue, scale_tile, scales, lo, hi):
             by_row = scales.bitcast(I32).rearrange("e s f i -> f (e s) i")
             for q in range(4):
-                queue.dma_start(plane[32 * q : 32 * q + 4, lo:hi].bitcast(I32), by_row[4 * q : 4 * q + 4, lo:hi])
+                queue.dma_start(scale_tile[32 * q : 32 * q + 4, lo:hi].bitcast(I32), by_row[4 * q : 4 * q + 4, lo:hi])
 
-        a1_home = {(0, 0): 2, (0, 1): 3, (1, 0): 4, (1, 1): 1, (2, 0): 5, (2, 1): 0, (3, 0): 2, (3, 1): 4}
-        a3_home = {(0, 0): 0, (0, 1): 1, (1, 0): 2, (1, 1): 3, (2, 0): 1, (2, 1): 2, (3, 0): 3, (3, 1): 1}
-
-        def load_a(which, e, g, h=None):
+        def load_saved(which, e, g, h=None):
             if not h:
-                home = SLOT[a1_home[e, g]] if which == 1 else RAW3[a3_home[e, g]]
-                a_tiles[which, e, g] = placed([P, X4, C], F32, f"a{which}_{e}{g}", home)
-            lo, hi = (0, C) if h is None else (HALF * h, HALF * (h + 1))
-            saved = (a1 if which == 1 else a3)[512 * g : 512 * (g + 1), C * e + lo : C * e + hi]
-            nc.sync.dma_start(a_tiles[which, e, g][:, :, lo:hi], saved.rearrange("(p t) s -> p t s", t=X4))
+                place = A1[A1_PLACE[e, g]] if which == 1 else A3[A3_PLACE[e, g]]
+                saved[which, e, g] = placed([P, X4, C], F32, f"a{which}_{e}{g}", place)
+            cols = slice(0, C) if h is None else quarter(h)
+            rows = (a1 if which == 1 else a3)[512 * g : 512 * (g + 1), C * e + cols.start : C * e + cols.stop]
+            nc.sync.dma_start(saved[which, e, g][:, :, cols], rows.rearrange("(p t) s -> p t s", t=X4))
 
         def load_w13(pair):
-            lo, hi = E * pair, E * (pair + 1)
-            for tile_w, words, plane, scales in ((w3_w, w3_words, w3_sc, w3_scales), (w1_w, w1_words, w1_sc, w1_scales)):
-                load_scales(nc.sync, plane, scales, lo, hi)
+            lo, hi = 2 * NG * pair, 2 * NG * (pair + 1)
+            for w, words, scale_tile, scales in ((w3_w, w3_words, w3_sc, w3_scales), (w1_w, w1_words, w1_sc, w1_scales)):
+                load_scales(nc.sync, scale_tile, scales, lo, hi)
                 by_pass = words.bitcast(I32).rearrange("e s p k -> p (e s) k")
-                nc.sync.dma_start(tile_w[:, lo:hi].bitcast(I32), by_pass[:, lo:hi])
-
-        def load_dy(t):
-            dy_t = placed([P, T], F32, f"dy{t}", DY + 4 * t)
-            nc.sync.dma_start(dy_t[:], dy_rows[t])
-            dy.append(dy_t)
-
-        load_scales(nc.gpsimd, w2_sc, w2_scales, 0, E)
-        nc.sync.dma_start(offs_sb[:], offs)
-        load_dy(0)
-        load_gate(0)
-        load_gate(1)
-        load_gate(2)
-        load_a(1, 0, 0, 0)
-        load_dy(1)
-        load_a(1, 0, 0, 1)
-        load_dy(2)
-        load_a(1, 0, 1, 0)
-        load_a(1, 0, 1, 1)
-        load_dy(3)
-        load_a(1, 1, 0, 0)
-        load_w2(0)
-        load_a(3, 0, 0)
-        load_a(1, 1, 0, 1)
-        load_a(3, 0, 1)
-        load_a(3, 1, 0)
-        w1_w = held.tile([P, E * NG, 2 * K], U8, name="w1_w", align_bytes=64)
-        w3_w = held.tile([P, E * NG, 2 * K], U8, name="w3_w", align_bytes=64)
-
-        dx = []
-
-        g_planes = {}
-        g_bf16 = {}
-        g_codes = {}
-        turned_in = {}
-        steps = {}
-        masked = {}
-        masked_home = {(0, 0, 0): X0, (0, 0, 1): X1}
-        d_tiles = {}
-        codes = {}
+                nc.sync.dma_start(w[:, lo:hi].bitcast(I32), by_pass[:, lo:hi])
 
         def gather(e):
-            g4 = placed([P, X4, C], F32, f"g4_{e}", (SLOT[0], DX, DX + 8, X0 + 3)[e])
+            g_planes[e] = placed([P, X4, C], F32, f"g_planes{e}", (A1[0], DX, DX + 8, MASKED_A + 3)[e])
             for t in range(X4):
-                nc.vector.tensor_tensor(
-                    g4[:, t, :], dy[t][:].indirect(offs_sb[:, (C // 16) * e : (C // 16) * (e + 1)]), gates[e][:], ALU.mult
-                )
-            g_planes[e] = g4
+                picked = dy[t][:].indirect(offs_sb[:, (C // 16) * e : (C // 16) * (e + 1)])
+                nc.vector.tensor_tensor(g_planes[e][:, t, :], picked, gates[e][:], ALU.mult)
 
-        def weave_g(e, first, count):
-            if first == 0:
-                g_bf16[e] = placed([P, X4 * C], BF16, f"gb{e}", (X1, GB_B, GB_C, GB_A)[e])
-            run = g_bf16[e][:, X4 * first : X4 * (first + count)]
-            nc.scalar.copy(interleaved(run), by_lines(g_planes[e][:, :, first : first + count]))
+        def weave_g(e, h):
+            if h == 0:
+                g_woven[e] = placed([P, X4 * C], BF16, f"g_woven{e}", (MASKED_B, WOVEN_B, WOVEN_C, WOVEN_A)[e])
+            run = g_woven[e][:, X4 * HALF * h : X4 * HALF * (h + 1)]
+            nc.scalar.copy(woven(run), by_lines(g_planes[e][:, :, quarter(h)]))
 
-        def quantise_g(e, first, count):
-            if first == 0:
+        def quantise_g(e, cols):
+            if cols.start == 0:
                 if e == 0:
                     scales = held.tile([P, C], U8, name="g_scales0", align_bytes=64)
                 else:
-                    scales = placed([P, C], U8, f"g_scales{e}", {1: X0 + 2, 2: X0 + 2.5, 3: X1 + 2}[e])
+                    scales = placed([P, C], U8, f"g_scales{e}", (MASKED_A + 2, MASKED_A + 2.5, MASKED_B + 2)[e - 1])
                 g_codes[e] = (held.tile([P, C], U32, name="g_words", align_bytes=64, bufs=3), scales)
             words, scales = g_codes[e]
-            cols = slice(first, first + count)
-            run = g_bf16[e][:, X4 * first : X4 * (first + count)]
+            run = g_woven[e][:, X4 * cols.start : X4 * cols.stop]
             nc.vector.quantize_mx(out=words[:, cols].bitcast(E5M2), scales=scales[:, cols], in_=run)
 
         def first_product(e, n):
             g, s = divmod(n, SB)
             words, scales = g_codes[e]
-            bank = pa.tile([P, 512], F32, name="dh_bank")
+            bank = dh_banks.tile([P, 512], F32, name="dh_bank")
             nc.tensor.matmul_mx(
                 out=bank[:],
-                lhsT=words[:, P * s : P * s + P].bitcast(E5M2),
-                lhsT_scale=scales[:, P * s : P * s + P],
-                rhs=w2_w[e][:, 1024 * g : 1024 * g + 1024].bitcast(E2M1),
-                rhs_scale=w2_sc[:, e, 512 * g : 512 * g + 512],
+                lhsT=words[:, P * s : P * (s + 1)].bitcast(E5M2),
+                lhsT_scale=scales[:, P * s : P * (s + 1)],
+                rhs=w2_w[e][:, 1024 * g : 1024 * (g + 1)].bitcast(E2M1),
+                rhs_scale=w2_sc[:, e, 512 * g : 512 * (g + 1)],
                 start=True,
                 stop=True,
             )
-            dht = turn.tile([P, X4, P], F32, name="dht")
-            nc.scalar.copy(dht[:], bank[:].rearrange("p (m t) -> p t m", t=X4))
-            turned = pb.tile([P, X4, P], F32, name="turned")
+            dh_sb = unturned.tile([P, X4, P], F32, name="dh_sb")
+            nc.scalar.copy(dh_sb[:], bank[:].rearrange("p (m t) -> p t m", t=X4))
+            dh_turned[e, n] = turned_banks.tile([P, X4, P], F32, name="dh_turned")
             for t in range(X4):
-                nc.tensor.transpose(turned[:, t, :], dht[:, t, :], ident[:])
-            turned_in[e, n] = turned
+                nc.tensor.transpose(dh_turned[e, n][:, t, :], dh_sb[:, t, :], ident[:])
 
         def relu_a1(e, g, h):
-            kept = a_tiles[1, e, g][:, :, HALF * h : HALF * (h + 1)]
+            kept = saved[1, e, g][:, :, quarter(h)]
             nc.scalar.activation(kept, kept, ACT.Relu)
 
         def step_a1(e, g, h):
-            if g == 1 and e in ():
-                return
             relu_a1(e, g, h)
-            home = {(0, 1, 0): GB_B, (0, 1, 1): GB_C, (1, 1, 1): GB_A}.get((e, g, h), STEP[(4 * e + 2 * g + h) % len(STEP)])
-            steps[e, g, h] = placed([P, X4, HALF], BF16, f"step{e}{g}{h}", home)[:]
-            nc.scalar.activation(steps[e, g, h], a_tiles[1, e, g][:, :, HALF * h : HALF * (h + 1)], ACT.Sign)
+            under_woven = {(0, 1, 0): WOVEN_B, (0, 1, 1): WOVEN_C, (1, 1, 1): WOVEN_A}
+            place = under_woven.get((e, g, h), STEP_RING[(4 * e + 2 * g + h) % len(STEP_RING)])
+            steps[e, g, h] = placed([P, X4, HALF], BF16, f"step{e}{g}{h}", place)[:]
+            nc.scalar.activation(steps[e, g, h], saved[1, e, g][:, :, quarter(h)], ACT.Sign)
 
         def step_on_vector(e):
-            both = placed([P, X4, C], BF16, f"step{e}", X1 + 3)
-            nc.vector.tensor_scalar(both[:], a_tiles[1, e, 1][:], 0.0, None, ALU.is_gt)
+            both = placed([P, X4, C], BF16, f"step{e}", MASKED_B + 3)
+            nc.vector.tensor_scalar(both[:], saved[1, e, 1][:], 0.0, None, ALU.is_gt)
             for h in range(2):
-                steps[e, 1, h] = both[:, :, HALF * h : HALF * (h + 1)]
+                steps[e, 1, h] = both[:, :, quarter(h)]
 
         def mask_a3(e, g, h):
-            cols = slice(HALF * h, HALF * (h + 1))
             if (g, h) == (1, 0):
-                masked_home[e, g, h] = (RAW3[0], GATE3, DY, DY + 8)[e]
+                masked_place[e, g, h] = (A3[0], GATE_LAST, DY, DY + 8)[e]
             elif (g, h) == (1, 1):
-                masked_home[e, g, h] = masked_home[e, 0, 0]
-            elif e > 0 and h == 0:
-                masked_home[e, g, h] = masked_home[e - 1, 0, 1]
+                masked_place[e, g, h] = masked_place[e, 0, 0]
             elif e > 0:
-                masked_home[e, g, h] = (X0 - 3, X1 - 3, X0)[e - 1]
-            masked[e, g, h] = placed([P, X4, HALF], F32, f"a3m{e}{g}{h}", masked_home[e, g, h])
-            if (e, g) == (0, 0) or (g, h) == (0, 1):
-                nc.vector.scalar_tensor_tensor(
-                    masked[e, g, h][:], a_tiles[1, e, g][:, :, cols], 0.0, a_tiles[3, e, g][:, :, cols], ALU.is_gt, ALU.mult
-                )
+                masked_place[e, g, h] = masked_place[e - 1, h, 1 - h]
+            masked[e, g, h] = placed([P, X4, HALF], F32, f"masked{e}{g}{h}", masked_place[e, g, h])
+            raw = saved[3, e, g][:, :, quarter(h)]
+            if (e, g) == (0, 0):
+                kept = saved[1, e, g][:, :, quarter(h)]
+                nc.vector.scalar_tensor_tensor(masked[e, g, h][:], kept, 0.0, raw, ALU.is_gt, ALU.mult)
             else:
-                nc.gpsimd.tensor_tensor(masked[e, g, h][:], a_tiles[3, e, g][:, :, cols], steps[e, g, h], ALU.mult)
+                nc.gpsimd.tensor_tensor(masked[e, g, h][:], raw, steps[e, g, h], ALU.mult)
 
         def hidden(e, n):
             g, s = divmod(n, SB)
-            if n == 0:
-                d_tiles[1, e] = placed([P, NG * X4 * C], BF16, f"d1_{e}", (D1, DY, DY + 8, D1)[e])
-                d_tiles[3, e] = placed([P, NG * X4 * C], BF16, f"d3_{e}", D3)
-            run = slice(X4 * P * n, X4 * P * (n + 1))
-            bank = turned_in[e, n]
             h, r = divmod(s, 2)
+            if n == 0:
+                da[1, e] = placed([P, NG * X4 * C], BF16, f"da1_{e}", (DA1, DY, DY + 8, A1[3])[e])
+                da[3, e] = placed([P, NG * X4 * C], BF16, f"da3_{e}", DA3)
             factors = {
-                3: a_tiles[1, e, g][:, :, P * s : P * (s + 1)],
+                3: saved[1, e, g][:, :, P * s : P * (s + 1)],
                 1: masked[e, g, h][:, :, P * r : P * (r + 1)],
             }
-            for which in (1, 3) if n == NG * SB - 1 else (3, 1):
-                nc.vector.tensor_tensor(
-                    interleaved(d_tiles[which, e][:, run]), by_lines(bank[:]), by_lines(factors[which]), ALU.mult
-                )
+            for which in (1, 3) if n == STEPS - 1 and e < LAST else (3, 1):
+                run = da[which, e][:, X4 * P * n : X4 * P * (n + 1)]
+                nc.vector.tensor_tensor(woven(run), by_lines(dh_turned[e, n][:]), by_lines(factors[which]), ALU.mult)
 
-        def quantise_d(which, e, first, count):
+        def quantise_da(which, e, first, count):
             cols = C * count
-            if e == E - 1:
-                scales = placed([P, cols], U8, f"d_scales{which}{e}{first}", CLOSING[e] + 2 * first + (which == 1))
+            if e == LAST:
+                place = masked_place[e, 1, 0] + 2 * first + (which == 1)
+                scales = placed([P, cols], U8, f"da_scales{which}{e}{first}", place)
             elif which == 3:
-                scales = placed([P, cols], U8, f"d_scales{which}{e}", CLOSING[e])
+                scales = placed([P, cols], U8, f"da_scales{which}{e}", (MASKED_A + 1, MASKED_B + 1, A3[0])[e])
             else:
-                scales = held.tile([P, cols], U8, name="d_scales1", align_bytes=64, bufs=2)
-            if which == 1 and e < 2:
-                words = placed([P, cols], U32, f"d_words1{e}", (GB_C, GB_A)[e])
+                scales = held.tile([P, cols], U8, name="da_scales1", align_bytes=64, bufs=2)
+            if which == 1 and e + 2 < E:
+                words = placed([P, cols], U32, f"da_words1{e}", (WOVEN_C, WOVEN_A)[e])
             else:
-                words = held.tile([P, cols], U32, name=f"d_words{which}", align_bytes=64, bufs=2)
-            run = d_tiles[which, e][:, X4 * C * first : X4 * C * (first + count)]
+                words = held.tile([P, cols], U32, name=f"da_words{which}", align_bytes=64, bufs=2)
+            run = da[which, e][:, X4 * C * first : X4 * C * (first + count)]
             nc.vector.quantize_mx(out=words[:].bitcast(E5M2), scales=scales[:], in_=run)
             for g in range(count):
-                codes[which, e, first + g] = (words[:, C * g : C * (g + 1)], scales[:, C * g : C * (g + 1)])
+                da_codes[which, e, first + g] = (words[:, C * g : C * (g + 1)], scales[:, C * g : C * (g + 1)])
 
-        def second_product(e, kb):
-            bank = pc.tile([P, C], F32, name="dx_bank")
-            passes = [(which, g) for g in range(NG) for which in (1, 3)]
-            for n, (which, g) in enumerate(passes):
-                w, sc = (w1_w, w1_sc) if which == 1 else (w3_w, w3_sc)
-                words, scales = codes[which, e, g]
-                nc.tensor.matmul_mx(
-                    out=bank[:],
-                    lhsT=w[:, NG * e + g, 2 * P * kb : 2 * P * (kb + 1)].bitcast(E2M1),
-                    lhsT_scale=sc[:, NG * e + g, P * kb : P * (kb + 1)],
-                    rhs=words.bitcast(E5M2),
-                    rhs_scale=scales,
-                    start=(n == 0),
-                    stop=(n == len(passes) - 1),
-                )
-            if e == 0:
-                dx.append(placed([P, S], F32, f"dx{kb}", DX + 8 * kb))
-            nc.scalar.copy(dx[kb][:, C * e : C * (e + 1)], bank[:])
+        def second_product(e):
+            passes = [(which, g) for g in range(NG) for which in (3, 1)]
+            for kb in range(KB):
+                bank = dx_banks.tile([P, C], F32, name="dx_bank")
+                for n, (which, g) in enumerate(passes):
+                    w, scale_tile = (w1_w, w1_sc) if which == 1 else (w3_w, w3_sc)
+                    words, scales = da_codes[which, e, g]
+                    nc.tensor.matmul_mx(
+                        out=bank[:],
+                        lhsT=w[:, NG * e + g, 2 * P * kb : 2 * P * (kb + 1)].bitcast(E2M1),
+                        lhsT_scale=scale_tile[:, NG * e + g, P * kb : P * (kb + 1)],
+                        rhs=words.bitcast(E5M2),
+                        rhs_scale=scales,
+                        start=(n == 0),
+                        stop=(n == len(passes) - 1),
+                    )
+                if e == 0:
+                    dx.append(placed([P, S], F32, f"dx{kb}", DX + 8 * kb))
+                nc.scalar.copy(dx[kb][:, C * e : C * (e + 1)], bank[:])
 
-        relu_a1(0, 0, 0)
-        relu_a1(0, 0, 1)
-        step_a1(0, 1, 0)
-        step_a1(0, 1, 1)
-        for e in range(3):
+        load_scales(nc.gpsimd, w2_sc, w2_scales, 0, E)
+        nc.sync.dma_start(offs_sb[:], offs)
+        load_dy(0)
+        for e in range(LAST):
+            load_gate(e)
+        load_saved(1, 0, 0, 0)
+        load_dy(1)
+        load_saved(1, 0, 0, 1)
+        load_dy(2)
+        load_saved(1, 0, 1, 0)
+        load_saved(1, 0, 1, 1)
+        load_dy(3)
+        load_saved(1, 1, 0, 0)
+        load_w2(0)
+        load_saved(3, 0, 0)
+        load_saved(1, 1, 0, 1)
+        load_saved(3, 0, 1)
+        load_saved(3, 1, 0)
+        w1_w = held.tile([P, E * NG, 2 * K], U8, name="w1_w", align_bytes=64)
+        w3_w = held.tile([P, E * NG, 2 * K], U8, name="w3_w", align_bytes=64)
+
+        for h in range(2):
+            relu_a1(0, 0, h)
+        for h in range(2):
+            step_a1(0, 1, h)
+        for e in range(LAST):
             gather(e)
-        for first, count in ((0, HALF), (HALF, HALF)):
-            weave_g(0, first, count)
-            quantise_g(0, first, count)
-        load_a(1, 1, 1)
+        for h in range(2):
+            weave_g(0, h)
+            quantise_g(0, quarter(h))
+        load_saved(1, 1, 1)
         load_w2(1)
-        load_gate(3)
-        load_a(1, 2, 0)
-        load_a(3, 1, 1)
-        load_a(1, 2, 1)
-        for n in range(4):
+        load_gate(LAST)
+        load_saved(1, 2, 0)
+        load_saved(3, 1, 1)
+        load_saved(1, 2, 1)
+        for n in range(SB):
             first_product(0, n)
         for h in range(2):
             mask_a3(0, 0, h)
         step_a1(1, 0, 0)
-        for n in range(4, 8):
+        for n in range(SB, STEPS):
             first_product(0, n)
 
         for e in range(E):
-            last = e == E - 1
+            late = e >= 2
             mask_a3(e, 1, 0)
             hidden(e, 0)
             hidden(e, 1)
-            if e > 1:
+            if late and e != STEP_ON_VECTOR:
                 step_a1(e, 1, 1)
             mask_a3(e, 1, 1)
-            if e > 1:
-                first_product(e, 4)
-            if e in (1, 2):
+            if late:
+                first_product(e, SB)
+            if 0 < e < LAST:
                 step_a1(e + 1, 0, 0)
-            if e > 1:
-                first_product(e, 5)
+            if late:
+                first_product(e, SB + 1)
             hidden(e, 2)
             hidden(e, 3)
-            if not last:
+            if e < LAST:
                 mask_a3(e + 1, 0, 0)
-            if e in ():
+            if e == STEP_ON_VECTOR:
                 relu_a1(e, 1, 0)
-            if e > 1:
-                first_product(e, 6)
-            if e in ():
+            if late:
+                first_product(e, SB + 2)
+            if e < LAST:
+                step_a1(e + 1, 0, 1)
+            if e == STEP_ON_VECTOR:
                 relu_a1(e, 1, 1)
-            if e > 1:
-                first_product(e, 7)
-            if last:
-                for kb in range(KB):
-                    second_product(2, kb)
+            if late:
+                first_product(e, SB + 3)
+            if e == LAST:
+                second_product(e - 1)
             hidden(e, 4)
             hidden(e, 5)
-            if last:
-                quantise_d(3, e, 0, 1)
-                quantise_d(1, e, 0, 1)
-            if e == 0:
-                for n in range(4):
-                    weave_g(1 + n // 2, HALF * (n % 2), HALF)
-            if e == 1:
-                weave_g(3, 0, HALF)
-                weave_g(3, HALF, HALF)
-            if e in (1, 2):
+            if e < LAST:
+                mask_a3(e + 1, 0, 1)
+            else:
+                quantise_da(3, e, 0, 1)
+                quantise_da(1, e, 0, 1)
+            for woven_e in ((1, 2), (3,), (), ())[e]:
+                for h in range(2):
+                    weave_g(woven_e, h)
+            if 0 < e < LAST:
                 first_product(e + 1, 0)
-                step_a1(e + 1, 1, 0)
-                for n in range(1, 4):
+                if e + 1 != STEP_ON_VECTOR:
+                    step_a1(e + 1, 1, 0)
+                for n in range(1, SB):
                     first_product(e + 1, n)
-            if e in (1, 2):
-                for kb in range(KB):
-                    second_product(e - 1, kb)
+                second_product(e - 1)
             hidden(e, 6)
             hidden(e, 7)
+
             if e == 0:
-                load_a(3, 2, 0)
+                load_saved(3, 2, 0)
                 load_w2(2)
                 load_w13(0)
-                load_a(3, 2, 1)
-                load_a(1, 3, 0)
+                load_saved(3, 2, 1)
+                load_saved(1, 3, 0)
                 load_w2(3)
                 nc.sync.dma_start(pos1_sb[:], pos1)
                 nc.sync.dma_start(pos2_sb[:], pos2)
-                quantise_g(1, 0, C)
-            if e == 1:
-                load_a(3, 3, 0)
-                load_a(1, 3, 1)
-                load_a(3, 3, 1)
-                load_w13(1)
-                quantise_g(3, 0, C)
-            if last:
-                quantise_d(1, e, 1, 1)
-                quantise_d(3, e, 1, 1)
-            else:
-                if e + 1 in ():
+                quantise_g(1, slice(0, C))
+                quantise_da(3, e, 0, NG)
+                quantise_g(2, slice(0, C))
+                quantise_da(1, e, 0, NG)
+                gather(LAST)
+                for h in range(2):
+                    step_a1(1, 1, h)
+                    for n in range(SB * h, SB * (h + 1)):
+                        first_product(1, n)
+            elif e < LAST:
+                if e == 1:
+                    load_saved(3, 3, 0)
+                    load_saved(1, 3, 1)
+                    load_saved(3, 3, 1)
+                    load_w13(1)
+                    quantise_g(LAST, slice(0, C))
+                if e + 1 == STEP_ON_VECTOR:
                     step_on_vector(e + 1)
-                mask_a3(e + 1, 0, 1)
-                relu_a1(e + 1, 0, 1)
-                quantise_d(3, e, 0, NG)
-                if e == 0:
-                    quantise_g(2, 0, C)
-                quantise_d(1, e, 0, NG)
-            if e == 0:
-                gather(3)
-                step_a1(1, 1, 0)
-                for n in range(4):
-                    first_product(1, n)
-                step_a1(1, 1, 1)
-                for n in range(4, 8):
-                    first_product(1, n)
-        for kb in range(KB):
-            second_product(E - 1, kb)
+                quantise_da(3, e, 0, NG)
+                quantise_da(1, e, 0, NG)
+            else:
+                quantise_da(3, e, 1, 1)
+                quantise_da(1, e, 1, 1)
+        second_product(LAST)
 
         for kb in range(KB):
-            first = placed([P, T], F32, f"first{kb}", SLOT[1] + 4 * kb)
-            total = placed([P, T], F32, f"total{kb}", SLOT[5] + 4 * kb)
-            for lo, hi in ((0, 512), (512, T)):
+            first = placed([P, T], F32, f"first{kb}", A1[1] + 4 * kb)
+            total = placed([P, T], F32, f"total{kb}", A1[5] + 4 * kb)
+            for lo, hi in ((0, T // 2), (T // 2, T)):
                 nc.vector.tensor_copy(first[:, lo:hi], dx[kb][:].indirect(pos1_sb[:, lo // 16 : hi // 16]))
-            for lo, hi in ((0, 512), (512, T)) if kb == 0 else ((0, 512), (512, T - P), (T - P, T)):
-                nc.vector.tensor_tensor(
-                    total[:, lo:hi], dx[kb][:].indirect(pos2_sb[:, lo // 16 : hi // 16]), first[:, lo:hi], ALU.add
-                )
+            cuts = (0, T // 2, T) if kb < KB - 1 else (0, T // 2, T - P, T)
+            for lo, hi in zip(cuts, cuts[1:]):
+                picked = dx[kb][:].indirect(pos2_sb[:, lo // 16 : hi // 16])
+                nc.vector.tensor_tensor(total[:, lo:hi], picked, first[:, lo:hi], ALU.add)
                 nc.sync.dma_start(out[P * kb : P * (kb + 1), lo:hi], total[:, lo:hi])

@@ -108,13 +108,13 @@ def tile_moe_bdx_glu_relu_kernel(
             for q in range(4):
                 queue.dma_start(scale_tile[32 * q : 32 * q + 4, lo:hi].bitcast(I32), by_row[4 * q : 4 * q + 4, lo:hi])
 
-        def load_saved(which, e, g, h=None):
-            if not h:
+        def load_saved(which, e, g, pair=None):
+            if not pair:
                 place = A1[A1_PLACE[e, g]] if which == 1 else A3[A3_PLACE[e, g]]
                 saved[which, e, g] = placed([P, X4, C], F32, f"a{which}_{e}{g}", place)
-            cols = slice(0, C) if h is None else quarter(h)
-            rows = (a1 if which == 1 else a3)[512 * g : 512 * (g + 1), C * e + cols.start : C * e + cols.stop]
-            nc.sync.dma_start(saved[which, e, g][:, :, cols], rows.rearrange("(p t) s -> p t s", t=X4))
+            planes = slice(0, X4) if pair is None else slice(2 * pair, 2 * pair + 2)
+            rows = (a1 if which == 1 else a3)[512 * g : 512 * (g + 1), C * e : C * (e + 1)]
+            nc.sync.dma_start(saved[which, e, g][:, planes, :], rows.rearrange("(p t) s -> p t s", t=X4)[:, planes, :])
 
         def load_w13(pair):
             lo, hi = 2 * NG * pair, 2 * NG * (pair + 1)
@@ -169,8 +169,15 @@ def tile_moe_bdx_glu_relu_kernel(
             kept = saved[1, e, g][:, :, quarter(h)]
             nc.scalar.activation(kept, kept, ACT.Relu)
 
+        def relu_pair(e, g, pair):
+            kept = saved[1, e, g][:, 2 * pair : 2 * pair + 2, :]
+            nc.scalar.activation(kept, kept, ACT.Relu)
+
         def step_a1(e, g, h):
             relu_a1(e, g, h)
+            sign_a1(e, g, h)
+
+        def sign_a1(e, g, h):
             under_woven = {(0, 1, 0): WOVEN_B, (0, 1, 1): WOVEN_C, (1, 1, 1): WOVEN_A}
             place = under_woven.get((e, g, h), STEP_RING[(4 * e + 2 * g + h) % len(STEP_RING)])
             steps[e, g, h] = placed([P, X4, HALF], BF16, f"step{e}{g}{h}", place)[:]
@@ -232,7 +239,10 @@ def tile_moe_bdx_glu_relu_kernel(
         def second_product(e):
             passes = [(which, g) for g in range(NG) for which in (3, 1)]
             for kb in range(KB):
-                bank = dx_banks.tile([P, C], F32, name="dx_bank")
+                if e == LAST and kb > 0:
+                    bank = dh_banks.tile([P, C], F32, name="dh_bank")
+                else:
+                    bank = dx_banks.tile([P, C], F32, name="dx_bank")
                 for n, (which, g) in enumerate(passes):
                     w, scale_tile = (w1_w, w1_sc) if which == 1 else (w3_w, w3_sc)
                     words, scales = da_codes[which, e, g]
@@ -252,14 +262,15 @@ def tile_moe_bdx_glu_relu_kernel(
         load_scales(nc.gpsimd, w2_sc, w2_scales, 0, E)
         nc.sync.dma_start(offs_sb[:], offs)
         load_dy(0)
-        for e in range(LAST):
-            load_gate(e)
-        load_saved(1, 0, 0, 0)
-        load_dy(1)
-        load_saved(1, 0, 0, 1)
-        load_dy(2)
+        load_gate(0)
+        load_gate(1)
+        load_gate(2)
         load_saved(1, 0, 1, 0)
+        load_dy(1)
         load_saved(1, 0, 1, 1)
+        load_dy(2)
+        load_saved(1, 0, 0, 0)
+        load_saved(1, 0, 0, 1)
         load_dy(3)
         load_saved(1, 1, 0, 0)
         load_w2(0)
@@ -270,10 +281,12 @@ def tile_moe_bdx_glu_relu_kernel(
         w1_w = held.tile([P, E * NG, 2 * K], U8, name="w1_w", align_bytes=64)
         w3_w = held.tile([P, E * NG, 2 * K], U8, name="w3_w", align_bytes=64)
 
+        for pair in range(2):
+            relu_pair(0, 1, pair)
         for h in range(2):
-            relu_a1(0, 0, h)
-        for h in range(2):
-            step_a1(0, 1, h)
+            sign_a1(0, 1, h)
+        for pair in range(2):
+            relu_pair(0, 0, pair)
         for e in range(LAST):
             gather(e)
         for h in range(2):
@@ -289,7 +302,9 @@ def tile_moe_bdx_glu_relu_kernel(
             first_product(0, n)
         for h in range(2):
             mask_a3(0, 0, h)
-        step_a1(1, 0, 0)
+        for pair in range(2):
+            relu_pair(1, 0, pair)
+        sign_a1(1, 0, 0)
         for n in range(SB, STEPS):
             first_product(0, n)
 
@@ -303,7 +318,7 @@ def tile_moe_bdx_glu_relu_kernel(
             mask_a3(e, 1, 1)
             if late:
                 first_product(e, SB)
-            if 0 < e < LAST:
+            if late and e < LAST:
                 step_a1(e + 1, 0, 0)
             if late:
                 first_product(e, SB + 1)
@@ -315,7 +330,9 @@ def tile_moe_bdx_glu_relu_kernel(
                 relu_a1(e, 1, 0)
             if late:
                 first_product(e, SB + 2)
-            if e < LAST:
+            if e == 0:
+                sign_a1(1, 0, 1)
+            if late and e < LAST:
                 step_a1(e + 1, 0, 1)
             if e == STEP_ON_VECTOR:
                 relu_a1(e, 1, 1)
@@ -357,10 +374,15 @@ def tile_moe_bdx_glu_relu_kernel(
                 quantise_g(2, slice(0, C))
                 quantise_da(1, e, 0, NG)
                 gather(LAST)
+                step_a1(1, 1, 0)
+                for n in range(SB):
+                    first_product(1, n)
+                step_a1(1, 1, 1)
                 for h in range(2):
-                    step_a1(1, 1, h)
-                    for n in range(SB * h, SB * (h + 1)):
-                        first_product(1, n)
+                    first_product(1, SB + h)
+                    step_a1(2, 0, h)
+                first_product(1, SB + 2)
+                first_product(1, SB + 3)
             elif e < LAST:
                 if e == 1:
                     load_saved(3, 3, 0)

@@ -30,18 +30,16 @@ FLOPS = 2 * S * N * H + 2 * 2 * S * H * K
 BYTES = 4 * (N * T + 2 * H * S + S + K * T) + E * (N * H + 2 * H * K) // 2 + E * (N * H + 2 * H * K) // 32 + 2 * 128 * 256
 
 DY = 0
-MASKED_A = 19
-A1 = (47, 55, 63, 23, 31, 39)
-A3 = (71, 79, 87, 95)
-GATE_LAST = 105
-DA1, DA3 = 107, 115
-WOVEN_A, WOVEN_B, WOVEN_C = 123, 127, 131
-MASKED_B = 138
-STEP_RING = (146, 148, 150, 152, 154)
-DX = 156
-
-A1_PLACE = {(0, 0): 2, (0, 1): 3, (1, 0): 4, (1, 1): 1, (2, 0): 5, (2, 1): 0, (3, 0): 2, (3, 1): 4}
-A3_PLACE = {(0, 0): 0, (0, 1): 1, (1, 0): 2, (1, 1): 3, (2, 0): 1, (2, 1): 2, (3, 0): 3, (3, 1): 1}
+MASKED_REST = 16
+WOVEN = (22, MASKED_REST, 26, 22)
+A1 = {(0, 1): 30, (0, 0): 38, (1, 0): 46, (1, 1): 54, (2, 0): 62, (2, 1): DY, (3, 0): 38, (3, 1): 30}
+A3 = {(0, 0): 70, (1, 0): 78, (2, 0): DY + 8, (3, 0): 86, (0, 1): 94, (1, 1): 102, (2, 1): 94, (3, 1): 102}
+DA1, DA3 = 110, 118
+STEP_SECOND = (126, 130, WOVEN[3], 126)
+STEP_REST = (None, 134, 137, 134)
+DX = 140
+G_PLANES = (156, DX, DX + 8, 156)
+WORDS = {2: A3[2, 1], 3: A1[2, 0]}
 
 
 def by_lines(planes):
@@ -86,17 +84,13 @@ def tile_moe_bdx_glu_relu_kernel(
         gates, w2_w, saved = {}, {}, {}
         g_planes, g_woven, g_codes = {}, {}, {}
         dh_turned, steps, masked, da, da_codes = {}, {}, {}, {}, {}
-        masked_place = {(0, 0, 0): MASKED_A, (0, 0, 1): MASKED_B}
 
         def load_dy(t):
             dy.append(placed([P, T], F32, f"dy{t}", DY + 4 * t))
             nc.sync.dma_start(dy[t][:], dyT.rearrange("(p t) s -> t p s", t=X4)[t])
 
         def load_gate(e):
-            if e == LAST:
-                gates[e] = placed([P, C], F32, f"gate{e}", GATE_LAST)
-            else:
-                gates[e] = held.tile([P, C], F32, name=f"gate{e}")
+            gates[e] = held.tile([P, C], F32, name=f"gate{e}")
             nc.sync.dma_start(gates[e][:], gate[0:P, C * e : C * (e + 1)])
 
         def load_w2(e):
@@ -110,7 +104,7 @@ def tile_moe_bdx_glu_relu_kernel(
 
         def load_saved(which, e, g, pair=None):
             if not pair:
-                place = A1[A1_PLACE[e, g]] if which == 1 else A3[A3_PLACE[e, g]]
+                place = (A1 if which == 1 else A3)[e, g]
                 saved[which, e, g] = placed([P, X4, C], F32, f"a{which}_{e}{g}", place)
             planes = slice(0, X4) if pair is None else slice(2 * pair, 2 * pair + 2)
             rows = (a1 if which == 1 else a3)[512 * g : 512 * (g + 1), C * e : C * (e + 1)]
@@ -123,25 +117,26 @@ def tile_moe_bdx_glu_relu_kernel(
                 by_pass = words.bitcast(I32).rearrange("e s p k -> p (e s) k")
                 nc.sync.dma_start(w[:, lo:hi].bitcast(I32), by_pass[:, lo:hi])
 
-        def gather(e):
-            g_planes[e] = placed([P, X4, C], F32, f"g_planes{e}", (A1[0], DX, DX + 8, MASKED_A + 3)[e])
-            for t in range(X4):
-                picked = dy[t][:].indirect(offs_sb[:, (C // 16) * e : (C // 16) * (e + 1)])
-                nc.vector.tensor_tensor(g_planes[e][:, t, :], picked, gates[e][:], ALU.mult)
+        def gather(e, t):
+            if t == 0:
+                g_planes[e] = placed([P, X4, C], F32, f"g_planes{e}", G_PLANES[e])
+            picked = dy[t][:].indirect(offs_sb[:, (C // 16) * e : (C // 16) * (e + 1)])
+            nc.vector.tensor_tensor(g_planes[e][:, t, :], picked, gates[e][:], ALU.mult)
 
         def weave_g(e, h):
             if h == 0:
-                g_woven[e] = placed([P, X4 * C], BF16, f"g_woven{e}", (MASKED_B, WOVEN_B, WOVEN_C, WOVEN_A)[e])
+                g_woven[e] = placed([P, X4 * C], BF16, f"g_woven{e}", WOVEN[e])
             run = g_woven[e][:, X4 * HALF * h : X4 * HALF * (h + 1)]
             nc.scalar.copy(woven(run), by_lines(g_planes[e][:, :, quarter(h)]))
 
         def quantise_g(e, cols):
             if cols.start == 0:
-                if e == 0:
-                    scales = held.tile([P, C], U8, name="g_scales0", align_bytes=64)
+                if e >= 2:
+                    scales = placed([P, C], U8, f"g_scales{e}", A3[e - 2, 0] + 7)
                 else:
-                    scales = placed([P, C], U8, f"g_scales{e}", (MASKED_A + 2, MASKED_A + 2.5, MASKED_B + 2)[e - 1])
-                g_codes[e] = (held.tile([P, C], U32, name="g_words", align_bytes=64, bufs=3), scales)
+                    scales = held.tile([P, C], U8, name=f"g_scales{e}", align_bytes=64)
+                words = held.tile([P, C], U32, name="g_words", align_bytes=64, bufs=3)
+                g_codes[e] = (words, scales)
             words, scales = g_codes[e]
             run = g_woven[e][:, X4 * cols.start : X4 * cols.stop]
             nc.vector.quantize_mx(out=words[:, cols].bitcast(E5M2), scales=scales[:, cols], in_=run)
@@ -173,47 +168,52 @@ def tile_moe_bdx_glu_relu_kernel(
             kept = saved[1, e, g][:, 2 * pair : 2 * pair + 2, :]
             nc.scalar.activation(kept, kept, ACT.Relu)
 
-        def step_a1(e, g, h):
-            relu_a1(e, g, h)
-            sign_a1(e, g, h)
+        def sign_second(e, h):
+            if h == 0:
+                steps[e, 1] = placed([P, X4, C], BF16, f"step{e}1", STEP_SECOND[e])
+            nc.scalar.activation(steps[e, 1][:, :, quarter(h)], saved[1, e, 1][:, :, quarter(h)], ACT.Sign)
 
-        def sign_a1(e, g, h):
-            under_woven = {(0, 1, 0): WOVEN_B, (0, 1, 1): WOVEN_C, (1, 1, 1): WOVEN_A}
-            place = under_woven.get((e, g, h), STEP_RING[(4 * e + 2 * g + h) % len(STEP_RING)])
-            steps[e, g, h] = placed([P, X4, HALF], BF16, f"step{e}{g}{h}", place)[:]
-            nc.scalar.activation(steps[e, g, h], saved[1, e, g][:, :, quarter(h)], ACT.Sign)
+        def sign_rest(e):
+            steps[e, 0] = placed([P, X4, C - P], BF16, f"step{e}0", STEP_REST[e])
+            nc.scalar.activation(steps[e, 0][:], saved[1, e, 0][:, :, P:C], ACT.Sign)
 
         def step_on_vector(e):
-            both = placed([P, X4, C], BF16, f"step{e}", MASKED_B + 3)
-            nc.vector.tensor_scalar(both[:], saved[1, e, 1][:], 0.0, None, ALU.is_gt)
-            for h in range(2):
-                steps[e, 1, h] = both[:, :, quarter(h)]
+            steps[e, 1] = placed([P, X4, C], BF16, f"step{e}1", STEP_SECOND[e])
+            nc.vector.tensor_scalar(steps[e, 1][:], saved[1, e, 1][:], 0.0, None, ALU.is_gt)
 
-        def mask_a3(e, g, h):
-            if (g, h) == (1, 0):
-                masked_place[e, g, h] = (A3[0], GATE_LAST, DY, DY + 8)[e]
-            elif (g, h) == (1, 1):
-                masked_place[e, g, h] = masked_place[e, 0, 0]
-            elif e > 0:
-                masked_place[e, g, h] = masked_place[e - 1, h, 1 - h]
-            masked[e, g, h] = placed([P, X4, HALF], F32, f"masked{e}{g}{h}", masked_place[e, g, h])
-            raw = saved[3, e, g][:, :, quarter(h)]
-            if (e, g) == (0, 0):
-                kept = saved[1, e, g][:, :, quarter(h)]
-                nc.vector.scalar_tensor_tensor(masked[e, g, h][:], kept, 0.0, raw, ALU.is_gt, ALU.mult)
+        def mask_on_vector(tile, e, cols):
+            kept, raw = saved[1, e, 0][:, :, cols], saved[3, e, 0][:, :, cols]
+            nc.vector.scalar_tensor_tensor(tile[:], kept, 0.0, raw, ALU.is_gt, ALU.mult)
+
+        def mask_first(e):
+            if e == 0:
+                tile = held.tile([P, X4, P], F32, name="masked_first0")
             else:
-                nc.gpsimd.tensor_tensor(masked[e, g, h][:], raw, steps[e, g, h], ALU.mult)
+                tile = placed([P, X4, P], F32, f"masked_first{e}", A3[e - 1, 0] + 4)
+            mask_on_vector(tile, e, slice(0, P))
+            masked[e, 0] = tile[:]
+
+        def mask_rest(e):
+            tile = placed([P, X4, C - P], F32, f"masked_rest{e}", MASKED_REST)
+            if e == 0:
+                mask_on_vector(tile, e, slice(P, C))
+            else:
+                nc.gpsimd.tensor_tensor(tile[:], saved[3, e, 0][:, :, P:C], steps[e, 0][:], ALU.mult)
+            for s in range(1, SB):
+                masked[e, s] = tile[:, :, P * (s - 1) : P * s]
+
+        def mask_second(e, h):
+            tile = placed([P, X4, HALF], F32, f"masked_second{e}{h}", A3[e, 0] + 4 * h)
+            nc.gpsimd.tensor_tensor(tile[:], saved[3, e, 1][:, :, quarter(h)], steps[e, 1][:, :, quarter(h)], ALU.mult)
+            for r in range(2):
+                masked[e, SB + 2 * h + r] = tile[:, :, P * r : P * (r + 1)]
 
         def hidden(e, n):
             g, s = divmod(n, SB)
-            h, r = divmod(s, 2)
             if n == 0:
-                da[1, e] = placed([P, NG * X4 * C], BF16, f"da1_{e}", (DA1, DY, DY + 8, A1[3])[e])
+                da[1, e] = placed([P, NG * X4 * C], BF16, f"da1_{e}", DA1)
                 da[3, e] = placed([P, NG * X4 * C], BF16, f"da3_{e}", DA3)
-            factors = {
-                3: saved[1, e, g][:, :, P * s : P * (s + 1)],
-                1: masked[e, g, h][:, :, P * r : P * (r + 1)],
-            }
+            factors = {3: saved[1, e, g][:, :, P * s : P * (s + 1)], 1: masked[e, n]}
             for which in (1, 3) if n == STEPS - 1 and e < LAST else (3, 1):
                 run = da[which, e][:, X4 * P * n : X4 * P * (n + 1)]
                 nc.vector.tensor_tensor(woven(run), by_lines(dh_turned[e, n][:]), by_lines(factors[which]), ALU.mult)
@@ -221,14 +221,13 @@ def tile_moe_bdx_glu_relu_kernel(
         def quantise_da(which, e, first, count):
             cols = C * count
             if e == LAST:
-                place = masked_place[e, 1, 0] + 2 * first + (which == 1)
-                scales = placed([P, cols], U8, f"da_scales{which}{e}{first}", place)
+                scales = placed([P, cols], U8, f"da_scales{which}{e}{first}", A3[e, 0] + 2 * first + (which == 1))
             elif which == 3:
-                scales = placed([P, cols], U8, f"da_scales{which}{e}", (MASKED_A + 1, MASKED_B + 1, A3[0])[e])
+                scales = placed([P, cols], U8, f"da_scales{which}{e}", A3[e, 0] + 6)
             else:
-                scales = held.tile([P, cols], U8, name="da_scales1", align_bytes=64, bufs=2)
-            if which == 1 and e + 2 < E:
-                words = placed([P, cols], U32, f"da_words1{e}", (WOVEN_C, WOVEN_A)[e])
+                scales = held.tile([P, cols], U8, name="da_scales1", align_bytes=64, bufs=3)
+            if e in WORDS:
+                words = placed([P, cols], U32, f"da_words{which}{e}{first}", WORDS[e] + 4 * (which == 1) + 2 * first)
             else:
                 words = held.tile([P, cols], U32, name=f"da_words{which}", align_bytes=64, bufs=2)
             run = da[which, e][:, X4 * C * first : X4 * C * (first + count)]
@@ -239,7 +238,7 @@ def tile_moe_bdx_glu_relu_kernel(
         def second_product(e):
             passes = [(which, g) for g in range(NG) for which in (3, 1)]
             for kb in range(KB):
-                if e == LAST and kb > 0:
+                if e > 0 and kb > 0:
                     bank = dh_banks.tile([P, C], F32, name="dh_bank")
                 else:
                     bank = dx_banks.tile([P, C], F32, name="dx_bank")
@@ -264,144 +263,161 @@ def tile_moe_bdx_glu_relu_kernel(
         load_dy(0)
         load_gate(0)
         load_gate(1)
-        load_gate(2)
-        load_saved(1, 0, 1, 0)
         load_dy(1)
-        load_saved(1, 0, 1, 1)
+        load_saved(1, 0, 1, 0)
         load_dy(2)
-        load_saved(1, 0, 0, 0)
-        load_saved(1, 0, 0, 1)
+        load_saved(1, 0, 1, 1)
         load_dy(3)
-        load_saved(1, 1, 0, 0)
+        load_saved(1, 0, 0, 0)
+        load_gate(2)
         load_w2(0)
+        load_saved(1, 0, 0, 1)
+        load_gate(LAST)
+        load_saved(1, 1, 0)
         load_saved(3, 0, 0)
-        load_saved(1, 1, 0, 1)
         load_saved(3, 0, 1)
+        load_w2(1)
+        load_saved(1, 1, 1)
         load_saved(3, 1, 0)
+        load_saved(1, 2, 0)
+        load_saved(3, 1, 1)
         w1_w = held.tile([P, E * NG, 2 * K], U8, name="w1_w", align_bytes=64)
         w3_w = held.tile([P, E * NG, 2 * K], U8, name="w3_w", align_bytes=64)
 
         for pair in range(2):
             relu_pair(0, 1, pair)
         for h in range(2):
-            sign_a1(0, 1, h)
-        for pair in range(2):
-            relu_pair(0, 0, pair)
-        for e in range(LAST):
-            gather(e)
+            sign_second(0, h)
+        for t in range(X4):
+            gather(0, t)
+            gather(1, t)
         for h in range(2):
             weave_g(0, h)
             quantise_g(0, quarter(h))
-        load_saved(1, 1, 1)
-        load_w2(1)
-        load_gate(LAST)
-        load_saved(1, 2, 0)
-        load_saved(3, 1, 1)
+        for t in range(X4):
+            gather(2, t)
+        for pair in range(2):
+            relu_pair(0, 0, pair)
+        for t in range(X4):
+            gather(LAST, t)
+        load_w2(2)
+        load_saved(3, 2, 0)
         load_saved(1, 2, 1)
+        for h in range(2):
+            weave_g(1, h)
         for n in range(SB):
             first_product(0, n)
+        quantise_g(1, slice(0, C))
+        mask_first(0)
+        mask_rest(0)
+
+        mask_second(0, 0)
+        mask_second(0, 1)
+        relu_a1(1, 0, 0)
+        relu_a1(1, 0, 1)
+        first_product(0, 4)
+        sign_rest(1)
+        first_product(0, 5)
+        first_product(0, 6)
+        first_product(0, 7)
+        for n in range(SB):
+            hidden(0, n)
+        mask_rest(1)
         for h in range(2):
-            mask_a3(0, 0, h)
-        for pair in range(2):
-            relu_pair(1, 0, pair)
-        sign_a1(1, 0, 0)
+            weave_g(2, h)
+        relu_a1(1, 1, 0)
+        sign_second(1, 0)
         for n in range(SB, STEPS):
-            first_product(0, n)
+            hidden(0, n)
+        for n in range(SB):
+            first_product(1, n)
+        load_saved(1, 3, 0)
+        load_saved(3, 2, 1)
+        load_w2(3)
+        load_saved(1, 3, 1)
+        load_saved(3, 3, 0)
+        quantise_g(2, slice(0, C))
+        quantise_da(3, 0, 0, NG)
+        quantise_da(1, 0, 0, NG)
+        mask_first(1)
 
-        for e in range(E):
-            late = e >= 2
-            mask_a3(e, 1, 0)
-            hidden(e, 0)
-            hidden(e, 1)
-            if late and e != STEP_ON_VECTOR:
-                step_a1(e, 1, 1)
-            mask_a3(e, 1, 1)
-            if late:
-                first_product(e, SB)
-            if late and e < LAST:
-                step_a1(e + 1, 0, 0)
-            if late:
-                first_product(e, SB + 1)
-            hidden(e, 2)
-            hidden(e, 3)
-            if e < LAST:
-                mask_a3(e + 1, 0, 0)
-            if e == STEP_ON_VECTOR:
-                relu_a1(e, 1, 0)
-            if late:
-                first_product(e, SB + 2)
-            if e == 0:
-                sign_a1(1, 0, 1)
-            if late and e < LAST:
-                step_a1(e + 1, 0, 1)
-            if e == STEP_ON_VECTOR:
-                relu_a1(e, 1, 1)
-            if late:
-                first_product(e, SB + 3)
-            if e == LAST:
-                second_product(e - 1)
-            hidden(e, 4)
-            hidden(e, 5)
-            if e < LAST:
-                mask_a3(e + 1, 0, 1)
-            else:
-                quantise_da(3, e, 0, 1)
-                quantise_da(1, e, 0, 1)
-            for woven_e in ((1, 2), (3,), (), ())[e]:
-                for h in range(2):
-                    weave_g(woven_e, h)
-            if 0 < e < LAST:
-                first_product(e + 1, 0)
-                if e + 1 != STEP_ON_VECTOR:
-                    step_a1(e + 1, 1, 0)
-                for n in range(1, SB):
-                    first_product(e + 1, n)
-                second_product(e - 1)
-            hidden(e, 6)
-            hidden(e, 7)
+        mask_second(1, 0)
+        relu_a1(1, 1, 1)
+        sign_second(1, 1)
+        mask_second(1, 1)
+        first_product(1, 4)
+        relu_a1(2, 0, 0)
+        relu_a1(2, 0, 1)
+        first_product(1, 5)
+        sign_rest(2)
+        first_product(1, 6)
+        first_product(1, 7)
+        for n in range(SB):
+            hidden(1, n)
+        mask_rest(2)
+        for h in range(2):
+            weave_g(LAST, h)
+        for n in range(SB, STEPS):
+            hidden(1, n)
+        for n in range(SB):
+            first_product(2, n)
+        load_w13(0)
+        load_saved(3, 3, 1)
+        load_w13(1)
+        nc.sync.dma_start(pos1_sb[:], pos1)
+        nc.sync.dma_start(pos2_sb[:], pos2)
+        quantise_g(LAST, slice(0, C))
+        quantise_da(3, 1, 0, NG)
+        step_on_vector(2)
+        quantise_da(1, 1, 0, NG)
+        mask_first(2)
 
-            if e == 0:
-                load_saved(3, 2, 0)
-                load_w2(2)
-                load_w13(0)
-                load_saved(3, 2, 1)
-                load_saved(1, 3, 0)
-                load_w2(3)
-                nc.sync.dma_start(pos1_sb[:], pos1)
-                nc.sync.dma_start(pos2_sb[:], pos2)
-                quantise_g(1, slice(0, C))
-                quantise_da(3, e, 0, NG)
-                quantise_g(2, slice(0, C))
-                quantise_da(1, e, 0, NG)
-                gather(LAST)
-                step_a1(1, 1, 0)
-                for n in range(SB):
-                    first_product(1, n)
-                step_a1(1, 1, 1)
-                for h in range(2):
-                    first_product(1, SB + h)
-                    step_a1(2, 0, h)
-                first_product(1, SB + 2)
-                first_product(1, SB + 3)
-            elif e < LAST:
-                if e == 1:
-                    load_saved(3, 3, 0)
-                    load_saved(1, 3, 1)
-                    load_saved(3, 3, 1)
-                    load_w13(1)
-                    quantise_g(LAST, slice(0, C))
-                if e + 1 == STEP_ON_VECTOR:
-                    step_on_vector(e + 1)
-                quantise_da(3, e, 0, NG)
-                quantise_da(1, e, 0, NG)
-            else:
-                quantise_da(3, e, 1, 1)
-                quantise_da(1, e, 1, 1)
+        mask_second(2, 0)
+        mask_second(2, 1)
+        relu_a1(3, 0, 0)
+        relu_a1(3, 0, 1)
+        first_product(2, 4)
+        sign_rest(3)
+        relu_a1(2, 1, 0)
+        first_product(2, 5)
+        first_product(2, 6)
+        relu_a1(2, 1, 1)
+        first_product(2, 7)
+        for n in range(SB):
+            hidden(2, n)
+        mask_rest(3)
+        for n in range(SB, STEPS):
+            hidden(2, n)
+        relu_a1(3, 1, 0)
+        sign_second(3, 0)
+        for n in range(SB):
+            first_product(3, n)
+        second_product(0)
+        quantise_da(3, 2, 0, NG)
+        quantise_da(1, 2, 0, NG)
+        mask_first(3)
+
+        mask_second(3, 0)
+        relu_a1(3, 1, 1)
+        sign_second(3, 1)
+        mask_second(3, 1)
+        for n in range(SB, STEPS):
+            first_product(3, n)
+        for e in range(1, LAST):
+            second_product(e)
+        for n in range(STEPS - 2):
+            hidden(3, n)
+        quantise_da(3, 3, 0, 1)
+        quantise_da(1, 3, 0, 1)
+        hidden(3, 6)
+        hidden(3, 7)
+        quantise_da(3, 3, 1, 1)
+        quantise_da(1, 3, 1, 1)
         second_product(LAST)
 
         for kb in range(KB):
-            first = placed([P, T], F32, f"first{kb}", A1[1] + 4 * kb)
-            total = placed([P, T], F32, f"total{kb}", A1[5] + 4 * kb)
+            first = placed([P, T], F32, f"first{kb}", A1[1, 0] + 4 * kb)
+            total = placed([P, T], F32, f"total{kb}", A1[1, 1] + 4 * kb)
             for lo, hi in ((0, T // 2), (T // 2, T)):
                 nc.vector.tensor_copy(first[:, lo:hi], dx[kb][:].indirect(pos1_sb[:, lo // 16 : hi // 16]))
             cuts = (0, T // 2, T) if kb < KB - 1 else (0, T // 2, T - P, T)

@@ -31,14 +31,19 @@ BYTES = 4 * (N * T + 2 * H * S + S + K * T) + E * (N * H + 2 * H * K) // 2 + E *
 
 DY = 0
 MASKED_REST = 16
-WOVEN = (22, MASKED_REST, 26, 22)
+WOVEN = (22, 26, 26, 22)
 A1 = {(0, 1): 30, (0, 0): 38, (1, 0): 46, (1, 1): 54, (2, 0): 62, (2, 1): DY, (3, 0): 38, (3, 1): 30}
-A3 = {(0, 0): 70, (1, 0): 78, (2, 0): DY + 8, (3, 0): 86, (0, 1): 94, (1, 1): 102, (2, 1): 94, (3, 1): 102}
-DA1, DA3 = 110, 118
-STEP_SECOND = (126, 130, WOVEN[3], 126)
+A3 = {(0, 0): 117.75, (1, 0): 70, (2, 0): DY + 8, (3, 0): 78, (0, 1): 86, (1, 1): 94, (2, 1): 86, (3, 1): 94}
+DA1 = 102
+DA3 = (110, 118, 110, 120)
+MASKED_SECOND = (118, 110, 118, 112)
+MASKED_LATE = 110
+STEP_SECOND = (126, 130, WOVEN[3], 156)
 STEP_REST = (None, 134, 137, 134)
 DX = 140
 G_PLANES = (156, DX, DX + 8, 156)
+PAIRS = [(e, n) for e in range(E) for n in (2, 0, 4, 6)]
+AHEAD = 1
 WORDS = {2: A3[2, 1], 3: A1[2, 0]}
 
 
@@ -61,10 +66,9 @@ def tile_moe_bdx_glu_relu_kernel(
     with ExitStack() as ctx:
         held = ctx.enter_context(tc.tile_pool(name="held", bufs=1))
         arena = ctx.enter_context(tc.tile_pool(name="arena", bufs=1))
-        unturned = ctx.enter_context(tc.tile_pool(name="unturned", bufs=4))
+        unturned = ctx.enter_context(tc.tile_pool(name="unturned", bufs=6))
         dh_banks = ctx.enter_context(tc.psum_pool(name="dh_banks", bufs=3))
-        turned_banks = ctx.enter_context(tc.psum_pool(name="turned_banks", bufs=4))
-        dx_banks = ctx.enter_context(tc.psum_pool(name="dx_banks", bufs=1))
+        turned_banks = ctx.enter_context(tc.psum_pool(name="turned_banks", bufs=5))
 
         def placed(shape, dtype, name, kib):
             return arena.tile(shape, dtype, name=name, offset=int(1024 * kib), align_bytes=64)
@@ -83,15 +87,17 @@ def tile_moe_bdx_glu_relu_kernel(
         dy, dx = [], []
         gates, w2_w, saved = {}, {}, {}
         g_planes, g_woven, g_codes = {}, {}, {}
-        dh_turned, steps, masked, da, da_codes = {}, {}, {}, {}, {}
+        dh, dh_sb, dh_turned, steps, masked, da, da_codes = {}, {}, {}, {}, {}, {}, {}
 
         def load_dy(t):
             dy.append(placed([P, T], F32, f"dy{t}", DY + 4 * t))
             nc.sync.dma_start(dy[t][:], dyT.rearrange("(p t) s -> t p s", t=X4)[t])
 
-        def load_gate(e):
-            gates[e] = held.tile([P, C], F32, name=f"gate{e}")
-            nc.sync.dma_start(gates[e][:], gate[0:P, C * e : C * (e + 1)])
+        def load_gates(lo, hi):
+            tile = held.tile([P, C * (hi - lo)], F32, name=f"gate{lo}")
+            nc.sync.dma_start(tile[:], gate[0:P, C * lo : C * hi])
+            for e in range(lo, hi):
+                gates[e] = tile[:, C * (e - lo) : C * (e - lo + 1)]
 
         def load_w2(e):
             w2_w[e] = held.tile([P, 2 * H], U8, name=f"w2_{e}", align_bytes=64)
@@ -121,25 +127,20 @@ def tile_moe_bdx_glu_relu_kernel(
             if t == 0:
                 g_planes[e] = placed([P, X4, C], F32, f"g_planes{e}", G_PLANES[e])
             picked = dy[t][:].indirect(offs_sb[:, (C // 16) * e : (C // 16) * (e + 1)])
-            nc.vector.tensor_tensor(g_planes[e][:, t, :], picked, gates[e][:], ALU.mult)
+            nc.vector.tensor_tensor(g_planes[e][:, t, :], picked, gates[e], ALU.mult)
 
-        def weave_g(e, h):
-            if h == 0:
-                g_woven[e] = placed([P, X4 * C], BF16, f"g_woven{e}", WOVEN[e])
-            run = g_woven[e][:, X4 * HALF * h : X4 * HALF * (h + 1)]
-            nc.scalar.copy(woven(run), by_lines(g_planes[e][:, :, quarter(h)]))
+        def weave_g(e):
+            g_woven[e] = placed([P, X4 * C], BF16, f"g_woven{e}", WOVEN[e])
+            nc.scalar.copy(woven(g_woven[e][:]), by_lines(g_planes[e][:]))
 
-        def quantise_g(e, cols):
-            if cols.start == 0:
-                if e >= 2:
-                    scales = placed([P, C], U8, f"g_scales{e}", A3[e - 2, 0] + 7)
-                else:
-                    scales = held.tile([P, C], U8, name=f"g_scales{e}", align_bytes=64)
-                words = held.tile([P, C], U32, name="g_words", align_bytes=64, bufs=3)
-                g_codes[e] = (words, scales)
-            words, scales = g_codes[e]
-            run = g_woven[e][:, X4 * cols.start : X4 * cols.stop]
-            nc.vector.quantize_mx(out=words[:, cols].bitcast(E5M2), scales=scales[:, cols], in_=run)
+        def quantise_g(e):
+            if e >= 2:
+                scales = placed([P, C], U8, f"g_scales{e}", STEP_SECOND[e - 2] + 3)
+            else:
+                scales = held.tile([P, C], U8, name=f"g_scales{e}", align_bytes=64)
+            words = held.tile([P, C], U32, name="g_words", align_bytes=64, bufs=3)
+            g_codes[e] = (words, scales)
+            nc.vector.quantize_mx(out=words[:].bitcast(E5M2), scales=scales[:], in_=g_woven[e][:])
 
         def first_product(e, n):
             g, s = divmod(n, SB)
@@ -154,76 +155,106 @@ def tile_moe_bdx_glu_relu_kernel(
                 start=True,
                 stop=True,
             )
-            dh_sb = unturned.tile([P, X4, P], F32, name="dh_sb")
-            nc.scalar.copy(dh_sb[:], bank[:].rearrange("p (m t) -> p t m", t=X4))
+            dh[e, n] = bank
+
+        def copy_dh(e, n):
+            dh_sb[e, n] = unturned.tile([P, X4, P], F32, name="dh_sb")
+            nc.scalar.copy(dh_sb[e, n][:], dh[e, n][:].rearrange("p (m t) -> p t m", t=X4))
+
+        def turn(e, n):
             dh_turned[e, n] = turned_banks.tile([P, X4, P], F32, name="dh_turned")
             for t in range(X4):
-                nc.tensor.transpose(dh_turned[e, n][:, t, :], dh_sb[:, t, :], ident[:])
+                nc.tensor.transpose(dh_turned[e, n][:, t, :], dh_sb[e, n][:, t, :], ident[:])
 
-        def relu_a1(e, g, h):
-            kept = saved[1, e, g][:, :, quarter(h)]
+        def first_products(k):
+            e, n = PAIRS[k]
+            for m in (n, n + 1) if n < SB else (n + 1, n):
+                first_product(e, m)
+
+        def pair_of_steps(e, n):
+            k = PAIRS.index((e, n))
+            order = (n + 1, n) if n < SB else (n, n + 1)
+            for m in order:
+                copy_dh(e, m)
+            if k + AHEAD < len(PAIRS):
+                first_products(k + AHEAD)
+            for m in order:
+                turn(e, m)
+
+        def relu_a1(e, g):
+            kept = saved[1, e, g][:]
             nc.scalar.activation(kept, kept, ACT.Relu)
 
         def relu_pair(e, g, pair):
             kept = saved[1, e, g][:, 2 * pair : 2 * pair + 2, :]
             nc.scalar.activation(kept, kept, ACT.Relu)
 
-        def sign_second(e, h):
-            if h == 0:
-                steps[e, 1] = placed([P, X4, C], BF16, f"step{e}1", STEP_SECOND[e])
-            nc.scalar.activation(steps[e, 1][:, :, quarter(h)], saved[1, e, 1][:, :, quarter(h)], ACT.Sign)
+        def sign_second(e):
+            steps[e, 1] = placed([P, X4, C], BF16, f"step{e}1", STEP_SECOND[e])
+            nc.scalar.activation(steps[e, 1][:], saved[1, e, 1][:], ACT.Sign)
 
         def sign_rest(e):
+            lo = 0 if e == LAST else P
             steps[e, 0] = placed([P, X4, C - P], BF16, f"step{e}0", STEP_REST[e])
-            nc.scalar.activation(steps[e, 0][:], saved[1, e, 0][:, :, P:C], ACT.Sign)
+            nc.scalar.activation(steps[e, 0][:], saved[1, e, 0][:, :, lo : lo + C - P], ACT.Sign)
+
+        def sign_late():
+            steps["late"] = held.tile([P, X4, P], BF16, name="step_late")
+            nc.scalar.activation(steps["late"][:], saved[1, LAST, 0][:, :, C - P : C], ACT.Sign)
+
+        def mask_late():
+            tile = placed([P, X4, P], F32, "masked_late", MASKED_LATE)
+            nc.gpsimd.tensor_tensor(tile[:], saved[3, LAST, 0][:, :, C - P : C], steps["late"][:], ALU.mult)
+            masked[LAST, SB - 1] = tile[:]
 
         def step_on_vector(e):
             steps[e, 1] = placed([P, X4, C], BF16, f"step{e}1", STEP_SECOND[e])
-            nc.vector.tensor_scalar(steps[e, 1][:], saved[1, e, 1][:], 0.0, None, ALU.is_gt)
+            nc.vector.tensor_scalar(steps[e, 1][:, :, quarter(0)], saved[1, e, 1][:, :, quarter(0)], 0.0, None, ALU.is_gt)
 
         def mask_on_vector(tile, e, cols):
             kept, raw = saved[1, e, 0][:, :, cols], saved[3, e, 0][:, :, cols]
             nc.vector.scalar_tensor_tensor(tile[:], kept, 0.0, raw, ALU.is_gt, ALU.mult)
 
         def mask_first(e):
-            if e == 0:
-                tile = held.tile([P, X4, P], F32, name="masked_first0")
-            else:
-                tile = placed([P, X4, P], F32, f"masked_first{e}", A3[e - 1, 0] + 4)
-            mask_on_vector(tile, e, slice(0, P))
-            masked[e, 0] = tile[:]
+            width, place = (C, MASKED_REST) if e == 0 else (P, STEP_SECOND[e - 1])
+            tile = placed([P, X4, width], F32, f"masked_first{e}", place)
+            mask_on_vector(tile, e, slice(0, width))
+            for s in range(width // P):
+                masked[e, s] = tile[:, :, P * s : P * (s + 1)]
 
         def mask_rest(e):
             tile = placed([P, X4, C - P], F32, f"masked_rest{e}", MASKED_REST)
-            if e == 0:
-                mask_on_vector(tile, e, slice(P, C))
-            else:
-                nc.gpsimd.tensor_tensor(tile[:], saved[3, e, 0][:, :, P:C], steps[e, 0][:], ALU.mult)
-            for s in range(1, SB):
-                masked[e, s] = tile[:, :, P * (s - 1) : P * s]
+            lo = 0 if e == LAST else 1
+            nc.gpsimd.tensor_tensor(tile[:], saved[3, e, 0][:, :, P * lo : P * lo + C - P], steps[e, 0][:], ALU.mult)
+            for s in range(SB - 1):
+                masked[e, lo + s] = tile[:, :, P * s : P * (s + 1)]
 
-        def mask_second(e, h):
-            tile = placed([P, X4, HALF], F32, f"masked_second{e}{h}", A3[e, 0] + 4 * h)
-            nc.gpsimd.tensor_tensor(tile[:], saved[3, e, 1][:, :, quarter(h)], steps[e, 1][:, :, quarter(h)], ALU.mult)
-            for r in range(2):
-                masked[e, SB + 2 * h + r] = tile[:, :, P * r : P * (r + 1)]
+        def mask_second(e):
+            for h in range(2):
+                tile = placed([P, X4, HALF], F32, f"masked_second{e}{h}", MASKED_SECOND[e] + 4 * h)
+                nc.gpsimd.tensor_tensor(tile[:], saved[3, e, 1][:, :, quarter(h)], steps[e, 1][:, :, quarter(h)], ALU.mult)
+                for r in range(2):
+                    masked[e, SB + 2 * h + r] = tile[:, :, P * r : P * (r + 1)]
 
-        def hidden(e, n):
+        def product(which, e, n):
             g, s = divmod(n, SB)
             if n == 0:
-                da[1, e] = placed([P, NG * X4 * C], BF16, f"da1_{e}", DA1)
-                da[3, e] = placed([P, NG * X4 * C], BF16, f"da3_{e}", DA3)
-            factors = {3: saved[1, e, g][:, :, P * s : P * (s + 1)], 1: masked[e, n]}
-            for which in (1, 3) if n == STEPS - 1 and e < LAST else (3, 1):
-                run = da[which, e][:, X4 * P * n : X4 * P * (n + 1)]
-                nc.vector.tensor_tensor(woven(run), by_lines(dh_turned[e, n][:]), by_lines(factors[which]), ALU.mult)
+                da[which, e] = placed([P, NG * X4 * C], BF16, f"da{which}_{e}", DA1 if which == 1 else DA3[e])
+            factor = masked[e, n] if which == 1 else saved[1, e, g][:, :, P * s : P * (s + 1)]
+            run = da[which, e][:, X4 * P * n : X4 * P * (n + 1)]
+            nc.vector.tensor_tensor(woven(run), by_lines(dh_turned[e, n][:]), by_lines(factor), ALU.mult)
+
+        def both_products(e, lo, hi):
+            for n in range(lo, hi):
+                product(3, e, n)
+                product(1, e, n)
 
         def quantise_da(which, e, first, count):
             cols = C * count
             if e == LAST:
-                scales = placed([P, cols], U8, f"da_scales{which}{e}{first}", A3[e, 0] + 2 * first + (which == 1))
+                scales = placed([P, cols], U8, f"da_scales{which}{e}{first}", STEP_SECOND[e] + first + (which == 1) / 2)
             elif which == 3:
-                scales = placed([P, cols], U8, f"da_scales{which}{e}", A3[e, 0] + 6)
+                scales = placed([P, cols], U8, f"da_scales{which}{e}", STEP_SECOND[e] + 2)
             else:
                 scales = held.tile([P, cols], U8, name="da_scales1", align_bytes=64, bufs=3)
             if e in WORDS:
@@ -238,10 +269,7 @@ def tile_moe_bdx_glu_relu_kernel(
         def second_product(e):
             passes = [(which, g) for g in range(NG) for which in (3, 1)]
             for kb in range(KB):
-                if e > 0 and kb > 0:
-                    bank = dh_banks.tile([P, C], F32, name="dh_bank")
-                else:
-                    bank = dx_banks.tile([P, C], F32, name="dx_bank")
+                bank = dh_banks.tile([P, C], F32, name="dh_bank")
                 for n, (which, g) in enumerate(passes):
                     w, scale_tile = (w1_w, w1_sc) if which == 1 else (w3_w, w3_sc)
                     words, scales = da_codes[which, e, g]
@@ -261,21 +289,21 @@ def tile_moe_bdx_glu_relu_kernel(
         load_scales(nc.gpsimd, w2_sc, w2_scales, 0, E)
         nc.sync.dma_start(offs_sb[:], offs)
         load_dy(0)
-        load_gate(0)
-        load_gate(1)
+        load_gates(0, 1)
+        load_gates(1, 2)
         load_dy(1)
         load_saved(1, 0, 1, 0)
         load_dy(2)
         load_saved(1, 0, 1, 1)
         load_dy(3)
         load_saved(1, 0, 0, 0)
-        load_gate(2)
+        load_gates(2, 3)
         load_w2(0)
         load_saved(1, 0, 0, 1)
-        load_gate(LAST)
+        load_gates(3, E)
         load_saved(1, 1, 0)
-        load_saved(3, 0, 0)
         load_saved(3, 0, 1)
+        load_saved(3, 0, 0)
         load_w2(1)
         load_saved(1, 1, 1)
         load_saved(3, 1, 0)
@@ -286,14 +314,12 @@ def tile_moe_bdx_glu_relu_kernel(
 
         for pair in range(2):
             relu_pair(0, 1, pair)
-        for h in range(2):
-            sign_second(0, h)
+        sign_second(0)
         for t in range(X4):
             gather(0, t)
             gather(1, t)
-        for h in range(2):
-            weave_g(0, h)
-            quantise_g(0, quarter(h))
+        weave_g(0)
+        quantise_g(0)
         for t in range(X4):
             gather(2, t)
         for pair in range(2):
@@ -303,125 +329,99 @@ def tile_moe_bdx_glu_relu_kernel(
         load_w2(2)
         load_saved(3, 2, 0)
         load_saved(1, 2, 1)
-        for h in range(2):
-            weave_g(1, h)
-        for n in range(SB):
-            first_product(0, n)
-        quantise_g(1, slice(0, C))
+        weave_g(1)
+        for k in range(AHEAD):
+            first_products(k)
+        pair_of_steps(0, 2)
+        pair_of_steps(0, 0)
+        quantise_g(1)
         mask_first(0)
-        mask_rest(0)
 
-        mask_second(0, 0)
-        mask_second(0, 1)
-        relu_a1(1, 0, 0)
-        relu_a1(1, 0, 1)
-        first_product(0, 4)
+        mask_second(0)
+        relu_a1(1, 0)
+        pair_of_steps(0, 4)
         sign_rest(1)
-        first_product(0, 5)
-        first_product(0, 6)
-        first_product(0, 7)
-        for n in range(SB):
-            hidden(0, n)
+        pair_of_steps(0, 6)
+        both_products(0, 0, SB)
         mask_rest(1)
-        for h in range(2):
-            weave_g(2, h)
-        relu_a1(1, 1, 0)
-        sign_second(1, 0)
-        for n in range(SB, STEPS):
-            hidden(0, n)
-        for n in range(SB):
-            first_product(1, n)
+        weave_g(2)
+        both_products(0, SB, STEPS)
+        pair_of_steps(1, 2)
+        relu_a1(1, 1)
+        pair_of_steps(1, 0)
+        sign_second(1)
         load_saved(1, 3, 0)
         load_saved(3, 2, 1)
         load_w2(3)
         load_saved(1, 3, 1)
         load_saved(3, 3, 0)
-        quantise_g(2, slice(0, C))
+        quantise_g(2)
+        mask_first(1)
         quantise_da(3, 0, 0, NG)
         quantise_da(1, 0, 0, NG)
-        mask_first(1)
 
-        mask_second(1, 0)
-        relu_a1(1, 1, 1)
-        sign_second(1, 1)
-        mask_second(1, 1)
-        first_product(1, 4)
-        relu_a1(2, 0, 0)
-        relu_a1(2, 0, 1)
-        first_product(1, 5)
+        mask_second(1)
+        pair_of_steps(1, 4)
+        relu_a1(2, 0)
+        pair_of_steps(1, 6)
         sign_rest(2)
-        first_product(1, 6)
-        first_product(1, 7)
-        for n in range(SB):
-            hidden(1, n)
+        both_products(1, 0, SB)
         mask_rest(2)
-        for h in range(2):
-            weave_g(LAST, h)
-        for n in range(SB, STEPS):
-            hidden(1, n)
-        for n in range(SB):
-            first_product(2, n)
+        weave_g(LAST)
+        both_products(1, SB, STEPS)
+        pair_of_steps(2, 2)
+        pair_of_steps(2, 0)
+        relu_a1(2, 1)
         load_w13(0)
         load_saved(3, 3, 1)
         load_w13(1)
         nc.sync.dma_start(pos1_sb[:], pos1)
         nc.sync.dma_start(pos2_sb[:], pos2)
-        quantise_g(LAST, slice(0, C))
-        quantise_da(3, 1, 0, NG)
-        step_on_vector(2)
-        quantise_da(1, 1, 0, NG)
+        quantise_g(LAST)
         mask_first(2)
+        step_on_vector(2)
+        quantise_da(3, 1, 0, NG)
+        quantise_da(1, 1, 0, NG)
 
-        mask_second(2, 0)
-        mask_second(2, 1)
-        relu_a1(3, 0, 0)
-        relu_a1(3, 0, 1)
-        first_product(2, 4)
+        pair_of_steps(2, 4)
+        relu_a1(3, 0)
+        nc.scalar.activation(steps[2, 1][:, :, quarter(1)], saved[1, 2, 1][:, :, quarter(1)], ACT.Sign)
+        mask_second(2)
         sign_rest(3)
-        relu_a1(2, 1, 0)
-        first_product(2, 5)
-        first_product(2, 6)
-        relu_a1(2, 1, 1)
-        first_product(2, 7)
-        for n in range(SB):
-            hidden(2, n)
+        pair_of_steps(2, 6)
+        both_products(2, 0, SB)
         mask_rest(3)
-        for n in range(SB, STEPS):
-            hidden(2, n)
-        relu_a1(3, 1, 0)
-        sign_second(3, 0)
-        for n in range(SB):
-            first_product(3, n)
+        both_products(2, SB, STEPS)
+        pair_of_steps(3, 2)
+        relu_a1(3, 1)
+        pair_of_steps(3, 0)
+        sign_late()
+        sign_second(3)
         second_product(0)
         quantise_da(3, 2, 0, NG)
         quantise_da(1, 2, 0, NG)
-        mask_first(3)
 
-        mask_second(3, 0)
-        relu_a1(3, 1, 1)
-        sign_second(3, 1)
-        mask_second(3, 1)
-        for n in range(SB, STEPS):
-            first_product(3, n)
+        mask_late()
+        mask_second(3)
+        pair_of_steps(3, 4)
+        pair_of_steps(3, 6)
         for e in range(1, LAST):
             second_product(e)
-        for n in range(STEPS - 2):
-            hidden(3, n)
+        both_products(3, 0, STEPS)
         quantise_da(3, 3, 0, 1)
         quantise_da(1, 3, 0, 1)
-        hidden(3, 6)
-        hidden(3, 7)
         quantise_da(3, 3, 1, 1)
         quantise_da(1, 3, 1, 1)
         second_product(LAST)
 
+        firsts = []
         for kb in range(KB):
-            first = placed([P, T], F32, f"first{kb}", A1[1, 0] + 4 * kb)
+            firsts.append(placed([P, T], F32, f"first{kb}", A1[1, 0] + 4 * kb))
+            nc.vector.tensor_copy(firsts[kb][:], dx[kb][:].indirect(pos1_sb[:]))
+        for kb in range(KB):
             total = placed([P, T], F32, f"total{kb}", A1[1, 1] + 4 * kb)
-            for lo, hi in ((0, T // 2), (T // 2, T)):
-                nc.vector.tensor_copy(first[:, lo:hi], dx[kb][:].indirect(pos1_sb[:, lo // 16 : hi // 16]))
             cuts = (0, T // 2, T) if kb < KB - 1 else (0, T // 2, T - P, T)
             for lo, hi in zip(cuts, cuts[1:]):
                 picked = dx[kb][:].indirect(pos2_sb[:, lo // 16 : hi // 16])
-                nc.vector.tensor_tensor(total[:, lo:hi], picked, first[:, lo:hi], ALU.add)
+                nc.vector.tensor_tensor(total[:, lo:hi], picked, firsts[kb][:, lo:hi], ALU.add)
                 nc.sync.dma_start(out[P * kb : P * (kb + 1), lo:hi], total[:, lo:hi])

@@ -9,11 +9,11 @@ P = 128
 X4 = 4
 NG = H // 512
 SB = C // P
-STEPS = NG * SB
 KB = K // P
-HALF = C // 2
-LAST = E - 1
-STEP_ON_VECTOR = 2
+HALVES = E * NG
+CHUNK = 2 * P
+CHUNKS = S // CHUNK
+EARLY = 32
 
 F32 = mybir.dt.float32
 BF16 = mybir.dt.bfloat16
@@ -29,34 +29,28 @@ ACT = mybir.ActivationFunctionType
 FLOPS = 2 * S * N * H + 2 * 2 * S * H * K
 BYTES = 4 * (N * T + 2 * H * S + S + K * T) + E * (N * H + 2 * H * K) // 2 + E * (N * H + 2 * H * K) // 32 + 2 * 128 * 256
 
-DY = 0
-MASKED_REST = 16
-WOVEN = (22, 26, 26, 22)
-A1 = {(0, 1): 30, (0, 0): 38, (1, 0): 46, (1, 1): 54, (2, 0): 62, (2, 1): DY, (3, 0): 38, (3, 1): 30}
-A3 = {(0, 0): 117.75, (1, 0): 70, (2, 0): DY + 8, (3, 0): 78, (0, 1): 86, (1, 1): 94, (2, 1): 86, (3, 1): 94}
-DA1 = 102
-DA3 = (110, 118, 110, 120)
-MASKED_SECOND = (118, 110, 118, 112)
-MASKED_LATE = 110
-STEP_SECOND = (126, 130, WOVEN[3], 156)
-STEP_REST = (None, 134, 137, 134)
-DX = 140
-G_PLANES = (156, DX, DX + 8, 156)
-PAIRS = [(e, n) for e in range(E) for n in (2, 0, 4, 6)]
-AHEAD = 1
-WORDS = {2: A3[2, 1], 3: A1[2, 0]}
+DY = 16 * HALVES
+DA = DY + 16
+WOVEN = DA + 8
+KEPT = WOVEN + 4
+PLANES = KEPT + 16
+DX_LAST = PLANES + 12
+
+
+def a_place(which, h):
+    return 16 * h + (0 if which == 1 else 8)
 
 
 def by_lines(planes):
     return planes.rearrange("p t (c i) -> p c t i", i=4)
 
 
+def in_turn(planes):
+    return planes.rearrange("p t j -> p j t")
+
+
 def woven(flat):
     return flat.rearrange("p (c i t) -> p c t i", i=4, t=X4)
-
-
-def quarter(h):
-    return slice(HALF * h, HALF * (h + 1))
 
 
 def tile_moe_bdx_glu_relu_kernel(
@@ -66,9 +60,8 @@ def tile_moe_bdx_glu_relu_kernel(
     with ExitStack() as ctx:
         held = ctx.enter_context(tc.tile_pool(name="held", bufs=1))
         arena = ctx.enter_context(tc.tile_pool(name="arena", bufs=1))
-        unturned = ctx.enter_context(tc.tile_pool(name="unturned", bufs=6))
-        dh_banks = ctx.enter_context(tc.psum_pool(name="dh_banks", bufs=3))
-        turned_banks = ctx.enter_context(tc.psum_pool(name="turned_banks", bufs=5))
+        dh_banks = ctx.enter_context(tc.psum_pool(name="dh_banks", bufs=5))
+        dx_banks = ctx.enter_context(tc.psum_pool(name="dx_banks", bufs=1))
 
         def placed(shape, dtype, name, kib):
             return arena.tile(shape, dtype, name=name, offset=int(1024 * kib), align_bytes=64)
@@ -76,352 +69,302 @@ def tile_moe_bdx_glu_relu_kernel(
         offs_sb = held.tile([P, S // 16], U16, name="offs_sb")
         pos1_sb = held.tile([P, T // 16], U16, name="pos1_sb")
         pos2_sb = held.tile([P, T // 16], U16, name="pos2_sb")
-        w2_sc = held.tile([P, E, H], U8, name="w2_sc", align_bytes=64)
+        w2_sc_raw = held.tile([P, 512], U8, name="w2_sc_raw")
+        w2_sc_sorted = held.tile([P, 512], U8, name="w2_sc_sorted")
+        w2_sc_first_raw = held.tile([P, H], U8, name="w2_sc_first_raw")
+        w2_sc_first = held.tile([P, H], U8, name="w2_sc_first", align_bytes=64)
+        w2_sc_rest = held.tile([P, E - 1, H], U8, name="w2_sc_rest", align_bytes=64)
+        w2_sc = [w2_sc_first[:]] + [w2_sc_rest[:, e, :] for e in range(E - 1)]
         w1_sc = held.tile([P, E * NG, K], U8, name="w1_sc", align_bytes=64)
         w3_sc = held.tile([P, E * NG, K], U8, name="w3_sc", align_bytes=64)
+        w1_w = held.tile([P, E * NG, 2 * K], U8, name="w1_w", align_bytes=64)
+        w3_w = held.tile([P, E * NG, 2 * K], U8, name="w3_w", align_bytes=64)
         ident = held.tile([P, P], F32, name="ident")
-        for scale_tile in (w2_sc, w1_sc, w3_sc):
+        gate_col = held.tile([P, E, X4], F32, name="gate_col")
+        for scale_tile in (w2_sc_first_raw, w2_sc_raw):
+            nc.vector.memset(scale_tile[:].bitcast(I32), 0)
+        for scale_tile in (w2_sc_rest, w1_sc, w3_sc):
             nc.vector.memset(scale_tile[:].rearrange("p e i -> p (e i)").bitcast(I32), 0)
-        make_identity(nc, ident[:])
 
         dy, dx = [], []
-        gates, w2_w, saved = {}, {}, {}
+        w2_raw, w2_w, saved, gate_bank = {}, {}, {}, {}
         g_planes, g_woven, g_codes = {}, {}, {}
-        dh, dh_sb, dh_turned, steps, masked, da, da_codes = {}, {}, {}, {}, {}, {}, {}
+        dh, dhm, da, da_codes, dx_bank, kept = {}, {}, {}, {}, {}, {}
 
         def load_dy(t):
             dy.append(placed([P, T], F32, f"dy{t}", DY + 4 * t))
             nc.sync.dma_start(dy[t][:], dyT.rearrange("(p t) s -> t p s", t=X4)[t])
 
-        def load_gates(lo, hi):
-            tile = held.tile([P, C * (hi - lo)], F32, name=f"gate{lo}")
-            nc.sync.dma_start(tile[:], gate[0:P, C * lo : C * hi])
-            for e in range(lo, hi):
-                gates[e] = tile[:, C * (e - lo) : C * (e - lo + 1)]
-
         def load_w2(e):
-            w2_w[e] = held.tile([P, 2 * H], U8, name=f"w2_{e}", align_bytes=64)
-            nc.sync.dma_start(w2_w[e][:].bitcast(I32), w2_words[e, 0].bitcast(I32))
+            if e < 2:
+                w2_raw[e] = held.tile([P, 2 * H], U8, name=f"w2_raw{e}")
+            else:
+                w2_raw[e] = placed([P, 2 * H], U8, f"w2_raw{e}", PLANES + 2 * (e - 2))
+            nc.sync.dma_start(w2_raw[e][:].bitcast(I32), w2_words[e, 0].bitcast(I32))
 
-        def load_scales(queue, scale_tile, scales, lo, hi):
+        def load_scales(queue, scale_tile, scales):
             by_row = scales.bitcast(I32).rearrange("e s f i -> f (e s) i")
             for q in range(4):
-                queue.dma_start(scale_tile[32 * q : 32 * q + 4, lo:hi].bitcast(I32), by_row[4 * q : 4 * q + 4, lo:hi])
+                queue.dma_start(scale_tile[32 * q : 32 * q + 4].bitcast(I32), by_row[4 * q : 4 * q + 4])
 
-        def load_saved(which, e, g, pair=None):
-            if not pair:
-                place = (A1 if which == 1 else A3)[e, g]
-                saved[which, e, g] = placed([P, X4, C], F32, f"a{which}_{e}{g}", place)
-            planes = slice(0, X4) if pair is None else slice(2 * pair, 2 * pair + 2)
-            rows = (a1 if which == 1 else a3)[512 * g : 512 * (g + 1), C * e : C * (e + 1)]
-            nc.sync.dma_start(saved[which, e, g][:, planes, :], rows.rearrange("(p t) s -> p t s", t=X4)[:, planes, :])
+        def load_saved(which, h, lo=0, hi=C):
+            e, g = divmod(h, NG)
+            if lo == 0:
+                saved[which, h] = placed([P, X4, C], F32, f"a{which}_{h}", a_place(which, h))
+            rows = (a1 if which == 1 else a3)[512 * g : 512 * (g + 1), C * e + lo : C * e + hi]
+            nc.sync.dma_start(saved[which, h][:, :, lo:hi], rows.rearrange("(p t) s -> p t s", t=X4))
 
-        def load_w13(pair):
-            lo, hi = 2 * NG * pair, 2 * NG * (pair + 1)
-            for w, words, scale_tile, scales in ((w3_w, w3_words, w3_sc, w3_scales), (w1_w, w1_words, w1_sc, w1_scales)):
-                load_scales(nc.sync, scale_tile, scales, lo, hi)
+        def load_w13(lo, hi):
+            for w, words in ((w3_w, w3_words), (w1_w, w1_words)):
                 by_pass = words.bitcast(I32).rearrange("e s p k -> p (e s) k")
                 nc.sync.dma_start(w[:, lo:hi].bitcast(I32), by_pass[:, lo:hi])
 
-        def gather(e, t):
-            if t == 0:
-                g_planes[e] = placed([P, X4, C], F32, f"g_planes{e}", G_PLANES[e])
-            picked = dy[t][:].indirect(offs_sb[:, (C // 16) * e : (C // 16) * (e + 1)])
-            nc.vector.tensor_tensor(g_planes[e][:, t, :], picked, gates[e], ALU.mult)
-
-        def weave_g(e):
-            g_woven[e] = placed([P, X4 * C], BF16, f"g_woven{e}", WOVEN[e])
-            nc.scalar.copy(woven(g_woven[e][:]), by_lines(g_planes[e][:]))
-
-        def quantise_g(e):
-            if e >= 2:
-                scales = placed([P, C], U8, f"g_scales{e}", STEP_SECOND[e - 2] + 3)
-            else:
-                scales = held.tile([P, C], U8, name=f"g_scales{e}", align_bytes=64)
-            words = held.tile([P, C], U32, name="g_words", align_bytes=64, bufs=3)
-            g_codes[e] = (words, scales)
-            nc.vector.quantize_mx(out=words[:].bitcast(E5M2), scales=scales[:], in_=g_woven[e][:])
-
-        def first_product(e, n):
-            g, s = divmod(n, SB)
-            words, scales = g_codes[e]
-            bank = dh_banks.tile([P, 512], F32, name="dh_bank")
-            nc.tensor.matmul_mx(
-                out=bank[:],
-                lhsT=words[:, P * s : P * (s + 1)].bitcast(E5M2),
-                lhsT_scale=scales[:, P * s : P * (s + 1)],
-                rhs=w2_w[e][:, 1024 * g : 1024 * (g + 1)].bitcast(E2M1),
-                rhs_scale=w2_sc[:, e, 512 * g : 512 * (g + 1)],
-                start=True,
-                stop=True,
+        def sort_words(e, engine_copy):
+            w2_w[e] = held.tile([P, 2 * H], U8, name=f"w2_w{e}", align_bytes=64)
+            engine_copy(
+                w2_w[e][:].bitcast(U16).rearrange("p (g t m) -> p g t m", g=NG, t=X4),
+                w2_raw[e][:].bitcast(U16).rearrange("p (g m t) -> p g t m", g=NG, t=X4),
             )
-            dh[e, n] = bank
 
-        def copy_dh(e, n):
-            dh_sb[e, n] = unturned.tile([P, X4, P], F32, name="dh_sb")
-            nc.scalar.copy(dh_sb[e, n][:], dh[e, n][:].rearrange("p (m t) -> p t m", t=X4))
+        def sort_first_scales():
+            nc.vector.tensor_copy(
+                w2_sc_first[:].rearrange("p (g t m) -> p g t m", g=NG, t=X4),
+                w2_sc_first_raw[:].rearrange("p (g m t) -> p g t m", g=NG, t=X4),
+            )
 
-        def turn(e, n):
-            dh_turned[e, n] = turned_banks.tile([P, X4, P], F32, name="dh_turned")
+        def sort_scales():
+            nc.vector.tensor_copy(
+                w2_sc_sorted[:].rearrange("p (t m) -> p t m", t=X4),
+                w2_sc_raw[:].rearrange("p (m t) -> p t m", t=X4),
+            )
+            for q in range(4):
+                rows = w2_sc_rest[32 * q : 32 * q + 4].rearrange("p e i -> p (e i)")
+                nc.gpsimd.dma_start(rows.bitcast(I32), w2_sc_sorted[24 * q : 24 * (q + 1), :].bitcast(I32))
+
+        def spread_gate(e):
+            gate_bank[e] = dx_banks.tile([P, X4, P], F32, name="gate_bank")
+            for i in range(X4):
+                nc.tensor.transpose(gate_bank[e][:, i, :], gate_col[:, e, i : i + 1].to_broadcast([P, P]), ident[:])
+
+        def gather(k, t, on_vector=False):
+            if t == 0:
+                g_planes[k] = placed([P, X4, CHUNK], F32, f"g_planes{k}", PLANES + 4 * k if k < 3 else a_place(1, k - 2))
+            picked = dy[t][:].indirect(offs_sb[:, CHUNK * k // 16 : CHUNK * (k + 1) // 16])
+            if on_vector:
+                nc.vector.tensor_copy(g_planes[k][:, t, :], picked)
+            else:
+                nc.scalar.activation(g_planes[k][:, t, :], picked, ACT.Copy)
+
+        def gate_block(b):
+            e, s = divmod(b, SB)
+            k, r = divmod(b, 2)
+            if r == 0:
+                g_woven[k] = placed([P, X4 * CHUNK], BF16, f"g_woven{k}", {0: WOVEN + 2, 2: a_place(1, 0)}.get(k, WOVEN))
+            gates = gate_bank[e][:, :, 32 * s : 32 * (s + 1)].rearrange("p i c -> p c i").unsqueeze(2)
+            nc.vector.tensor_tensor(
+                woven(g_woven[k][:, X4 * P * r : X4 * P * (r + 1)]),
+                by_lines(g_planes[k][:, :, P * r : P * (r + 1)]),
+                gates.to_broadcast([P, 32, X4, 4]),
+                ALU.mult,
+            )
+
+        def quantise_g(k):
+            if k < 2:
+                words = held.tile([P, CHUNK], U32, name=f"g_words{k}", align_bytes=64)
+                scales = held.tile([P, CHUNK], U8, name=f"g_scales{k}", align_bytes=64)
+            else:
+                words = placed([P, CHUNK], U32, f"g_words{k}", a_place(3, k - 2))
+                scales = placed([P, CHUNK], U8, f"g_scales{k}", a_place(1, k - 1) + 5)
+            g_codes[k] = (words, scales)
+            nc.vector.quantize_mx(out=words[:].bitcast(E5M2), scales=scales[:], in_=g_woven[k][:])
+
+        def first_product(n):
+            h, s = divmod(n, SB)
+            e, g = divmod(h, NG)
+            k, r = divmod(SB * e + s, 2)
+            words, scales = g_codes[k]
+            dh[n] = dh_banks.tile([P, X4, P], F32, name="dh_bank")
             for t in range(X4):
-                nc.tensor.transpose(dh_turned[e, n][:, t, :], dh_sb[e, n][:, t, :], ident[:])
+                col = 512 * g + P * t
+                nc.tensor.matmul_mx(
+                    out=dh[n][:, t, :],
+                    lhsT=w2_w[e][:, 2 * col : 2 * (col + P)].bitcast(E2M1),
+                    lhsT_scale=w2_sc[e][:, col : col + P],
+                    rhs=words[:, P * r : P * (r + 1)].bitcast(E5M2),
+                    rhs_scale=scales[:, P * r : P * (r + 1)],
+                    start=True,
+                    stop=True,
+                )
 
-        def first_products(k):
-            e, n = PAIRS[k]
-            for m in (n, n + 1) if n < SB else (n + 1, n):
-                first_product(e, m)
+        def relu_a1(h, lo=0, hi=C):
+            if lo == 0:
+                kept[h] = placed([P, C, X4], F32, f"kept{h}", KEPT + 8 * (h % 2))
+            into = kept[h][:, lo:hi, :].rearrange("p (c i) t -> p c t i", i=4)
+            nc.scalar.activation(into, by_lines(saved[1, h][:, :, lo:hi]), ACT.Relu)
 
-        def pair_of_steps(e, n):
-            k = PAIRS.index((e, n))
-            order = (n + 1, n) if n < SB else (n, n + 1)
-            for m in order:
-                copy_dh(e, m)
-            if k + AHEAD < len(PAIRS):
-                first_products(k + AHEAD)
-            for m in order:
-                turn(e, m)
+        def kept_of(n):
+            h, s = divmod(n, SB)
+            return kept[h][:, P * s : P * (s + 1), :]
 
-        def relu_a1(e, g):
-            kept = saved[1, e, g][:]
-            nc.scalar.activation(kept, kept, ACT.Relu)
+        def mask_dh(n):
+            pair, r = divmod(n, 2)
+            if r == 0:
+                dhm[pair] = held.tile([P, CHUNK, X4], F32, name="dhm", bufs=2)
+            masked = dhm[pair][:, P * r : P * (r + 1), :]
+            nc.vector.scalar_tensor_tensor(masked, kept_of(n), 0.0, in_turn(dh[n][:]), ALU.is_gt, ALU.mult)
 
-        def relu_pair(e, g, pair):
-            kept = saved[1, e, g][:, 2 * pair : 2 * pair + 2, :]
-            nc.scalar.activation(kept, kept, ACT.Relu)
+        def make_da3(n):
+            h, s = divmod(n, SB)
+            nc.vector.tensor_tensor(da[h][:, 0, P * s : P * (s + 1), :], in_turn(dh[n][:]), kept_of(n), ALU.mult)
 
-        def sign_second(e):
-            steps[e, 1] = placed([P, X4, C], BF16, f"step{e}1", STEP_SECOND[e])
-            nc.scalar.activation(steps[e, 1][:], saved[1, e, 1][:], ACT.Sign)
+        def make_da1(pair):
+            h, r = divmod(pair, 2)
+            factor = saved[3, h][:, :, CHUNK * r : CHUNK * (r + 1)]
+            nc.gpsimd.tensor_tensor(da[h][:, 1, CHUNK * r : CHUNK * (r + 1), :], dhm[pair][:], in_turn(factor), ALU.mult)
 
-        def sign_rest(e):
-            lo = 0 if e == LAST else P
-            steps[e, 0] = placed([P, X4, C - P], BF16, f"step{e}0", STEP_REST[e])
-            nc.scalar.activation(steps[e, 0][:], saved[1, e, 0][:, :, lo : lo + C - P], ACT.Sign)
+        def quantise_da(h):
+            words = placed([P, 2 * C], U32, f"da_words{h}", a_place(3, h) + 2)
+            scales = placed([P, 2 * C], U8, f"da_scales{h}", a_place(1, min(h + 1, HALVES - 1)) + (4 if h + 1 < HALVES else 6))
+            nc.vector.quantize_mx(out=words[:].bitcast(E5M2), scales=scales[:], in_=da[h][:].rearrange("p w j t -> p (w j t)"))
+            da_codes[h] = (words, scales)
 
-        def sign_late():
-            steps["late"] = held.tile([P, X4, P], BF16, name="step_late")
-            nc.scalar.activation(steps["late"][:], saved[1, LAST, 0][:, :, C - P : C], ACT.Sign)
-
-        def mask_late():
-            tile = placed([P, X4, P], F32, "masked_late", MASKED_LATE)
-            nc.gpsimd.tensor_tensor(tile[:], saved[3, LAST, 0][:, :, C - P : C], steps["late"][:], ALU.mult)
-            masked[LAST, SB - 1] = tile[:]
-
-        def step_on_vector(e):
-            steps[e, 1] = placed([P, X4, C], BF16, f"step{e}1", STEP_SECOND[e])
-            nc.vector.tensor_scalar(steps[e, 1][:, :, quarter(0)], saved[1, e, 1][:, :, quarter(0)], 0.0, None, ALU.is_gt)
-
-        def mask_on_vector(tile, e, cols):
-            kept, raw = saved[1, e, 0][:, :, cols], saved[3, e, 0][:, :, cols]
-            nc.vector.scalar_tensor_tensor(tile[:], kept, 0.0, raw, ALU.is_gt, ALU.mult)
-
-        def mask_first(e):
-            width, place = (C, MASKED_REST) if e == 0 else (P, STEP_SECOND[e - 1])
-            tile = placed([P, X4, width], F32, f"masked_first{e}", place)
-            mask_on_vector(tile, e, slice(0, width))
-            for s in range(width // P):
-                masked[e, s] = tile[:, :, P * s : P * (s + 1)]
-
-        def mask_rest(e):
-            tile = placed([P, X4, C - P], F32, f"masked_rest{e}", MASKED_REST)
-            lo = 0 if e == LAST else 1
-            nc.gpsimd.tensor_tensor(tile[:], saved[3, e, 0][:, :, P * lo : P * lo + C - P], steps[e, 0][:], ALU.mult)
-            for s in range(SB - 1):
-                masked[e, lo + s] = tile[:, :, P * s : P * (s + 1)]
-
-        def mask_second(e):
-            for h in range(2):
-                tile = placed([P, X4, HALF], F32, f"masked_second{e}{h}", MASKED_SECOND[e] + 4 * h)
-                nc.gpsimd.tensor_tensor(tile[:], saved[3, e, 1][:, :, quarter(h)], steps[e, 1][:, :, quarter(h)], ALU.mult)
-                for r in range(2):
-                    masked[e, SB + 2 * h + r] = tile[:, :, P * r : P * (r + 1)]
-
-        def product(which, e, n):
-            g, s = divmod(n, SB)
-            if n == 0:
-                da[which, e] = placed([P, NG * X4 * C], BF16, f"da{which}_{e}", DA1 if which == 1 else DA3[e])
-            factor = masked[e, n] if which == 1 else saved[1, e, g][:, :, P * s : P * (s + 1)]
-            run = da[which, e][:, X4 * P * n : X4 * P * (n + 1)]
-            nc.vector.tensor_tensor(woven(run), by_lines(dh_turned[e, n][:]), by_lines(factor), ALU.mult)
-
-        def both_products(e, lo, hi):
-            for n in range(lo, hi):
-                product(3, e, n)
-                product(1, e, n)
-
-        def quantise_da(which, e, first, count):
-            cols = C * count
-            if e == LAST:
-                scales = placed([P, cols], U8, f"da_scales{which}{e}{first}", STEP_SECOND[e] + first + (which == 1) / 2)
-            elif which == 3:
-                scales = placed([P, cols], U8, f"da_scales{which}{e}", STEP_SECOND[e] + 2)
-            else:
-                scales = held.tile([P, cols], U8, name="da_scales1", align_bytes=64, bufs=3)
-            if e in WORDS:
-                words = placed([P, cols], U32, f"da_words{which}{e}{first}", WORDS[e] + 4 * (which == 1) + 2 * first)
-            else:
-                words = held.tile([P, cols], U32, name=f"da_words{which}", align_bytes=64, bufs=2)
-            run = da[which, e][:, X4 * C * first : X4 * C * (first + count)]
-            nc.vector.quantize_mx(out=words[:].bitcast(E5M2), scales=scales[:], in_=run)
-            for g in range(count):
-                da_codes[which, e, first + g] = (words[:, C * g : C * (g + 1)], scales[:, C * g : C * (g + 1)])
-
-        def second_product(e):
-            passes = [(which, g) for g in range(NG) for which in (3, 1)]
+        def second_product(h):
+            e, g = divmod(h, NG)
+            words, scales = da_codes[h]
             for kb in range(KB):
-                bank = dh_banks.tile([P, C], F32, name="dh_bank")
-                for n, (which, g) in enumerate(passes):
-                    w, scale_tile = (w1_w, w1_sc) if which == 1 else (w3_w, w3_sc)
-                    words, scales = da_codes[which, e, g]
+                if g == 0:
+                    dx_bank[kb] = dx_banks.tile([P, C], F32, name=f"dx_bank{kb}")
+                for n, (w, scale_tile) in enumerate(((w3_w, w3_sc), (w1_w, w1_sc))):
                     nc.tensor.matmul_mx(
-                        out=bank[:],
-                        lhsT=w[:, NG * e + g, 2 * P * kb : 2 * P * (kb + 1)].bitcast(E2M1),
-                        lhsT_scale=scale_tile[:, NG * e + g, P * kb : P * (kb + 1)],
-                        rhs=words.bitcast(E5M2),
-                        rhs_scale=scales,
-                        start=(n == 0),
-                        stop=(n == len(passes) - 1),
+                        out=dx_bank[kb][:],
+                        lhsT=w[:, h, 2 * P * kb : 2 * P * (kb + 1)].bitcast(E2M1),
+                        lhsT_scale=scale_tile[:, h, P * kb : P * (kb + 1)],
+                        rhs=words[:, C * n : C * (n + 1)].bitcast(E5M2),
+                        rhs_scale=scales[:, C * n : C * (n + 1)],
+                        start=(g == 0 and n == 0),
+                        stop=(g == NG - 1 and n == 1),
                     )
+
+        def copy_dx(e):
+            for kb in range(KB):
                 if e == 0:
-                    dx.append(placed([P, S], F32, f"dx{kb}", DX + 8 * kb))
-                nc.scalar.copy(dx[kb][:, C * e : C * (e + 1)], bank[:])
+                    dx.append(placed([P, S], F32, f"dx{kb}", DX_LAST if kb else a_place(1, 0)))
+                if e == E - 1 and kb == 1:
+                    nc.vector.tensor_copy(dx[kb][:, C * e : C * (e + 1)], dx_bank[kb][:])
+                else:
+                    nc.scalar.copy(dx[kb][:, C * e : C * (e + 1)], dx_bank[kb][:])
 
-        load_scales(nc.gpsimd, w2_sc, w2_scales, 0, E)
+        for q in range(4):
+            rows = w2_scales.bitcast(I32)[0, 0, 4 * q : 4 * q + 4]
+            nc.gpsimd.dma_start(w2_sc_first_raw[32 * q : 32 * q + 4, :].bitcast(I32), rows)
+        make_identity(nc, ident[:])
         nc.sync.dma_start(offs_sb[:], offs)
+        load_saved(1, 0, 0, EARLY)
         load_dy(0)
-        load_gates(0, 1)
-        load_gates(1, 2)
+        nc.sync.dma_start(gate_col[:], gate[0:1, :].rearrange("o (e p i) -> p (o e) i", e=E, i=X4))
         load_dy(1)
-        load_saved(1, 0, 1, 0)
         load_dy(2)
-        load_saved(1, 0, 1, 1)
-        load_dy(3)
-        load_saved(1, 0, 0, 0)
-        load_gates(2, 3)
         load_w2(0)
-        load_saved(1, 0, 0, 1)
-        load_gates(3, E)
-        load_saved(1, 1, 0)
-        load_saved(3, 0, 1)
-        load_saved(3, 0, 0)
+        load_dy(3)
+        load_saved(1, 0, EARLY, CHUNK)
+        load_saved(3, 0, 0, CHUNK)
+        load_saved(1, 0, CHUNK, C)
+        load_saved(3, 0, CHUNK, C)
+        by_half = w2_scales.bitcast(I32).rearrange("e s f (g i) -> g f (e s) i", g=NG)
+        for g in range(NG):
+            nc.sync.dma_start(w2_sc_raw[g : 96 : NG, :].bitcast(I32), by_half[g, :, 1:E])
+        load_saved(1, 1)
+        load_saved(3, 1)
         load_w2(1)
-        load_saved(1, 1, 1)
-        load_saved(3, 1, 0)
-        load_saved(1, 2, 0)
-        load_saved(3, 1, 1)
-        w1_w = held.tile([P, E * NG, 2 * K], U8, name="w1_w", align_bytes=64)
-        w3_w = held.tile([P, E * NG, 2 * K], U8, name="w3_w", align_bytes=64)
+        load_scales(nc.sync, w3_sc, w3_scales)
+        load_scales(nc.sync, w1_sc, w1_scales)
+        load_w13(0, 2 * NG)
 
-        for pair in range(2):
-            relu_pair(0, 1, pair)
-        sign_second(0)
-        for t in range(X4):
+        relu_a1(0, 0, EARLY)
+        spread_gate(0)
+        sort_first_scales()
+        for t in range(X4 - 1):
             gather(0, t)
-            gather(1, t)
-        weave_g(0)
-        quantise_g(0)
-        for t in range(X4):
+            gather(1, t, on_vector=True)
             gather(2, t)
-        for pair in range(2):
-            relu_pair(0, 0, pair)
-        for t in range(X4):
-            gather(LAST, t)
-        load_w2(2)
-        load_saved(3, 2, 0)
-        load_saved(1, 2, 1)
-        weave_g(1)
-        for k in range(AHEAD):
-            first_products(k)
-        pair_of_steps(0, 2)
-        pair_of_steps(0, 0)
-        quantise_g(1)
-        mask_first(0)
-
-        mask_second(0)
-        relu_a1(1, 0)
-        pair_of_steps(0, 4)
-        sign_rest(1)
-        pair_of_steps(0, 6)
-        both_products(0, 0, SB)
-        mask_rest(1)
-        weave_g(2)
-        both_products(0, SB, STEPS)
-        pair_of_steps(1, 2)
-        relu_a1(1, 1)
-        pair_of_steps(1, 0)
-        sign_second(1)
-        load_saved(1, 3, 0)
-        load_saved(3, 2, 1)
-        load_w2(3)
-        load_saved(1, 3, 1)
-        load_saved(3, 3, 0)
-        quantise_g(2)
-        mask_first(1)
-        quantise_da(3, 0, 0, NG)
-        quantise_da(1, 0, 0, NG)
-
-        mask_second(1)
-        pair_of_steps(1, 4)
-        relu_a1(2, 0)
-        pair_of_steps(1, 6)
-        sign_rest(2)
-        both_products(1, 0, SB)
-        mask_rest(2)
-        weave_g(LAST)
-        both_products(1, SB, STEPS)
-        pair_of_steps(2, 2)
-        pair_of_steps(2, 0)
-        relu_a1(2, 1)
-        load_w13(0)
-        load_saved(3, 3, 1)
-        load_w13(1)
+        sort_words(0, nc.vector.tensor_copy)
+        gather(0, X4 - 1)
+        gather(1, X4 - 1, on_vector=True)
+        for k in range(2):
+            gate_block(2 * k)
+            gate_block(2 * k + 1)
+            quantise_g(k)
+        relu_a1(0, EARLY, CHUNK)
+        relu_a1(0, CHUNK, C)
+        gather(2, X4 - 1)
+        for n in range(SB):
+            first_product(n)
+        mask_dh(0)
+        mask_dh(1)
+        sort_scales()
+        for h in range(2, HALVES):
+            load_saved(1, h)
+            load_saved(3, h)
+            if h in (2, 4):
+                load_w2(h // 2 + 1)
+            if h == 3:
+                load_w13(2 * NG, E * NG)
         nc.sync.dma_start(pos1_sb[:], pos1)
         nc.sync.dma_start(pos2_sb[:], pos2)
-        quantise_g(LAST)
-        mask_first(2)
-        step_on_vector(2)
-        quantise_da(3, 1, 0, NG)
-        quantise_da(1, 1, 0, NG)
 
-        pair_of_steps(2, 4)
-        relu_a1(3, 0)
-        nc.scalar.activation(steps[2, 1][:, :, quarter(1)], saved[1, 2, 1][:, :, quarter(1)], ACT.Sign)
-        mask_second(2)
-        sign_rest(3)
-        pair_of_steps(2, 6)
-        both_products(2, 0, SB)
-        mask_rest(3)
-        both_products(2, SB, STEPS)
-        pair_of_steps(3, 2)
-        relu_a1(3, 1)
-        pair_of_steps(3, 0)
-        sign_late()
-        sign_second(3)
-        second_product(0)
-        quantise_da(3, 2, 0, NG)
-        quantise_da(1, 2, 0, NG)
+        for h in range(HALVES):
+            e, g = divmod(h, NG)
+            k, n = h + 2, SB * h
+            more = h + 1 < HALVES
+            if k < CHUNKS and g == 0:
+                spread_gate(e + 1)
+            if more:
+                relu_a1(h + 1)
+            if k + 1 < CHUNKS:
+                for t in range(X4):
+                    gather(k + 1, t)
+            if g == 0 and e + 1 < E:
+                sort_words(e + 1, nc.scalar.copy)
+            da[h] = placed([P, 2, C, X4], BF16, f"da{h}", DA)
+            make_da1(2 * h)
+            make_da3(n)
+            mask_dh(n + 2)
+            mask_dh(n + 3)
+            make_da1(2 * h + 1)
+            if more:
+                first_product(n + SB)
+                first_product(n + SB + 1)
+            for s in range(1, SB):
+                make_da3(n + s)
+                if k < CHUNKS and s > 1:
+                    gate_block(2 * k + s - 2)
+            if more:
+                mask_dh(n + SB)
+                mask_dh(n + SB + 1)
+            if k < CHUNKS:
+                quantise_g(k)
+            if more:
+                first_product(n + SB + 2)
+                first_product(n + SB + 3)
+            quantise_da(h)
+            second_product(h)
+            if g == 1:
+                copy_dx(e)
 
-        mask_late()
-        mask_second(3)
-        pair_of_steps(3, 4)
-        pair_of_steps(3, 6)
-        for e in range(1, LAST):
-            second_product(e)
-        both_products(3, 0, STEPS)
-        quantise_da(3, 3, 0, 1)
-        quantise_da(1, 3, 0, 1)
-        quantise_da(3, 3, 1, 1)
-        quantise_da(1, 3, 1, 1)
-        second_product(LAST)
+        HT = T // 2
+        firsts = [placed([P, T], F32, f"first{kb}", DY + 4 * kb) for kb in range(KB)]
+        seconds = [placed([P, T], F32, f"second{kb}", DY + 8 + 4 * kb) for kb in range(KB)]
+        totals = [placed([P, T], F32, f"total{kb}", a_place(1, 2 + kb)) for kb in range(KB)]
 
-        firsts = []
+        def add_and_store(kb, lo, hi):
+            nc.vector.tensor_tensor(totals[kb][:, lo:hi], firsts[kb][:, lo:hi], seconds[kb][:, lo:hi], ALU.add)
+            nc.sync.dma_start(out[P * kb : P * (kb + 1), lo:hi], totals[kb][:, lo:hi])
+
         for kb in range(KB):
-            firsts.append(placed([P, T], F32, f"first{kb}", A1[1, 0] + 4 * kb))
-            nc.vector.tensor_copy(firsts[kb][:], dx[kb][:].indirect(pos1_sb[:]))
-        for kb in range(KB):
-            total = placed([P, T], F32, f"total{kb}", A1[1, 1] + 4 * kb)
-            cuts = (0, T // 2, T) if kb < KB - 1 else (0, T // 2, T - P, T)
-            for lo, hi in zip(cuts, cuts[1:]):
-                picked = dx[kb][:].indirect(pos2_sb[:, lo // 16 : hi // 16])
-                nc.vector.tensor_tensor(total[:, lo:hi], picked, firsts[kb][:, lo:hi], ALU.add)
-                nc.sync.dma_start(out[P * kb : P * (kb + 1), lo:hi], total[:, lo:hi])
+            nc.scalar.activation(firsts[kb][:], dx[kb][:].indirect(pos1_sb[:]), ACT.Copy)
+        nc.scalar.activation(seconds[1][:, HT:], dx[1][:].indirect(pos2_sb[:, HT // 16 :]), ACT.Copy)
+        nc.vector.tensor_copy(seconds[0][:], dx[0][:].indirect(pos2_sb[:]))
+        add_and_store(0, 0, T)
+        nc.vector.tensor_copy(seconds[1][:, :HT], dx[1][:].indirect(pos2_sb[:, : HT // 16]))
+        add_and_store(1, 0, HT)
+        add_and_store(1, HT, T)

@@ -13,6 +13,7 @@ KB = K // P
 HALVES = E * NG
 CHUNK = 2 * P
 CHUNKS = S // CHUNK
+GPSIMD_SLOTS = (C, C, C, C, C, C, C - P, C - CHUNK)
 EARLY = 32
 
 F32 = mybir.dt.float32
@@ -45,10 +46,6 @@ def by_lines(planes):
     return planes.rearrange("p t (c i) -> p c t i", i=4)
 
 
-def in_turn(planes):
-    return planes.rearrange("p t j -> p j t")
-
-
 def woven(flat):
     return flat.rearrange("p (c i t) -> p c t i", i=4, t=X4)
 
@@ -70,21 +67,13 @@ def tile_moe_bdx_glu_relu_kernel(
         pos1_sb = held.tile([P, T // 16], U16, name="pos1_sb")
         pos2_sb = held.tile([P, T // 16], U16, name="pos2_sb")
         w2_sc_raw = held.tile([P, 512], U8, name="w2_sc_raw")
-        w2_sc_sorted = held.tile([P, 512], U8, name="w2_sc_sorted")
-        w2_sc_first_raw = held.tile([P, H], U8, name="w2_sc_first_raw")
-        w2_sc_first = held.tile([P, H], U8, name="w2_sc_first", align_bytes=64)
-        w2_sc_rest = held.tile([P, E - 1, H], U8, name="w2_sc_rest", align_bytes=64)
-        w2_sc = [w2_sc_first[:]] + [w2_sc_rest[:, e, :] for e in range(E - 1)]
-        w1_sc = held.tile([P, E * NG, K], U8, name="w1_sc", align_bytes=64)
-        w3_sc = held.tile([P, E * NG, K], U8, name="w3_sc", align_bytes=64)
+        spread = held.tile([P, 512 + 2 * K], U8, name="spread")
+        scale_rows = held.tile([P, HALVES, 512 + 2 * K], U8, name="scale_rows", align_bytes=64)
         w1_w = held.tile([P, E * NG, 2 * K], U8, name="w1_w", align_bytes=64)
         w3_w = held.tile([P, E * NG, 2 * K], U8, name="w3_w", align_bytes=64)
         ident = held.tile([P, P], F32, name="ident")
         gate_col = held.tile([P, E, X4], F32, name="gate_col")
-        for scale_tile in (w2_sc_first_raw, w2_sc_raw):
-            nc.vector.memset(scale_tile[:].bitcast(I32), 0)
-        for scale_tile in (w2_sc_rest, w1_sc, w3_sc):
-            nc.vector.memset(scale_tile[:].rearrange("p e i -> p (e i)").bitcast(I32), 0)
+        nc.vector.memset(scale_rows[:].rearrange("p h i -> p (h i)").bitcast(I32), 0)
 
         dy, dx = [], []
         w2_raw, w2_w, saved, gate_bank = {}, {}, {}, {}
@@ -96,16 +85,16 @@ def tile_moe_bdx_glu_relu_kernel(
             nc.sync.dma_start(dy[t][:], dyT.rearrange("(p t) s -> t p s", t=X4)[t])
 
         def load_w2(e):
-            if e < 2:
-                w2_raw[e] = held.tile([P, 2 * H], U8, name=f"w2_raw{e}")
-            else:
-                w2_raw[e] = placed([P, 2 * H], U8, f"w2_raw{e}", PLANES + 2 * (e - 2))
+            w2_raw[e] = held.tile([P, 2 * H], U8, name=f"w2_raw{e}")
             nc.sync.dma_start(w2_raw[e][:].bitcast(I32), w2_words[e, 0].bitcast(I32))
 
-        def load_scales(queue, scale_tile, scales):
-            by_row = scales.bitcast(I32).rearrange("e s f i -> f (e s) i")
-            for q in range(4):
-                queue.dma_start(scale_tile[32 * q : 32 * q + 4].bitcast(I32), by_row[4 * q : 4 * q + 4])
+        def load_scales():
+            by_half = w2_scales.bitcast(I32).rearrange("e s f (g i) -> g f (e s) i", g=NG)
+            for g in range(NG):
+                nc.sync.dma_start(w2_sc_raw[g:P:NG, :].bitcast(I32), by_half[g])
+            for n, scales in enumerate((w3_scales, w1_scales)):
+                into = spread[:, 512 + K * n : 512 + K * (n + 1)]
+                nc.sync.dma_start(into.bitcast(I32), scales.bitcast(I32).rearrange("e s f i -> f (e s) i"))
 
         def load_saved(which, h, lo=0, hi=C):
             e, g = divmod(h, NG)
@@ -126,20 +115,14 @@ def tile_moe_bdx_glu_relu_kernel(
                 w2_raw[e][:].bitcast(U16).rearrange("p (g m t) -> p g t m", g=NG, t=X4),
             )
 
-        def sort_first_scales():
+        def deal_scales():
             nc.vector.tensor_copy(
-                w2_sc_first[:].rearrange("p (g t m) -> p g t m", g=NG, t=X4),
-                w2_sc_first_raw[:].rearrange("p (g m t) -> p g t m", g=NG, t=X4),
-            )
-
-        def sort_scales():
-            nc.vector.tensor_copy(
-                w2_sc_sorted[:].rearrange("p (t m) -> p t m", t=X4),
+                spread[:, 0:512].rearrange("p (t m) -> p t m", t=X4),
                 w2_sc_raw[:].rearrange("p (m t) -> p t m", t=X4),
             )
             for q in range(4):
-                rows = w2_sc_rest[32 * q : 32 * q + 4].rearrange("p e i -> p (e i)")
-                nc.gpsimd.dma_start(rows.bitcast(I32), w2_sc_sorted[24 * q : 24 * (q + 1), :].bitcast(I32))
+                rows = scale_rows[32 * q : 32 * q + 4].rearrange("p h i -> p (h i)")
+                nc.gpsimd.dma_start(rows.bitcast(I32), spread[32 * q : 32 * (q + 1), :].bitcast(I32))
 
         def spread_gate(e):
             gate_bank[e] = dx_banks.tile([P, X4, P], F32, name="gate_bank")
@@ -189,7 +172,7 @@ def tile_moe_bdx_glu_relu_kernel(
                 nc.tensor.matmul_mx(
                     out=dh[n][:, t, :],
                     lhsT=w2_w[e][:, 2 * col : 2 * (col + P)].bitcast(E2M1),
-                    lhsT_scale=w2_sc[e][:, col : col + P],
+                    lhsT_scale=scale_rows[:, h, P * t : P * (t + 1)],
                     rhs=words[:, P * r : P * (r + 1)].bitcast(E5M2),
                     rhs_scale=scales[:, P * r : P * (r + 1)],
                     start=True,
@@ -198,34 +181,35 @@ def tile_moe_bdx_glu_relu_kernel(
 
         def relu_a1(h, lo=0, hi=C):
             if lo == 0:
-                kept[h] = placed([P, C, X4], F32, f"kept{h}", KEPT + 8 * (h % 2))
-            into = kept[h][:, lo:hi, :].rearrange("p (c i) t -> p c t i", i=4)
-            nc.scalar.activation(into, by_lines(saved[1, h][:, :, lo:hi]), ACT.Relu)
+                kept[h] = placed([P, X4, C], F32, f"kept{h}", KEPT + 8 * (h % 2))
+            nc.scalar.activation(kept[h][:, :, lo:hi], saved[1, h][:, :, lo:hi], ACT.Relu)
 
         def kept_of(n):
             h, s = divmod(n, SB)
-            return kept[h][:, P * s : P * (s + 1), :]
+            return kept[h][:, :, P * s : P * (s + 1)]
 
         def mask_dh(n):
             pair, r = divmod(n, 2)
             if r == 0:
-                dhm[pair] = held.tile([P, CHUNK, X4], F32, name="dhm", bufs=2)
-            masked = dhm[pair][:, P * r : P * (r + 1), :]
-            nc.vector.scalar_tensor_tensor(masked, kept_of(n), 0.0, in_turn(dh[n][:]), ALU.is_gt, ALU.mult)
+                dhm[pair] = held.tile([P, X4, CHUNK], F32, name="dhm", bufs=2)
+            masked = dhm[pair][:, :, P * r : P * (r + 1)]
+            nc.vector.scalar_tensor_tensor(masked, kept_of(n), 0.0, dh[n][:], ALU.is_gt, ALU.mult)
 
         def make_da3(n):
             h, s = divmod(n, SB)
-            nc.vector.tensor_tensor(da[h][:, 0, P * s : P * (s + 1), :], in_turn(dh[n][:]), kept_of(n), ALU.mult)
+            run = da[h][:, 0, X4 * P * s : X4 * P * (s + 1)]
+            nc.vector.tensor_tensor(woven(run), by_lines(dh[n][:]), by_lines(kept_of(n)), ALU.mult)
 
-        def make_da1(pair):
-            h, r = divmod(pair, 2)
-            factor = saved[3, h][:, :, CHUNK * r : CHUNK * (r + 1)]
-            nc.gpsimd.tensor_tensor(da[h][:, 1, CHUNK * r : CHUNK * (r + 1), :], dhm[pair][:], in_turn(factor), ALU.mult)
+        def make_da1(engine, h, lo, hi):
+            pair, start = 2 * h + lo // CHUNK, lo % CHUNK
+            masked = dhm[pair][:, :, start : start + hi - lo]
+            run = da[h][:, 1, X4 * lo : X4 * hi]
+            engine.tensor_tensor(woven(run), by_lines(masked), by_lines(saved[3, h][:, :, lo:hi]), ALU.mult)
 
         def quantise_da(h):
             words = placed([P, 2 * C], U32, f"da_words{h}", a_place(3, h) + 2)
             scales = placed([P, 2 * C], U8, f"da_scales{h}", a_place(1, min(h + 1, HALVES - 1)) + (4 if h + 1 < HALVES else 6))
-            nc.vector.quantize_mx(out=words[:].bitcast(E5M2), scales=scales[:], in_=da[h][:].rearrange("p w j t -> p (w j t)"))
+            nc.vector.quantize_mx(out=words[:].bitcast(E5M2), scales=scales[:], in_=da[h][:].rearrange("p w j -> p (w j)"))
             da_codes[h] = (words, scales)
 
         def second_product(h):
@@ -234,11 +218,12 @@ def tile_moe_bdx_glu_relu_kernel(
             for kb in range(KB):
                 if g == 0:
                     dx_bank[kb] = dx_banks.tile([P, C], F32, name=f"dx_bank{kb}")
-                for n, (w, scale_tile) in enumerate(((w3_w, w3_sc), (w1_w, w1_sc))):
+                for n, w in enumerate((w3_w, w1_w)):
+                    col = 512 + K * n + P * kb
                     nc.tensor.matmul_mx(
                         out=dx_bank[kb][:],
                         lhsT=w[:, h, 2 * P * kb : 2 * P * (kb + 1)].bitcast(E2M1),
-                        lhsT_scale=scale_tile[:, h, P * kb : P * (kb + 1)],
+                        lhsT_scale=scale_rows[:, h, col : col + P],
                         rhs=words[:, C * n : C * (n + 1)].bitcast(E5M2),
                         rhs_scale=scales[:, C * n : C * (n + 1)],
                         start=(g == 0 and n == 0),
@@ -254,13 +239,11 @@ def tile_moe_bdx_glu_relu_kernel(
                 else:
                     nc.scalar.copy(dx[kb][:, C * e : C * (e + 1)], dx_bank[kb][:])
 
-        for q in range(4):
-            rows = w2_scales.bitcast(I32)[0, 0, 4 * q : 4 * q + 4]
-            nc.gpsimd.dma_start(w2_sc_first_raw[32 * q : 32 * q + 4, :].bitcast(I32), rows)
         make_identity(nc, ident[:])
         nc.sync.dma_start(offs_sb[:], offs)
         load_saved(1, 0, 0, EARLY)
         load_dy(0)
+        load_scales()
         nc.sync.dma_start(gate_col[:], gate[0:1, :].rearrange("o (e p i) -> p (o e) i", e=E, i=X4))
         load_dy(1)
         load_dy(2)
@@ -270,19 +253,14 @@ def tile_moe_bdx_glu_relu_kernel(
         load_saved(3, 0, 0, CHUNK)
         load_saved(1, 0, CHUNK, C)
         load_saved(3, 0, CHUNK, C)
-        by_half = w2_scales.bitcast(I32).rearrange("e s f (g i) -> g f (e s) i", g=NG)
-        for g in range(NG):
-            nc.sync.dma_start(w2_sc_raw[g : 96 : NG, :].bitcast(I32), by_half[g, :, 1:E])
         load_saved(1, 1)
         load_saved(3, 1)
         load_w2(1)
-        load_scales(nc.sync, w3_sc, w3_scales)
-        load_scales(nc.sync, w1_sc, w1_scales)
         load_w13(0, 2 * NG)
 
         relu_a1(0, 0, EARLY)
         spread_gate(0)
-        sort_first_scales()
+        deal_scales()
         for t in range(X4 - 1):
             gather(0, t)
             gather(1, t, on_vector=True)
@@ -301,7 +279,6 @@ def tile_moe_bdx_glu_relu_kernel(
             first_product(n)
         mask_dh(0)
         mask_dh(1)
-        sort_scales()
         for h in range(2, HALVES):
             load_saved(1, h)
             load_saved(3, h)
@@ -325,12 +302,13 @@ def tile_moe_bdx_glu_relu_kernel(
                     gather(k + 1, t)
             if g == 0 and e + 1 < E:
                 sort_words(e + 1, nc.scalar.copy)
-            da[h] = placed([P, 2, C, X4], BF16, f"da{h}", DA)
-            make_da1(2 * h)
+            da[h] = placed([P, 2, X4 * C], BF16, f"da{h}", DA)
+            make_da1(nc.gpsimd, h, 0, CHUNK)
             make_da3(n)
             mask_dh(n + 2)
             mask_dh(n + 3)
-            make_da1(2 * h + 1)
+            if GPSIMD_SLOTS[h] > CHUNK:
+                make_da1(nc.gpsimd, h, CHUNK, GPSIMD_SLOTS[h])
             if more:
                 first_product(n + SB)
                 first_product(n + SB + 1)
@@ -343,6 +321,8 @@ def tile_moe_bdx_glu_relu_kernel(
                 mask_dh(n + SB + 1)
             if k < CHUNKS:
                 quantise_g(k)
+            if GPSIMD_SLOTS[h] < C:
+                make_da1(nc.vector, h, GPSIMD_SLOTS[h], C)
             if more:
                 first_product(n + SB + 2)
                 first_product(n + SB + 3)

@@ -13,7 +13,6 @@ KB = K // P
 HALVES = E * NG
 CHUNK = 2 * P
 CHUNKS = S // CHUNK
-GPSIMD_SLOTS = (C, C, C, C, C, C, C - P, C - CHUNK)
 EARLY = 32
 
 F32 = mybir.dt.float32
@@ -31,11 +30,10 @@ FLOPS = 2 * S * N * H + 2 * 2 * S * H * K
 BYTES = 4 * (N * T + 2 * H * S + S + K * T) + E * (N * H + 2 * H * K) // 2 + E * (N * H + 2 * H * K) // 32 + 2 * 128 * 256
 
 DY = 16 * HALVES
-DA = DY + 16
+MASKED = DY + 16
+PLANES = MASKED + 16
+DA = PLANES + 8
 WOVEN = DA + 8
-KEPT = WOVEN + 4
-PLANES = KEPT + 16
-DX_LAST = PLANES + 12
 
 
 def a_place(which, h):
@@ -73,12 +71,13 @@ def tile_moe_bdx_glu_relu_kernel(
         w3_w = held.tile([P, E * NG, 2 * K], U8, name="w3_w", align_bytes=64)
         ident = held.tile([P, P], F32, name="ident")
         gate_col = held.tile([P, E, X4], F32, name="gate_col")
+        gates_sb = held.tile([P, C], F32, name="gates_sb")
         nc.vector.memset(scale_rows[:].rearrange("p h i -> p (h i)").bitcast(I32), 0)
 
         dy, dx = [], []
         w2_raw, w2_w, saved, gate_bank = {}, {}, {}, {}
         g_planes, g_woven, g_codes = {}, {}, {}
-        dh, dhm, da, da_codes, dx_bank, kept = {}, {}, {}, {}, {}, {}
+        dh, dhm, da, da3_codes, da1_codes, dx_bank = {}, {}, {}, {}, {}, {}
 
         def load_dy(t):
             dy.append(placed([P, T], F32, f"dy{t}", DY + 4 * t))
@@ -124,42 +123,40 @@ def tile_moe_bdx_glu_relu_kernel(
                 rows = scale_rows[32 * q : 32 * q + 4].rearrange("p h i -> p (h i)")
                 nc.gpsimd.dma_start(rows.bitcast(I32), spread[32 * q : 32 * (q + 1), :].bitcast(I32))
 
-        def spread_gate(e):
-            gate_bank[e] = dx_banks.tile([P, X4, P], F32, name="gate_bank")
+        def spread_gate(e, bank_name):
+            gate_bank[e] = dx_banks.tile([P, C], F32, name=bank_name)
             for i in range(X4):
-                nc.tensor.transpose(gate_bank[e][:, i, :], gate_col[:, e, i : i + 1].to_broadcast([P, P]), ident[:])
+                nc.tensor.transpose(gate_bank[e][:, i:C:X4], gate_col[:, e, i : i + 1].to_broadcast([P, P]), ident[:])
 
         def gather(k, t, on_vector=False):
             if t == 0:
-                g_planes[k] = placed([P, X4, CHUNK], F32, f"g_planes{k}", PLANES + 4 * k if k < 3 else a_place(1, k - 2))
+                place = MASKED + 8 + 4 * k if k < 4 else a_place(1, k - 4)
+                g_planes[k] = placed([P, X4, CHUNK], F32, f"g_planes{k}", place)
             picked = dy[t][:].indirect(offs_sb[:, CHUNK * k // 16 : CHUNK * (k + 1) // 16])
             if on_vector:
                 nc.vector.tensor_copy(g_planes[k][:, t, :], picked)
             else:
                 nc.scalar.activation(g_planes[k][:, t, :], picked, ACT.Copy)
 
-        def gate_block(b):
-            e, s = divmod(b, SB)
-            k, r = divmod(b, 2)
-            if r == 0:
-                g_woven[k] = placed([P, X4 * CHUNK], BF16, f"g_woven{k}", {0: WOVEN + 2, 2: a_place(1, 0)}.get(k, WOVEN))
-            gates = gate_bank[e][:, :, 32 * s : 32 * (s + 1)].rearrange("p i c -> p c i").unsqueeze(2)
-            nc.vector.tensor_tensor(
-                woven(g_woven[k][:, X4 * P * r : X4 * P * (r + 1)]),
-                by_lines(g_planes[k][:, :, P * r : P * (r + 1)]),
-                gates.to_broadcast([P, 32, X4, 4]),
-                ALU.mult,
+        def gate_chunk(engine, k, gates, into):
+            r = k % 2
+            by_slot = gates[:, CHUNK * r : CHUNK * (r + 1)].rearrange("p (c i) -> p c i", i=4).unsqueeze(2)
+            engine.tensor_tensor(
+                woven(into), by_lines(g_planes[k][:]), by_slot.to_broadcast([P, CHUNK // 4, X4, 4]), ALU.mult
             )
 
-        def quantise_g(k):
-            if k < 2:
-                words = held.tile([P, CHUNK], U32, name=f"g_words{k}", align_bytes=64)
-                scales = held.tile([P, CHUNK], U8, name=f"g_scales{k}", align_bytes=64)
-            else:
-                words = placed([P, CHUNK], U32, f"g_words{k}", a_place(3, k - 2))
-                scales = placed([P, CHUNK], U8, f"g_scales{k}", a_place(1, k - 1) + 5)
-            g_codes[k] = (words, scales)
-            nc.vector.quantize_mx(out=words[:].bitcast(E5M2), scales=scales[:], in_=g_woven[k][:])
+        def quantise(values, words, scales):
+            nc.vector.quantize_mx(out=words.bitcast(E5M2), scales=scales, in_=values)
+
+        def held_codes(name, width):
+            words = held.tile([P, width], U32, name=f"{name}_words", align_bytes=64)
+            scales = held.tile([P, width], U8, name=f"{name}_scales", align_bytes=64)
+            return words, scales
+
+        def placed_codes(name, width, kib):
+            words = placed([P, width], U32, f"{name}_words", kib)
+            scales = placed([P, width], U8, f"{name}_scales", kib + 4 * width / 1024)
+            return words, scales
 
         def first_product(n):
             h, s = divmod(n, SB)
@@ -180,60 +177,47 @@ def tile_moe_bdx_glu_relu_kernel(
                 )
 
         def relu_a1(h, lo=0, hi=C):
-            if lo == 0:
-                kept[h] = placed([P, X4, C], F32, f"kept{h}", KEPT + 8 * (h % 2))
-            nc.scalar.activation(kept[h][:, :, lo:hi], saved[1, h][:, :, lo:hi], ACT.Relu)
-
-        def kept_of(n):
-            h, s = divmod(n, SB)
-            return kept[h][:, :, P * s : P * (s + 1)]
+            nc.scalar.activation(saved[1, h][:, :, lo:hi], saved[1, h][:, :, lo:hi], ACT.Relu)
 
         def mask_dh(n):
-            pair, r = divmod(n, 2)
-            if r == 0:
-                dhm[pair] = held.tile([P, X4, CHUNK], F32, name="dhm", bufs=2)
-            masked = dhm[pair][:, :, P * r : P * (r + 1)]
-            nc.vector.scalar_tensor_tensor(masked, kept_of(n), 0.0, dh[n][:], ALU.is_gt, ALU.mult)
+            h, s = divmod(n, SB)
+            slots = slice(P * s, P * (s + 1))
+            nc.vector.scalar_tensor_tensor(
+                dhm[h][:, :, slots], saved[1, h][:, :, slots], 0.0, dh[n][:], ALU.is_gt, ALU.mult
+            )
 
         def make_da3(n):
             h, s = divmod(n, SB)
             run = da[h][:, 0, X4 * P * s : X4 * P * (s + 1)]
-            nc.vector.tensor_tensor(woven(run), by_lines(dh[n][:]), by_lines(kept_of(n)), ALU.mult)
+            nc.vector.tensor_tensor(
+                woven(run), by_lines(dh[n][:]), by_lines(saved[1, h][:, :, P * s : P * (s + 1)]), ALU.mult
+            )
 
-        def make_da1(engine, h, lo, hi):
-            pair, start = 2 * h + lo // CHUNK, lo % CHUNK
-            masked = dhm[pair][:, :, start : start + hi - lo]
-            run = da[h][:, 1, X4 * lo : X4 * hi]
-            engine.tensor_tensor(woven(run), by_lines(masked), by_lines(saved[3, h][:, :, lo:hi]), ALU.mult)
+        def make_da1(engine, h, into):
+            engine.tensor_tensor(woven(into), by_lines(dhm[h][:]), by_lines(saved[3, h][:]), ALU.mult)
 
-        def quantise_da(h):
-            words = placed([P, 2 * C], U32, f"da_words{h}", a_place(3, h) + 2)
-            scales = placed([P, 2 * C], U8, f"da_scales{h}", a_place(1, min(h + 1, HALVES - 1)) + (4 if h + 1 < HALVES else 6))
-            nc.vector.quantize_mx(out=words[:].bitcast(E5M2), scales=scales[:], in_=da[h][:].rearrange("p w j -> p (w j)"))
-            da_codes[h] = (words, scales)
-
-        def second_product(h):
+        def second_pass(n, h, codes):
             e, g = divmod(h, NG)
-            words, scales = da_codes[h]
+            words, scales = codes
+            opens, closes = (g == 0 and n == 0), (g == NG - 1 and n == 1)
             for kb in range(KB):
-                if g == 0:
+                if opens:
                     dx_bank[kb] = dx_banks.tile([P, C], F32, name=f"dx_bank{kb}")
-                for n, w in enumerate((w3_w, w1_w)):
-                    col = 512 + K * n + P * kb
-                    nc.tensor.matmul_mx(
-                        out=dx_bank[kb][:],
-                        lhsT=w[:, h, 2 * P * kb : 2 * P * (kb + 1)].bitcast(E2M1),
-                        lhsT_scale=scale_rows[:, h, col : col + P],
-                        rhs=words[:, C * n : C * (n + 1)].bitcast(E5M2),
-                        rhs_scale=scales[:, C * n : C * (n + 1)],
-                        start=(g == 0 and n == 0),
-                        stop=(g == NG - 1 and n == 1),
-                    )
+                col = 512 + K * n + P * kb
+                nc.tensor.matmul_mx(
+                    out=dx_bank[kb][:],
+                    lhsT=(w3_w, w1_w)[n][:, h, 2 * P * kb : 2 * P * (kb + 1)].bitcast(E2M1),
+                    lhsT_scale=scale_rows[:, h, col : col + P],
+                    rhs=words.bitcast(E5M2),
+                    rhs_scale=scales,
+                    start=opens,
+                    stop=closes,
+                )
 
         def copy_dx(e):
             for kb in range(KB):
                 if e == 0:
-                    dx.append(placed([P, S], F32, f"dx{kb}", DX_LAST if kb else a_place(1, 0)))
+                    dx.append(placed([P, S], F32, f"dx{kb}", a_place(1, 0) if kb else PLANES))
                 if e == E - 1 and kb == 1:
                     nc.vector.tensor_copy(dx[kb][:, C * e : C * (e + 1)], dx_bank[kb][:])
                 else:
@@ -242,94 +226,125 @@ def tile_moe_bdx_glu_relu_kernel(
         make_identity(nc, ident[:])
         nc.sync.dma_start(offs_sb[:], offs)
         load_saved(1, 0, 0, EARLY)
-        load_dy(0)
         load_scales()
-        nc.sync.dma_start(gate_col[:], gate[0:1, :].rearrange("o (e p i) -> p (o e) i", e=E, i=X4))
+        load_dy(0)
         load_dy(1)
         load_dy(2)
-        load_w2(0)
+        nc.sync.dma_start(gate_col[:], gate[0:1, :].rearrange("o (e p i) -> p (o e) i", e=E, i=X4))
         load_dy(3)
+        load_w2(0)
         load_saved(1, 0, EARLY, CHUNK)
-        load_saved(3, 0, 0, CHUNK)
         load_saved(1, 0, CHUNK, C)
-        load_saved(3, 0, CHUNK, C)
         load_saved(1, 1)
-        load_saved(3, 1)
+        load_saved(3, 0)
         load_w2(1)
-        load_w13(0, 2 * NG)
+        load_saved(1, 2)
+        load_w13(0, NG)
+        for h in range(1, HALVES):
+            load_saved(3, h)
+            if h in (1, 3):
+                load_w2(h // 2 + 2)
+            if h == 2:
+                load_w13(NG, E * NG)
+            if h + 2 < HALVES:
+                load_saved(1, h + 2)
+        nc.sync.dma_start(pos1_sb[:], pos1)
+        nc.sync.dma_start(pos2_sb[:], pos2)
 
         relu_a1(0, 0, EARLY)
-        spread_gate(0)
+        spread_gate(0, "gate_bank")
+        spread_gate(1, "dx_bank0")
         deal_scales()
         for t in range(X4 - 1):
             gather(0, t)
             gather(1, t, on_vector=True)
             gather(2, t)
+            gather(3, t, on_vector=True)
         sort_words(0, nc.vector.tensor_copy)
         gather(0, X4 - 1)
         gather(1, X4 - 1, on_vector=True)
         for k in range(2):
-            gate_block(2 * k)
-            gate_block(2 * k + 1)
-            quantise_g(k)
+            g_woven[k] = placed([P, X4 * CHUNK], BF16, f"g_woven{k}", DA + 4 + 2 * k)
+            gate_chunk(nc.vector, k, gate_bank[0], g_woven[k][:])
+            words, scales = held_codes(f"g{k}", CHUNK)
+            quantise(g_woven[k][:], words[:], scales[:])
+            g_codes[k] = (words, scales)
         relu_a1(0, EARLY, CHUNK)
-        relu_a1(0, CHUNK, C)
         gather(2, X4 - 1)
+        nc.scalar.copy(gates_sb[:], gate_bank[1][:])
+        relu_a1(0, CHUNK, C)
+        gather(3, X4 - 1)
         for n in range(SB):
             first_product(n)
-        mask_dh(0)
-        mask_dh(1)
-        for h in range(2, HALVES):
-            load_saved(1, h)
-            load_saved(3, h)
-            if h in (2, 4):
-                load_w2(h // 2 + 1)
-            if h == 3:
-                load_w13(2 * NG, E * NG)
-        nc.sync.dma_start(pos1_sb[:], pos1)
-        nc.sync.dma_start(pos2_sb[:], pos2)
+        woven_e1 = placed([P, 2, X4 * CHUNK], BF16, "woven_e1", DA + 4)
+        for r in range(2):
+            gate_chunk(nc.gpsimd, 2 + r, gates_sb, woven_e1[:, r, :])
 
         for h in range(HALVES):
             e, g = divmod(h, NG)
             k, n = h + 2, SB * h
             more = h + 1 < HALVES
-            if k < CHUNKS and g == 0:
-                spread_gate(e + 1)
             if more:
                 relu_a1(h + 1)
-            if k + 1 < CHUNKS:
+            if g == 1 and e + 1 < E:
+                sort_words(e + 1, nc.scalar.copy)
+            if h >= 1 and k + 1 < CHUNKS:
                 for t in range(X4):
                     gather(k + 1, t)
-            if g == 0 and e + 1 < E:
-                sort_words(e + 1, nc.scalar.copy)
-            da[h] = placed([P, 2, X4 * C], BF16, f"da{h}", DA)
-            make_da1(nc.gpsimd, h, 0, CHUNK)
-            make_da3(n)
-            mask_dh(n + 2)
-            mask_dh(n + 3)
-            if GPSIMD_SLOTS[h] > CHUNK:
-                make_da1(nc.gpsimd, h, CHUNK, GPSIMD_SLOTS[h])
-            if more:
-                first_product(n + SB)
-                first_product(n + SB + 1)
-            for s in range(1, SB):
-                make_da3(n + s)
-                if k < CHUNKS and s > 1:
-                    gate_block(2 * k + s - 2)
-            if more:
-                mask_dh(n + SB)
-                mask_dh(n + SB + 1)
-            if k < CHUNKS:
-                quantise_g(k)
-            if GPSIMD_SLOTS[h] < C:
-                make_da1(nc.vector, h, GPSIMD_SLOTS[h], C)
+            if g == 0 and 4 <= k < CHUNKS:
+                spread_gate(e + 1, "gate_bank")
+            dhm[h] = placed([P, X4, C], F32, f"dhm{h}", MASKED + 8 * (h % 2))
+            da[h] = placed([P, 2 if h else 1, X4 * C], BF16, f"da{h}", DA)
+            if h:
+                make_da1(nc.gpsimd, h - 1, da[h][:, 1, :])
+            for pair in range(2):
+                m = n + 2 * pair
+                mask_dh(m + 1)
+                make_da3(m + 1)
+                make_da3(m)
+                mask_dh(m)
+                if more and pair == 0:
+                    first_product(n + SB)
+                    first_product(n + SB + 1)
+                if pair == 0 and 4 <= k < CHUNKS:
+                    g_woven[k] = placed([P, X4 * CHUNK], BF16, f"g_woven{k}", WOVEN)
+                    gate_chunk(nc.vector, k, gate_bank[k // 2], g_woven[k][:])
+            if h == 0:
+                words, scales = held_codes("da0", C)
+                quantise(da[0][:, 0, :], words[:], scales[:])
+                da3_codes[0] = (words[:], scales[:])
+                words, scales = held_codes("g23", C)
+                quantise(woven_e1[:].rearrange("p r j -> p (r j)"), words[:], scales[:])
+                for r in range(2):
+                    g_codes[2 + r] = (words[:, CHUNK * r : CHUNK * (r + 1)], scales[:, CHUNK * r : CHUNK * (r + 1)])
+            else:
+                if 4 <= k < CHUNKS:
+                    words, scales = placed_codes(f"g{k}", CHUNK, a_place(3, h - 1) + 5)
+                    quantise(g_woven[k][:], words[:], scales[:])
+                    g_codes[k] = (words, scales)
+                words, scales = placed_codes(f"da{h}", 2 * C, a_place(3, h - 1))
+                quantise(da[h][:].rearrange("p w j -> p (w j)"), words[:], scales[:])
+                da3_codes[h] = (words[:, :C], scales[:, :C])
+                da1_codes[h - 1] = (words[:, C:], scales[:, C:])
             if more:
                 first_product(n + SB + 2)
                 first_product(n + SB + 3)
-            quantise_da(h)
-            second_product(h)
-            if g == 1:
-                copy_dx(e)
+            if g == 0:
+                if h:
+                    second_pass(1, h - 1, da1_codes[h - 1])
+                    copy_dx(e - 1)
+            else:
+                second_pass(0, h - 1, da3_codes[h - 1])
+                second_pass(1, h - 1, da1_codes[h - 1])
+                second_pass(0, h, da3_codes[h])
+
+        last = HALVES - 1
+        da1_last = placed([P, X4 * C], BF16, "da1_last", a_place(1, 4))
+        make_da1(nc.vector, last, da1_last[:])
+        words, scales = placed_codes("da1_last", C, a_place(1, 5))
+        quantise(da1_last[:], words[:], scales[:])
+        second_pass(1, last, (words[:], scales[:]))
+        copy_dx(E - 1)
 
         HT = T // 2
         firsts = [placed([P, T], F32, f"first{kb}", DY + 4 * kb) for kb in range(KB)]

@@ -13,6 +13,7 @@ KB = K // P
 HALVES = E * NG
 CHUNK = 2 * P
 CHUNKS = S // CHUNK
+MASK_LAST_FROM = 5
 EARLY = 32
 
 F32 = mybir.dt.float32
@@ -67,17 +68,20 @@ def tile_moe_bdx_glu_relu_kernel(
         w2_sc_raw = held.tile([P, 512], U8, name="w2_sc_raw")
         spread = held.tile([P, 512 + 2 * K], U8, name="spread")
         scale_rows = held.tile([P, HALVES, 512 + 2 * K], U8, name="scale_rows", align_bytes=64)
+        first_raw = held.tile([P, H], U8, name="first_raw")
+        first_rows = held.tile([P, NG, 512], U8, name="first_rows", align_bytes=64)
         w1_w = held.tile([P, E * NG, 2 * K], U8, name="w1_w", align_bytes=64)
         w3_w = held.tile([P, E * NG, 2 * K], U8, name="w3_w", align_bytes=64)
         ident = held.tile([P, P], F32, name="ident")
         gate_col = held.tile([P, E, X4], F32, name="gate_col")
-        gates_sb = held.tile([P, C], F32, name="gates_sb")
+        gates_sb = held.tile([P, CHUNK], F32, name="gates_sb")
+        nc.vector.memset(first_raw[:].bitcast(I32), 0)
         nc.vector.memset(scale_rows[:].rearrange("p h i -> p (h i)").bitcast(I32), 0)
 
         dy, dx = [], []
         w2_raw, w2_w, saved, gate_bank = {}, {}, {}, {}
         g_planes, g_woven, g_codes = {}, {}, {}
-        dh, dhm, da, da3_codes, da1_codes, dx_bank = {}, {}, {}, {}, {}, {}
+        dh, dhm, step, da, da3_codes, da1_codes, dx_bank = {}, {}, {}, {}, {}, {}, {}
 
         def load_dy(t):
             dy.append(placed([P, T], F32, f"dy{t}", DY + 4 * t))
@@ -107,18 +111,24 @@ def tile_moe_bdx_glu_relu_kernel(
                 by_pass = words.bitcast(I32).rearrange("e s p k -> p (e s) k")
                 nc.sync.dma_start(w[:, lo:hi].bitcast(I32), by_pass[:, lo:hi])
 
-        def sort_words(e, engine_copy):
-            w2_w[e] = held.tile([P, 2 * H], U8, name=f"w2_w{e}", align_bytes=64)
-            engine_copy(
-                w2_w[e][:].bitcast(U16).rearrange("p (g t m) -> p g t m", g=NG, t=X4),
-                w2_raw[e][:].bitcast(U16).rearrange("p (g m t) -> p g t m", g=NG, t=X4),
+        def sort_words(h):
+            e, g = divmod(h, NG)
+            w2_w[h] = held.tile([P, H], U8, name=f"w2_w{h}", align_bytes=64)
+            nc.scalar.copy(
+                w2_w[h][:].bitcast(U16).rearrange("p (t m) -> p t m", t=X4),
+                w2_raw[e][:, H * g : H * (g + 1)].bitcast(U16).rearrange("p (m t) -> p t m", t=X4),
             )
 
+        def sort_scales(into, raw):
+            nc.vector.tensor_copy(into.rearrange("p (t m) -> p t m", t=X4), raw.rearrange("p (m t) -> p t m", t=X4))
+
+        def load_first_scales():
+            rows = w2_scales.bitcast(I32)[0, 0]
+            for q in range(4):
+                nc.sync.dma_start(first_raw[32 * q : 32 * q + 4, :].bitcast(I32), rows[4 * q : 4 * q + 4, :])
+
         def deal_scales():
-            nc.vector.tensor_copy(
-                spread[:, 0:512].rearrange("p (t m) -> p t m", t=X4),
-                w2_sc_raw[:].rearrange("p (m t) -> p t m", t=X4),
-            )
+            sort_scales(spread[:, 0:512], w2_sc_raw[:])
             for q in range(4):
                 rows = scale_rows[32 * q : 32 * q + 4].rearrange("p h i -> p (h i)")
                 nc.gpsimd.dma_start(rows.bitcast(I32), spread[32 * q : 32 * (q + 1), :].bitcast(I32))
@@ -138,11 +148,14 @@ def tile_moe_bdx_glu_relu_kernel(
             else:
                 nc.scalar.activation(g_planes[k][:, t, :], picked, ACT.Copy)
 
-        def gate_chunk(engine, k, gates, into):
-            r = k % 2
-            by_slot = gates[:, CHUNK * r : CHUNK * (r + 1)].rearrange("p (c i) -> p c i", i=4).unsqueeze(2)
+        def gate_chunk(engine, k, gates, lo=0, hi=CHUNK):
+            start = CHUNK * (k % 2)
+            by_slot = gates[:, start + lo : start + hi].rearrange("p (c i) -> p c i", i=4).unsqueeze(2)
             engine.tensor_tensor(
-                woven(into), by_lines(g_planes[k][:]), by_slot.to_broadcast([P, CHUNK // 4, X4, 4]), ALU.mult
+                woven(g_woven[k][:, X4 * lo : X4 * hi]),
+                by_lines(g_planes[k][:, :, lo:hi]),
+                by_slot.to_broadcast([P, (hi - lo) // 4, X4, 4]),
+                ALU.mult,
             )
 
         def quantise(values, words, scales):
@@ -165,11 +178,10 @@ def tile_moe_bdx_glu_relu_kernel(
             words, scales = g_codes[k]
             dh[n] = dh_banks.tile([P, X4, P], F32, name="dh_bank")
             for t in range(X4):
-                col = 512 * g + P * t
                 nc.tensor.matmul_mx(
                     out=dh[n][:, t, :],
-                    lhsT=w2_w[e][:, 2 * col : 2 * (col + P)].bitcast(E2M1),
-                    lhsT_scale=scale_rows[:, h, P * t : P * (t + 1)],
+                    lhsT=w2_w[h][:, 2 * P * t : 2 * P * (t + 1)].bitcast(E2M1),
+                    lhsT_scale=(first_rows if e == 0 else scale_rows)[:, h, P * t : P * (t + 1)],
                     rhs=words[:, P * r : P * (r + 1)].bitcast(E5M2),
                     rhs_scale=scales[:, P * r : P * (r + 1)],
                     start=True,
@@ -179,12 +191,20 @@ def tile_moe_bdx_glu_relu_kernel(
         def relu_a1(h, lo=0, hi=C):
             nc.scalar.activation(saved[1, h][:, :, lo:hi], saved[1, h][:, :, lo:hi], ACT.Relu)
 
-        def mask_dh(n):
+        def step_a1(h):
+            step[h] = placed([P, X4 * C], BF16, f"step{h}", a_place(1, h - 4) + 4)
+            nc.scalar.activation(woven(step[h][:]), by_lines(saved[1, h][:]), ACT.Sign)
+
+        def start_da1(n):
             h, s = divmod(n, SB)
             slots = slice(P * s, P * (s + 1))
-            nc.vector.scalar_tensor_tensor(
-                dhm[h][:, :, slots], saved[1, h][:, :, slots], 0.0, dh[n][:], ALU.is_gt, ALU.mult
-            )
+            if h < MASK_LAST_FROM:
+                nc.vector.scalar_tensor_tensor(
+                    dhm[h][:, :, slots], saved[1, h][:, :, slots], 0.0, dh[n][:], ALU.is_gt, ALU.mult
+                )
+            else:
+                run = dhm[h][:, X4 * P * s : X4 * P * (s + 1)]
+                nc.vector.tensor_tensor(woven(run), by_lines(dh[n][:]), by_lines(saved[3, h][:, :, slots]), ALU.mult)
 
         def make_da3(n):
             h, s = divmod(n, SB)
@@ -194,7 +214,10 @@ def tile_moe_bdx_glu_relu_kernel(
             )
 
         def make_da1(engine, h, into):
-            engine.tensor_tensor(woven(into), by_lines(dhm[h][:]), by_lines(saved[3, h][:]), ALU.mult)
+            if h < MASK_LAST_FROM:
+                engine.tensor_tensor(woven(into), by_lines(dhm[h][:]), by_lines(saved[3, h][:]), ALU.mult)
+            else:
+                engine.tensor_tensor(into, dhm[h][:], step[h][:], ALU.mult)
 
         def second_pass(n, h, codes):
             e, g = divmod(h, NG)
@@ -229,6 +252,7 @@ def tile_moe_bdx_glu_relu_kernel(
         load_scales()
         load_dy(0)
         load_dy(1)
+        load_first_scales()
         load_dy(2)
         nc.sync.dma_start(gate_col[:], gate[0:1, :].rearrange("o (e p i) -> p (o e) i", e=E, i=X4))
         load_dy(3)
@@ -259,66 +283,73 @@ def tile_moe_bdx_glu_relu_kernel(
             gather(0, t)
             gather(1, t, on_vector=True)
             gather(2, t)
-            gather(3, t, on_vector=True)
-        sort_words(0, nc.vector.tensor_copy)
+            if t:
+                sort_scales(first_rows[:, t - 1], first_raw[:, 512 * (t - 1) : 512 * t])
         gather(0, X4 - 1)
         gather(1, X4 - 1, on_vector=True)
+        sort_words(0)
         for k in range(2):
             g_woven[k] = placed([P, X4 * CHUNK], BF16, f"g_woven{k}", DA + 4 + 2 * k)
-            gate_chunk(nc.vector, k, gate_bank[0], g_woven[k][:])
-            words, scales = held_codes(f"g{k}", CHUNK)
-            quantise(g_woven[k][:], words[:], scales[:])
-            g_codes[k] = (words, scales)
+            g_codes[k] = held_codes(f"g{k}", CHUNK)
+        gate_chunk(nc.vector, 0, gate_bank[0])
+        gate_chunk(nc.vector, 1, gate_bank[0], 0, P)
+        quantise(g_woven[0][:], g_codes[0][0][:], g_codes[0][1][:])
+        gate_chunk(nc.vector, 1, gate_bank[0], P, CHUNK)
+        quantise(g_woven[1][:], g_codes[1][0][:], g_codes[1][1][:])
         relu_a1(0, EARLY, CHUNK)
         gather(2, X4 - 1)
-        nc.scalar.copy(gates_sb[:], gate_bank[1][:])
+        nc.scalar.copy(gates_sb[:], gate_bank[1][:, :CHUNK])
         relu_a1(0, CHUNK, C)
-        gather(3, X4 - 1)
+        sort_words(1)
         for n in range(SB):
             first_product(n)
-        woven_e1 = placed([P, 2, X4 * CHUNK], BF16, "woven_e1", DA + 4)
-        for r in range(2):
-            gate_chunk(nc.gpsimd, 2 + r, gates_sb, woven_e1[:, r, :])
+        g_woven[2] = placed([P, X4 * CHUNK], BF16, "g_woven2", DA + 5)
+        gate_chunk(nc.gpsimd, 2, gates_sb)
 
         for h in range(HALVES):
             e, g = divmod(h, NG)
             k, n = h + 2, SB * h
             more = h + 1 < HALVES
+            gated = 3 <= k < CHUNKS
             if more:
                 relu_a1(h + 1)
-            if g == 1 and e + 1 < E:
-                sort_words(e + 1, nc.scalar.copy)
-            if h >= 1 and k + 1 < CHUNKS:
+            if k + 1 < CHUNKS:
                 for t in range(X4):
                     gather(k + 1, t)
+            if h + 2 < HALVES:
+                sort_words(h + 2)
             if g == 0 and 4 <= k < CHUNKS:
                 spread_gate(e + 1, "gate_bank")
-            dhm[h] = placed([P, X4, C], F32, f"dhm{h}", MASKED + 8 * (h % 2))
+            if h < MASK_LAST_FROM:
+                dhm[h] = placed([P, X4, C], F32, f"dhm{h}", MASKED + 8 * (h % 2))
+            else:
+                dhm[h] = placed([P, X4 * C], BF16, f"dhm{h}", MASKED + 8 * (h % 2))
+                step_a1(h)
             da[h] = placed([P, 2 if h else 1, X4 * C], BF16, f"da{h}", DA)
             if h:
                 make_da1(nc.gpsimd, h - 1, da[h][:, 1, :])
             for pair in range(2):
                 m = n + 2 * pair
-                mask_dh(m + 1)
-                make_da3(m + 1)
-                make_da3(m)
-                mask_dh(m)
+                first, second = (m + 1, m) if m else (m, m + 1)
+                start_da1(first)
+                make_da3(first)
+                make_da3(second)
+                start_da1(second)
                 if more and pair == 0:
                     first_product(n + SB)
                     first_product(n + SB + 1)
-                if pair == 0 and 4 <= k < CHUNKS:
-                    g_woven[k] = placed([P, X4 * CHUNK], BF16, f"g_woven{k}", WOVEN)
-                    gate_chunk(nc.vector, k, gate_bank[k // 2], g_woven[k][:])
+                if pair == 0 and gated:
+                    place = WOVEN if k > 3 else a_place(1, 0) + 4
+                    g_woven[k] = placed([P, X4 * CHUNK], BF16, f"g_woven{k}", place)
+                    gate_chunk(nc.vector, k, gate_bank[k // 2])
             if h == 0:
                 words, scales = held_codes("da0", C)
                 quantise(da[0][:, 0, :], words[:], scales[:])
                 da3_codes[0] = (words[:], scales[:])
-                words, scales = held_codes("g23", C)
-                quantise(woven_e1[:].rearrange("p r j -> p (r j)"), words[:], scales[:])
-                for r in range(2):
-                    g_codes[2 + r] = (words[:, CHUNK * r : CHUNK * (r + 1)], scales[:, CHUNK * r : CHUNK * (r + 1)])
+                g_codes[2] = held_codes("g2", CHUNK)
+                quantise(g_woven[2][:], g_codes[2][0][:], g_codes[2][1][:])
             else:
-                if 4 <= k < CHUNKS:
+                if gated:
                     words, scales = placed_codes(f"g{k}", CHUNK, a_place(3, h - 1) + 5)
                     quantise(g_woven[k][:], words[:], scales[:])
                     g_codes[k] = (words, scales)

@@ -14,6 +14,7 @@ HALVES = E * NG
 CHUNK = 2 * P
 CHUNKS = S // CHUNK
 MASK_LAST_FROM = 5
+DIRECT = HALVES // 2
 EARLY = 32
 
 F32 = mybir.dt.float32
@@ -66,17 +67,18 @@ def tile_moe_bdx_glu_relu_kernel(
         pos1_sb = held.tile([P, T // 16], U16, name="pos1_sb")
         pos2_sb = held.tile([P, T // 16], U16, name="pos2_sb")
         w2_sc_raw = held.tile([P, 512], U8, name="w2_sc_raw")
-        spread = held.tile([P, 512 + 2 * K], U8, name="spread")
-        scale_rows = held.tile([P, HALVES, 512 + 2 * K], U8, name="scale_rows", align_bytes=64)
-        first_raw = held.tile([P, H], U8, name="first_raw")
-        first_rows = held.tile([P, NG, 512], U8, name="first_rows", align_bytes=64)
+        spread = held.tile([P, 3, 512], U8, name="spread")
+        scale_rows = held.tile([P, E, 3, 512], U8, name="scale_rows", align_bytes=64)
+        first_raw = held.tile([P, DIRECT, 512], U8, name="first_raw")
+        first_rows = held.tile([P, DIRECT, 512], U8, name="first_rows", align_bytes=64)
         w1_w = held.tile([P, E * NG, 2 * K], U8, name="w1_w", align_bytes=64)
         w3_w = held.tile([P, E * NG, 2 * K], U8, name="w3_w", align_bytes=64)
         ident = held.tile([P, P], F32, name="ident")
         gate_col = held.tile([P, E, X4], F32, name="gate_col")
         gates_sb = held.tile([P, CHUNK], F32, name="gates_sb")
-        nc.vector.memset(first_raw[:].bitcast(I32), 0)
-        nc.vector.memset(scale_rows[:].rearrange("p h i -> p (h i)").bitcast(I32), 0)
+        nc.vector.memset(first_raw[:].rearrange("p h i -> p (h i)").bitcast(I32), 0)
+        nc.vector.memset(w2_sc_raw[P // 2 :, :].bitcast(I32), 0)
+        nc.vector.memset(scale_rows[:].rearrange("p j w i -> p (j w i)").bitcast(I32), 0)
 
         dy, dx = [], []
         w2_raw, w2_w, saved, gate_bank = {}, {}, {}, {}
@@ -94,9 +96,9 @@ def tile_moe_bdx_glu_relu_kernel(
         def load_scales():
             by_half = w2_scales.bitcast(I32).rearrange("e s f (g i) -> g f (e s) i", g=NG)
             for g in range(NG):
-                nc.sync.dma_start(w2_sc_raw[g:P:NG, :].bitcast(I32), by_half[g])
+                nc.sync.dma_start(w2_sc_raw[g : P // 2 : NG, :].bitcast(I32), by_half[g][:, DIRECT // NG :])
             for n, scales in enumerate((w3_scales, w1_scales)):
-                into = spread[:, 512 + K * n : 512 + K * (n + 1)]
+                into = spread[: P // 2, 1 + n].rearrange("p (s i) -> p s i", s=NG)
                 nc.sync.dma_start(into.bitcast(I32), scales.bitcast(I32).rearrange("e s f i -> f (e s) i"))
 
         def load_saved(which, h, lo=0, hi=C):
@@ -119,19 +121,21 @@ def tile_moe_bdx_glu_relu_kernel(
                 w2_raw[e][:, H * g : H * (g + 1)].bitcast(U16).rearrange("p (m t) -> p t m", t=X4),
             )
 
-        def sort_scales(into, raw):
-            nc.vector.tensor_copy(into.rearrange("p (t m) -> p t m", t=X4), raw.rearrange("p (m t) -> p t m", t=X4))
+        def sort_scales(engine, into, raw):
+            engine.tensor_copy(into.rearrange("p (t m) -> p t m", t=X4), raw.rearrange("p (m t) -> p t m", t=X4))
 
         def load_first_scales():
-            rows = w2_scales.bitcast(I32)[0, 0]
+            rows = w2_scales.bitcast(I32).rearrange("e s f i -> f (e s) i")
             for q in range(4):
-                nc.sync.dma_start(first_raw[32 * q : 32 * q + 4, :].bitcast(I32), rows[4 * q : 4 * q + 4, :])
+                into = first_raw[32 * q : 32 * q + 4].rearrange("p (e g) i -> p e (g i)", g=NG)
+                nc.sync.dma_start(into.bitcast(I32), rows[4 * q : 4 * q + 4, : DIRECT // NG])
 
         def deal_scales():
-            sort_scales(spread[:, 0:512], w2_sc_raw[:])
+            sort_scales(nc.vector, spread[:, 0], w2_sc_raw[:])
             for q in range(4):
-                rows = scale_rows[32 * q : 32 * q + 4].rearrange("p h i -> p (h i)")
-                nc.gpsimd.dma_start(rows.bitcast(I32), spread[32 * q : 32 * (q + 1), :].bitcast(I32))
+                rows = scale_rows[32 * q : 32 * q + 4].rearrange("p j w i -> p (j w i)")
+                dealt = spread[16 * q : 16 * (q + 1)].rearrange("p w i -> p (w i)")
+                nc.gpsimd.dma_start(rows.bitcast(I32), dealt.bitcast(I32))
 
         def spread_gate(e, bank_name):
             gate_bank[e] = dx_banks.tile([P, C], F32, name=bank_name)
@@ -176,12 +180,13 @@ def tile_moe_bdx_glu_relu_kernel(
             e, g = divmod(h, NG)
             k, r = divmod(SB * e + s, 2)
             words, scales = g_codes[k]
+            w2_rows = first_rows[:, h] if h < DIRECT else scale_rows[:, h - DIRECT, 0]
             dh[n] = dh_banks.tile([P, X4, P], F32, name="dh_bank")
             for t in range(X4):
                 nc.tensor.matmul_mx(
                     out=dh[n][:, t, :],
                     lhsT=w2_w[h][:, 2 * P * t : 2 * P * (t + 1)].bitcast(E2M1),
-                    lhsT_scale=(first_rows if e == 0 else scale_rows)[:, h, P * t : P * (t + 1)],
+                    lhsT_scale=w2_rows[:, P * t : P * (t + 1)],
                     rhs=words[:, P * r : P * (r + 1)].bitcast(E5M2),
                     rhs_scale=scales[:, P * r : P * (r + 1)],
                     start=True,
@@ -226,11 +231,11 @@ def tile_moe_bdx_glu_relu_kernel(
             for kb in range(KB):
                 if opens:
                     dx_bank[kb] = dx_banks.tile([P, C], F32, name=f"dx_bank{kb}")
-                col = 512 + K * n + P * kb
+                col = K * g + P * kb
                 nc.tensor.matmul_mx(
                     out=dx_bank[kb][:],
                     lhsT=(w3_w, w1_w)[n][:, h, 2 * P * kb : 2 * P * (kb + 1)].bitcast(E2M1),
-                    lhsT_scale=scale_rows[:, h, col : col + P],
+                    lhsT_scale=scale_rows[:, e, 1 + n, col : col + P],
                     rhs=words.bitcast(E5M2),
                     rhs_scale=scales,
                     start=opens,
@@ -264,14 +269,18 @@ def tile_moe_bdx_glu_relu_kernel(
         load_w2(1)
         load_saved(1, 2)
         load_w13(0, NG)
-        for h in range(1, HALVES):
+        for h in range(1, MASK_LAST_FROM):
             load_saved(3, h)
             if h in (1, 3):
                 load_w2(h // 2 + 2)
             if h == 2:
                 load_w13(NG, E * NG)
-            if h + 2 < HALVES:
+            if h + 2 <= MASK_LAST_FROM:
                 load_saved(1, h + 2)
+        for h in range(MASK_LAST_FROM, HALVES):
+            if h > MASK_LAST_FROM:
+                load_saved(1, h)
+            load_saved(3, h)
         nc.sync.dma_start(pos1_sb[:], pos1)
         nc.sync.dma_start(pos2_sb[:], pos2)
 
@@ -284,7 +293,9 @@ def tile_moe_bdx_glu_relu_kernel(
             gather(1, t, on_vector=True)
             gather(2, t)
             if t:
-                sort_scales(first_rows[:, t - 1], first_raw[:, 512 * (t - 1) : 512 * t])
+                sort_scales(nc.vector, first_rows[:, t - 1], first_raw[:, t - 1])
+        for h in range(NG, DIRECT):
+            sort_scales(nc.gpsimd, first_rows[:, h], first_raw[:, h])
         gather(0, X4 - 1)
         gather(1, X4 - 1, on_vector=True)
         sort_words(0)
@@ -318,13 +329,14 @@ def tile_moe_bdx_glu_relu_kernel(
                     gather(k + 1, t)
             if h + 2 < HALVES:
                 sort_words(h + 2)
+            if MASK_LAST_FROM <= h + 1 < HALVES:
+                step_a1(h + 1)
             if g == 0 and 4 <= k < CHUNKS:
                 spread_gate(e + 1, "gate_bank")
             if h < MASK_LAST_FROM:
                 dhm[h] = placed([P, X4, C], F32, f"dhm{h}", MASKED + 8 * (h % 2))
             else:
                 dhm[h] = placed([P, X4 * C], BF16, f"dhm{h}", MASKED + 8 * (h % 2))
-                step_a1(h)
             da[h] = placed([P, 2 if h else 1, X4 * C], BF16, f"da{h}", DA)
             if h:
                 make_da1(nc.gpsimd, h - 1, da[h][:, 1, :])

@@ -15,6 +15,7 @@ CHUNK = 2 * P
 CHUNKS = S // CHUNK
 MASK_LAST_FROM = 5
 DIRECT = HALVES // 2
+PIECE = 256
 EARLY = 32
 
 F32 = mybir.dt.float32
@@ -344,16 +345,16 @@ def tile_moe_bdx_glu_relu_kernel(
                 m = n + 2 * pair
                 first, second = (m + 1, m) if m else (m, m + 1)
                 start_da1(first)
+                if pair == 1 and gated:
+                    place = WOVEN if k > 3 else a_place(1, 0) + 4
+                    g_woven[k] = placed([P, X4 * CHUNK], BF16, f"g_woven{k}", place)
+                    gate_chunk(nc.vector, k, gate_bank[k // 2])
                 make_da3(first)
                 make_da3(second)
                 start_da1(second)
                 if more and pair == 0:
                     first_product(n + SB)
                     first_product(n + SB + 1)
-                if pair == 0 and gated:
-                    place = WOVEN if k > 3 else a_place(1, 0) + 4
-                    g_woven[k] = placed([P, X4 * CHUNK], BF16, f"g_woven{k}", place)
-                    gate_chunk(nc.vector, k, gate_bank[k // 2])
             if h == 0:
                 words, scales = held_codes("da0", C)
                 quantise(da[0][:, 0, :], words[:], scales[:])
@@ -361,14 +362,13 @@ def tile_moe_bdx_glu_relu_kernel(
                 g_codes[2] = held_codes("g2", CHUNK)
                 quantise(g_woven[2][:], g_codes[2][0][:], g_codes[2][1][:])
             else:
-                if gated:
-                    words, scales = placed_codes(f"g{k}", CHUNK, a_place(3, h - 1) + 5)
-                    quantise(g_woven[k][:], words[:], scales[:])
-                    g_codes[k] = (words, scales)
                 words, scales = placed_codes(f"da{h}", 2 * C, a_place(3, h - 1))
                 quantise(da[h][:].rearrange("p w j -> p (w j)"), words[:], scales[:])
                 da3_codes[h] = (words[:, :C], scales[:, :C])
                 da1_codes[h - 1] = (words[:, C:], scales[:, C:])
+                if gated:
+                    g_codes[k] = placed_codes(f"g{k}", CHUNK, a_place(3, h - 1) + 5)
+                    quantise(g_woven[k][:], g_codes[k][0][:], g_codes[k][1][:])
             if more:
                 first_product(n + SB + 2)
                 first_product(n + SB + 3)
@@ -389,20 +389,19 @@ def tile_moe_bdx_glu_relu_kernel(
         second_pass(1, last, (words[:], scales[:]))
         copy_dx(E - 1)
 
-        HT = T // 2
         firsts = [placed([P, T], F32, f"first{kb}", DY + 4 * kb) for kb in range(KB)]
-        seconds = [placed([P, T], F32, f"second{kb}", DY + 8 + 4 * kb) for kb in range(KB)]
-        totals = [placed([P, T], F32, f"total{kb}", a_place(1, 2 + kb)) for kb in range(KB)]
+        totals = [placed([P, T], F32, f"total{kb}", DY + 8 + 4 * kb) for kb in range(KB)]
+        second = placed([P, PIECE], F32, "second", a_place(1, 2))
 
-        def add_and_store(kb, lo, hi):
-            nc.vector.tensor_tensor(totals[kb][:, lo:hi], firsts[kb][:, lo:hi], seconds[kb][:, lo:hi], ALU.add)
+        def entries(pos_sb, lo):
+            return pos_sb[:, lo // 16 : (lo + PIECE) // 16]
+
+        pieces = [(kb, lo) for kb in range(KB) for lo in range(0, T, PIECE)]
+        nc.vector.tensor_copy(second[:], dx[1][:].indirect(entries(pos2_sb, T - PIECE)))
+        for kb, lo in pieces:
+            nc.scalar.activation(firsts[kb][:, lo : lo + PIECE], dx[kb][:].indirect(entries(pos1_sb, lo)), ACT.Copy)
+        for kb, lo in pieces:
+            hi = lo + PIECE
+            other = second[:] if (kb, lo) == pieces[-1] else dx[kb][:].indirect(entries(pos2_sb, lo))
+            nc.vector.tensor_tensor(totals[kb][:, lo:hi], other, firsts[kb][:, lo:hi], ALU.add)
             nc.sync.dma_start(out[P * kb : P * (kb + 1), lo:hi], totals[kb][:, lo:hi])
-
-        for kb in range(KB):
-            nc.scalar.activation(firsts[kb][:], dx[kb][:].indirect(pos1_sb[:]), ACT.Copy)
-        nc.scalar.activation(seconds[1][:, HT:], dx[1][:].indirect(pos2_sb[:, HT // 16 :]), ACT.Copy)
-        nc.vector.tensor_copy(seconds[0][:], dx[0][:].indirect(pos2_sb[:]))
-        add_and_store(0, 0, T)
-        nc.vector.tensor_copy(seconds[1][:, :HT], dx[1][:].indirect(pos2_sb[:, : HT // 16]))
-        add_and_store(1, 0, HT)
-        add_and_store(1, HT, T)

@@ -68,8 +68,9 @@ def tile_moe_bdx_glu_relu_kernel(
         pos1_sb = held.tile([P, T // 16], U16, name="pos1_sb")
         pos2_sb = held.tile([P, T // 16], U16, name="pos2_sb")
         w2_sc_raw = held.tile([P, 512], U8, name="w2_sc_raw")
-        spread = held.tile([P, 3, 512], U8, name="spread")
-        scale_rows = held.tile([P, E, 3, 512], U8, name="scale_rows", align_bytes=64)
+        spread = held.tile([P, 512], U8, name="spread")
+        late_rows = held.tile([P, HALVES - DIRECT, 512], U8, name="late_rows", align_bytes=64)
+        w31_rows = held.tile([P, 2, HALVES, K], U8, name="w31_rows", align_bytes=64)
         first_raw = held.tile([P, DIRECT, 512], U8, name="first_raw")
         first_rows = held.tile([P, DIRECT, 512], U8, name="first_rows", align_bytes=64)
         w1_w = held.tile([P, E * NG, 2 * K], U8, name="w1_w", align_bytes=64)
@@ -77,13 +78,16 @@ def tile_moe_bdx_glu_relu_kernel(
         ident = held.tile([P, P], F32, name="ident")
         gate_col = held.tile([P, E, X4], F32, name="gate_col")
         gates_sb = held.tile([P, CHUNK], F32, name="gates_sb")
-        nc.vector.memset(first_raw[:].rearrange("p h i -> p (h i)").bitcast(I32), 0)
+        nc.gpsimd.memset(first_raw[:].rearrange("p h i -> p (h i)").bitcast(I32), 0)
+        nc.vector.memset(w31_rows[:].rearrange("p w h i -> p (w h i)").bitcast(I32), 0)
         nc.vector.memset(w2_sc_raw[P // 2 :, :].bitcast(I32), 0)
-        nc.vector.memset(scale_rows[:].rearrange("p j w i -> p (j w i)").bitcast(I32), 0)
+        nc.vector.memset(late_rows[:].rearrange("p h i -> p (h i)").bitcast(I32), 0)
+
 
         dy, dx = [], []
         w2_raw, w2_w, saved, gate_bank = {}, {}, {}, {}
         g_planes, g_woven, g_codes = {}, {}, {}
+        kept = {}
         dh, dhm, step, da, da3_codes, da1_codes, dx_bank = {}, {}, {}, {}, {}, {}, {}
 
         def load_dy(t):
@@ -98,9 +102,12 @@ def tile_moe_bdx_glu_relu_kernel(
             by_half = w2_scales.bitcast(I32).rearrange("e s f (g i) -> g f (e s) i", g=NG)
             for g in range(NG):
                 nc.sync.dma_start(w2_sc_raw[g : P // 2 : NG, :].bitcast(I32), by_half[g][:, DIRECT // NG :])
+
+        def load_w31_scales():
             for n, scales in enumerate((w3_scales, w1_scales)):
-                into = spread[: P // 2, 1 + n].rearrange("p (s i) -> p s i", s=NG)
-                nc.sync.dma_start(into.bitcast(I32), scales.bitcast(I32).rearrange("e s f i -> f (e s) i"))
+                rows = scales.bitcast(I32).rearrange("e s f i -> f (e s) i")
+                for q in range(4):
+                    nc.sync.dma_start(w31_rows[32 * q : 32 * q + 4, n].bitcast(I32), rows[4 * q : 4 * q + 4])
 
         def load_saved(which, h, lo=0, hi=C):
             e, g = divmod(h, NG)
@@ -132,11 +139,10 @@ def tile_moe_bdx_glu_relu_kernel(
                 nc.sync.dma_start(into.bitcast(I32), rows[4 * q : 4 * q + 4, : DIRECT // NG])
 
         def deal_scales():
-            sort_scales(nc.vector, spread[:, 0], w2_sc_raw[:])
+            sort_scales(nc.vector, spread[:], w2_sc_raw[:])
             for q in range(4):
-                rows = scale_rows[32 * q : 32 * q + 4].rearrange("p j w i -> p (j w i)")
-                dealt = spread[16 * q : 16 * (q + 1)].rearrange("p w i -> p (w i)")
-                nc.gpsimd.dma_start(rows.bitcast(I32), dealt.bitcast(I32))
+                rows = late_rows[32 * q : 32 * q + 4].rearrange("p h i -> p (h i)")
+                nc.gpsimd.dma_start(rows.bitcast(I32), spread[16 * q : 16 * (q + 1), :].bitcast(I32))
 
         def spread_gate(e, bank_name):
             gate_bank[e] = dx_banks.tile([P, C], F32, name=bank_name)
@@ -145,7 +151,7 @@ def tile_moe_bdx_glu_relu_kernel(
 
         def gather(k, t, on_vector=False):
             if t == 0:
-                place = MASKED + 8 + 4 * k if k < 4 else a_place(1, k - 4)
+                place = MASKED + 8 + 4 * k if k < 4 else a_place(1, k - 2)
                 g_planes[k] = placed([P, X4, CHUNK], F32, f"g_planes{k}", place)
             picked = dy[t][:].indirect(offs_sb[:, CHUNK * k // 16 : CHUNK * (k + 1) // 16])
             if on_vector:
@@ -181,7 +187,7 @@ def tile_moe_bdx_glu_relu_kernel(
             e, g = divmod(h, NG)
             k, r = divmod(SB * e + s, 2)
             words, scales = g_codes[k]
-            w2_rows = first_rows[:, h] if h < DIRECT else scale_rows[:, h - DIRECT, 0]
+            w2_rows = first_rows[:, h] if h < DIRECT else late_rows[:, h - DIRECT]
             dh[n] = dh_banks.tile([P, X4, P], F32, name="dh_bank")
             for t in range(X4):
                 nc.tensor.matmul_mx(
@@ -195,18 +201,22 @@ def tile_moe_bdx_glu_relu_kernel(
                 )
 
         def relu_a1(h, lo=0, hi=C):
-            nc.scalar.activation(saved[1, h][:, :, lo:hi], saved[1, h][:, :, lo:hi], ACT.Relu)
+            if h >= 2:
+                kept[h] = placed([P, X4, C], F32, f"kept{h}", a_place(1, h - 2))
+            else:
+                kept[h] = saved[1, h]
+            nc.scalar.activation(kept[h][:, :, lo:hi], saved[1, h][:, :, lo:hi], ACT.Relu)
 
         def step_a1(h):
             step[h] = placed([P, X4 * C], BF16, f"step{h}", a_place(1, h - 4) + 4)
-            nc.scalar.activation(woven(step[h][:]), by_lines(saved[1, h][:]), ACT.Sign)
+            nc.scalar.activation(woven(step[h][:]), by_lines(kept[h][:]), ACT.Sign)
 
         def start_da1(n):
             h, s = divmod(n, SB)
             slots = slice(P * s, P * (s + 1))
             if h < MASK_LAST_FROM:
                 nc.vector.scalar_tensor_tensor(
-                    dhm[h][:, :, slots], saved[1, h][:, :, slots], 0.0, dh[n][:], ALU.is_gt, ALU.mult
+                    dhm[h][:, :, slots], kept[h][:, :, slots], 0.0, dh[n][:], ALU.is_gt, ALU.mult
                 )
             else:
                 run = dhm[h][:, X4 * P * s : X4 * P * (s + 1)]
@@ -216,7 +226,7 @@ def tile_moe_bdx_glu_relu_kernel(
             h, s = divmod(n, SB)
             run = da[h][:, 0, X4 * P * s : X4 * P * (s + 1)]
             nc.vector.tensor_tensor(
-                woven(run), by_lines(dh[n][:]), by_lines(saved[1, h][:, :, P * s : P * (s + 1)]), ALU.mult
+                woven(run), by_lines(dh[n][:]), by_lines(kept[h][:, :, P * s : P * (s + 1)]), ALU.mult
             )
 
         def make_da1(engine, h, into):
@@ -225,18 +235,17 @@ def tile_moe_bdx_glu_relu_kernel(
             else:
                 engine.tensor_tensor(into, dhm[h][:], step[h][:], ALU.mult)
 
-        def second_pass(n, h, codes):
+        def second_pass(n, h, codes, opens=False):
             e, g = divmod(h, NG)
             words, scales = codes
-            opens, closes = (g == 0 and n == 0), (g == NG - 1 and n == 1)
+            closes = g == NG - 1 and n == 1
             for kb in range(KB):
                 if opens:
                     dx_bank[kb] = dx_banks.tile([P, C], F32, name=f"dx_bank{kb}")
-                col = K * g + P * kb
                 nc.tensor.matmul_mx(
                     out=dx_bank[kb][:],
                     lhsT=(w3_w, w1_w)[n][:, h, 2 * P * kb : 2 * P * (kb + 1)].bitcast(E2M1),
-                    lhsT_scale=scale_rows[:, e, 1 + n, col : col + P],
+                    lhsT_scale=w31_rows[:, n, h, P * kb : P * (kb + 1)],
                     rhs=words.bitcast(E5M2),
                     rhs_scale=scales,
                     start=opens,
@@ -268,6 +277,7 @@ def tile_moe_bdx_glu_relu_kernel(
         load_saved(1, 1)
         load_saved(3, 0)
         load_w2(1)
+        load_w31_scales()
         load_saved(1, 2)
         load_w13(0, NG)
         for h in range(1, MASK_LAST_FROM):
@@ -346,8 +356,7 @@ def tile_moe_bdx_glu_relu_kernel(
                 first, second = (m + 1, m) if m else (m, m + 1)
                 start_da1(first)
                 if pair == 1 and gated:
-                    place = WOVEN if k > 3 else a_place(1, 0) + 4
-                    g_woven[k] = placed([P, X4 * CHUNK], BF16, f"g_woven{k}", place)
+                    g_woven[k] = placed([P, X4 * CHUNK], BF16, f"g_woven{k}", WOVEN)
                     gate_chunk(nc.vector, k, gate_bank[k // 2])
                 make_da3(first)
                 make_da3(second)
@@ -377,8 +386,9 @@ def tile_moe_bdx_glu_relu_kernel(
                     second_pass(1, h - 1, da1_codes[h - 1])
                     copy_dx(e - 1)
             else:
-                second_pass(0, h - 1, da3_codes[h - 1])
-                second_pass(1, h - 1, da1_codes[h - 1])
+                first_half = [(0, da3_codes[h - 1]), (1, da1_codes[h - 1])]
+                for place, (w, codes) in enumerate(first_half if e else first_half[::-1]):
+                    second_pass(w, h - 1, codes, opens=place == 0)
                 second_pass(0, h, da3_codes[h])
 
         last = HALVES - 1

@@ -16,7 +16,6 @@ CHUNKS = S // CHUNK
 MASK_LAST_FROM = 5
 DIRECT = HALVES // 2
 PIECE = 256
-EARLY = 32
 
 F32 = mybir.dt.float32
 BF16 = mybir.dt.bfloat16
@@ -88,7 +87,7 @@ def tile_moe_bdx_glu_relu_kernel(
         w2_raw, w2_w, saved, gate_bank = {}, {}, {}, {}
         g_planes, g_woven, g_codes = {}, {}, {}
         kept = {}
-        dh, dhm, step, da, da3_codes, da1_codes, dx_bank = {}, {}, {}, {}, {}, {}, {}
+        dh, dhm, step, da3, da3_codes, da1_codes, dx_bank = {}, {}, {}, {}, {}, {}, {}
 
         def load_dy(t):
             dy.append(placed([P, T], F32, f"dy{t}", DY + 4 * t))
@@ -109,12 +108,12 @@ def tile_moe_bdx_glu_relu_kernel(
                 for q in range(4):
                     nc.sync.dma_start(w31_rows[32 * q : 32 * q + 4, n].bitcast(I32), rows[4 * q : 4 * q + 4])
 
-        def load_saved(which, h, lo=0, hi=C):
+        def load_saved(which, h, lo=0, hi=C, planes=slice(0, X4)):
             e, g = divmod(h, NG)
-            if lo == 0:
+            if (which, h) not in saved:
                 saved[which, h] = placed([P, X4, C], F32, f"a{which}_{h}", a_place(which, h))
             rows = (a1 if which == 1 else a3)[512 * g : 512 * (g + 1), C * e + lo : C * e + hi]
-            nc.sync.dma_start(saved[which, h][:, :, lo:hi], rows.rearrange("(p t) s -> p t s", t=X4))
+            nc.sync.dma_start(saved[which, h][:, planes, lo:hi], rows.rearrange("(p t) s -> p t s", t=X4)[:, planes])
 
         def load_w13(lo, hi):
             for w, words in ((w3_w, w3_words), (w1_w, w1_words)):
@@ -151,7 +150,7 @@ def tile_moe_bdx_glu_relu_kernel(
 
         def gather(k, t, on_vector=False):
             if t == 0:
-                place = MASKED + 8 + 4 * k if k < 4 else a_place(1, k - 2)
+                place = MASKED + 8 + 4 * k if k < 3 else a_place(1, k - 2)
                 g_planes[k] = placed([P, X4, CHUNK], F32, f"g_planes{k}", place)
             picked = dy[t][:].indirect(offs_sb[:, CHUNK * k // 16 : CHUNK * (k + 1) // 16])
             if on_vector:
@@ -200,12 +199,12 @@ def tile_moe_bdx_glu_relu_kernel(
                     stop=True,
                 )
 
-        def relu_a1(h, lo=0, hi=C):
-            if h >= 2:
-                kept[h] = placed([P, X4, C], F32, f"kept{h}", a_place(1, h - 2))
+        def relu_a1(h, lo=0, hi=C, planes=slice(0, X4)):
+            if h:
+                kept[h] = placed([P, X4, C], F32, f"kept{h}", a_place(1, h - 2) if h > 1 else WOVEN + 2)
             else:
                 kept[h] = saved[1, h]
-            nc.scalar.activation(kept[h][:, :, lo:hi], saved[1, h][:, :, lo:hi], ACT.Relu)
+            nc.scalar.activation(kept[h][:, planes, lo:hi], saved[1, h][:, planes, lo:hi], ACT.Relu)
 
         def step_a1(h):
             step[h] = placed([P, X4 * C], BF16, f"step{h}", a_place(1, h - 4) + 4)
@@ -224,7 +223,7 @@ def tile_moe_bdx_glu_relu_kernel(
 
         def make_da3(n):
             h, s = divmod(n, SB)
-            run = da[h][:, 0, X4 * P * s : X4 * P * (s + 1)]
+            run = da3[h][:, X4 * P * s : X4 * P * (s + 1)]
             nc.vector.tensor_tensor(
                 woven(run), by_lines(dh[n][:]), by_lines(kept[h][:, :, P * s : P * (s + 1)]), ALU.mult
             )
@@ -263,7 +262,7 @@ def tile_moe_bdx_glu_relu_kernel(
 
         make_identity(nc, ident[:])
         nc.sync.dma_start(offs_sb[:], offs)
-        load_saved(1, 0, 0, EARLY)
+        load_saved(1, 0, 0, CHUNK, slice(0, 1))
         load_scales()
         load_dy(0)
         load_dy(1)
@@ -272,7 +271,7 @@ def tile_moe_bdx_glu_relu_kernel(
         nc.sync.dma_start(gate_col[:], gate[0:1, :].rearrange("o (e p i) -> p (o e) i", e=E, i=X4))
         load_dy(3)
         load_w2(0)
-        load_saved(1, 0, EARLY, CHUNK)
+        load_saved(1, 0, 0, CHUNK, slice(1, X4))
         load_saved(1, 0, CHUNK, C)
         load_saved(1, 1)
         load_saved(3, 0)
@@ -295,7 +294,7 @@ def tile_moe_bdx_glu_relu_kernel(
         nc.sync.dma_start(pos1_sb[:], pos1)
         nc.sync.dma_start(pos2_sb[:], pos2)
 
-        relu_a1(0, 0, EARLY)
+        relu_a1(0, 0, CHUNK, slice(0, 1))
         spread_gate(0, "gate_bank")
         spread_gate(1, "dx_bank0")
         deal_scales()
@@ -309,23 +308,23 @@ def tile_moe_bdx_glu_relu_kernel(
             sort_scales(nc.gpsimd, first_rows[:, h], first_raw[:, h])
         gather(0, X4 - 1)
         gather(1, X4 - 1, on_vector=True)
+        gather(2, X4 - 1)
         sort_words(0)
         for k in range(2):
-            g_woven[k] = placed([P, X4 * CHUNK], BF16, f"g_woven{k}", DA + 4 + 2 * k)
+            g_woven[k] = placed([P, X4 * CHUNK], BF16, f"g_woven{k}", DA + 2 - 3 * k)
             g_codes[k] = held_codes(f"g{k}", CHUNK)
         gate_chunk(nc.vector, 0, gate_bank[0])
         gate_chunk(nc.vector, 1, gate_bank[0], 0, P)
         quantise(g_woven[0][:], g_codes[0][0][:], g_codes[0][1][:])
         gate_chunk(nc.vector, 1, gate_bank[0], P, CHUNK)
         quantise(g_woven[1][:], g_codes[1][0][:], g_codes[1][1][:])
-        relu_a1(0, EARLY, CHUNK)
-        gather(2, X4 - 1)
+        relu_a1(0, 0, CHUNK, slice(1, X4))
         nc.scalar.copy(gates_sb[:], gate_bank[1][:, :CHUNK])
         relu_a1(0, CHUNK, C)
         sort_words(1)
         for n in range(SB):
             first_product(n)
-        g_woven[2] = placed([P, X4 * CHUNK], BF16, "g_woven2", DA + 5)
+        g_woven[2] = placed([P, X4 * CHUNK], BF16, "g_woven2", DA)
         gate_chunk(nc.gpsimd, 2, gates_sb)
 
         for h in range(HALVES):
@@ -348,9 +347,16 @@ def tile_moe_bdx_glu_relu_kernel(
                 dhm[h] = placed([P, X4, C], F32, f"dhm{h}", MASKED + 8 * (h % 2))
             else:
                 dhm[h] = placed([P, X4 * C], BF16, f"dhm{h}", MASKED + 8 * (h % 2))
-            da[h] = placed([P, 2 if h else 1, X4 * C], BF16, f"da{h}", DA)
+            if h == 0:
+                da3[h] = placed([P, X4 * C], BF16, "da3_0", DA - 4)[:]
+            elif k < CHUNKS:
+                da = placed([P, 2 * X4 * C], BF16, f"da{h}", DA)
+                da3[h], da1 = da[:, : X4 * C], da[:, X4 * C :]
+            else:
+                da3[h] = placed([P, X4 * C], BF16, f"da3_{h}", DA)[:]
+                da1 = placed([P, X4 * C], BF16, f"da1_{h}", DA + 4)[:]
             if h:
-                make_da1(nc.gpsimd, h - 1, da[h][:, 1, :])
+                make_da1(nc.gpsimd, h - 1, da1)
             for pair in range(2):
                 m = n + 2 * pair
                 first, second = (m + 1, m) if m else (m, m + 1)
@@ -365,14 +371,18 @@ def tile_moe_bdx_glu_relu_kernel(
                     first_product(n + SB)
                     first_product(n + SB + 1)
             if h == 0:
-                words, scales = held_codes("da0", C)
-                quantise(da[0][:, 0, :], words[:], scales[:])
-                da3_codes[0] = (words[:], scales[:])
                 g_codes[2] = held_codes("g2", CHUNK)
                 quantise(g_woven[2][:], g_codes[2][0][:], g_codes[2][1][:])
+                words, scales = placed_codes("da0", C, PLANES)
+                quantise(da3[0], words[:], scales[:])
+                da3_codes[0] = (words[:], scales[:])
             else:
                 words, scales = placed_codes(f"da{h}", 2 * C, a_place(3, h - 1))
-                quantise(da[h][:].rearrange("p w j -> p (w j)"), words[:], scales[:])
+                if gated:
+                    quantise(da[:], words[:], scales[:])
+                else:
+                    quantise(da1, words[:, C:], scales[:, C:])
+                    quantise(da3[h], words[:, :C], scales[:, :C])
                 da3_codes[h] = (words[:, :C], scales[:, :C])
                 da1_codes[h - 1] = (words[:, C:], scales[:, C:])
                 if gated:
@@ -387,7 +397,7 @@ def tile_moe_bdx_glu_relu_kernel(
                     copy_dx(e - 1)
             else:
                 first_half = [(0, da3_codes[h - 1]), (1, da1_codes[h - 1])]
-                for place, (w, codes) in enumerate(first_half if e else first_half[::-1]):
+                for place, (w, codes) in enumerate(first_half if e == E - 1 else first_half[::-1]):
                     second_pass(w, h - 1, codes, opens=place == 0)
                 second_pass(0, h, da3_codes[h])
 

@@ -102,11 +102,10 @@ def tile_moe_bdx_glu_relu_kernel(
             for g in range(NG):
                 nc.sync.dma_start(w2_sc_raw[g : P // 2 : NG, :].bitcast(I32), by_half[g][:, DIRECT // NG :])
 
-        def load_w31_scales():
-            for n, scales in enumerate((w3_scales, w1_scales)):
-                rows = scales.bitcast(I32).rearrange("e s f i -> f (e s) i")
-                for q in range(4):
-                    nc.sync.dma_start(w31_rows[32 * q : 32 * q + 4, n].bitcast(I32), rows[4 * q : 4 * q + 4])
+        def load_w31_scales(n):
+            rows = (w3_scales, w1_scales)[n].bitcast(I32).rearrange("e s f i -> f (e s) i")
+            for q in range(4):
+                nc.sync.dma_start(w31_rows[32 * q : 32 * q + 4, n].bitcast(I32), rows[4 * q : 4 * q + 4])
 
         def load_saved(which, h, lo=0, hi=C, planes=slice(0, X4)):
             e, g = divmod(h, NG)
@@ -228,21 +227,21 @@ def tile_moe_bdx_glu_relu_kernel(
                 woven(run), by_lines(dh[n][:]), by_lines(kept[h][:, :, P * s : P * (s + 1)]), ALU.mult
             )
 
-        def make_da1(engine, h, into):
+        def make_da1(engine, h, into, run=slice(0, X4 * C)):
             if h < MASK_LAST_FROM:
                 engine.tensor_tensor(woven(into), by_lines(dhm[h][:]), by_lines(saved[3, h][:]), ALU.mult)
             else:
-                engine.tensor_tensor(into, dhm[h][:], step[h][:], ALU.mult)
+                engine.tensor_tensor(into, dhm[h][:, run], step[h][:, run], ALU.mult)
 
-        def second_pass(n, h, codes, opens=False):
+        def second_pass(n, h, codes, opens=False, lo=0, hi=C):
             e, g = divmod(h, NG)
             words, scales = codes
-            closes = g == NG - 1 and n == 1
+            closes = g == NG - 1 and n == 1 and hi == C
             for kb in range(KB):
                 if opens:
                     dx_bank[kb] = dx_banks.tile([P, C], F32, name=f"dx_bank{kb}")
                 nc.tensor.matmul_mx(
-                    out=dx_bank[kb][:],
+                    out=dx_bank[kb][:, lo:hi],
                     lhsT=(w3_w, w1_w)[n][:, h, 2 * P * kb : 2 * P * (kb + 1)].bitcast(E2M1),
                     lhsT_scale=w31_rows[:, n, h, P * kb : P * (kb + 1)],
                     rhs=words.bitcast(E5M2),
@@ -276,8 +275,9 @@ def tile_moe_bdx_glu_relu_kernel(
         load_saved(1, 1)
         load_saved(3, 0)
         load_w2(1)
-        load_w31_scales()
+        load_w31_scales(1)
         load_saved(1, 2)
+        load_w31_scales(0)
         load_w13(0, NG)
         for h in range(1, MASK_LAST_FROM):
             load_saved(3, h)
@@ -357,19 +357,18 @@ def tile_moe_bdx_glu_relu_kernel(
                 da1 = placed([P, X4 * C], BF16, f"da1_{h}", DA + 4)[:]
             if h:
                 make_da1(nc.gpsimd, h - 1, da1)
-            for pair in range(2):
-                m = n + 2 * pair
-                first, second = (m + 1, m) if m else (m, m + 1)
-                start_da1(first)
-                if pair == 1 and gated:
+            for place, s in enumerate((3, 0, 1, 2) if g else (1, 0, 3, 2) if h else (0, 1, 3, 2)):
+                mask_first = place == 0 and h in (0, HALVES - 1)
+                opening, following = (start_da1, make_da3) if mask_first else (make_da3, start_da1)
+                opening(n + s)
+                if place == 2 and gated:
                     g_woven[k] = placed([P, X4 * CHUNK], BF16, f"g_woven{k}", WOVEN)
                     gate_chunk(nc.vector, k, gate_bank[k // 2])
-                make_da3(first)
-                make_da3(second)
-                start_da1(second)
-                if more and pair == 0:
+                following(n + s)
+                if more and place == 0:
                     first_product(n + SB)
-                    first_product(n + SB + 1)
+                if more and place < (1 if g else 3):
+                    first_product(n + SB + 1 + place)
             if h == 0:
                 g_codes[2] = held_codes("g2", CHUNK)
                 quantise(g_woven[2][:], g_codes[2][0][:], g_codes[2][1][:])
@@ -388,7 +387,7 @@ def tile_moe_bdx_glu_relu_kernel(
                 if gated:
                     g_codes[k] = placed_codes(f"g{k}", CHUNK, a_place(3, h - 1) + 5)
                     quantise(g_woven[k][:], g_codes[k][0][:], g_codes[k][1][:])
-            if more:
+            if more and g:
                 first_product(n + SB + 2)
                 first_product(n + SB + 3)
             if g == 0:
@@ -403,10 +402,14 @@ def tile_moe_bdx_glu_relu_kernel(
 
         last = HALVES - 1
         da1_last = placed([P, X4 * C], BF16, "da1_last", a_place(1, 4))
-        make_da1(nc.vector, last, da1_last[:])
         words, scales = placed_codes("da1_last", C, a_place(1, 5))
-        quantise(da1_last[:], words[:], scales[:])
-        second_pass(1, last, (words[:], scales[:]))
+        for lo in (0, CHUNK):
+            run = slice(X4 * lo, X4 * (lo + CHUNK))
+            make_da1(nc.vector, last, da1_last[:, run], run)
+        for lo in (0, CHUNK):
+            hi = lo + CHUNK
+            quantise(da1_last[:, X4 * lo : X4 * hi], words[:, lo:hi], scales[:, lo:hi])
+            second_pass(1, last, (words[:, lo:hi], scales[:, lo:hi]), lo=lo, hi=hi)
         copy_dx(E - 1)
 
         firsts = [placed([P, T], F32, f"first{kb}", DY + 4 * kb) for kb in range(KB)]

from contextlib import ExitStack

import concourse.mybir as mybir
from concourse.masks import make_identity

K, T, E, C, H, N = 256, 1024, 4, 512, 1024, 512
S = E * C
P = 128
X4 = 4
NG = H // 512
SB = C // P
KB = K // P
HALVES = E * NG
CHUNK = 2 * P
CHUNKS = S // CHUNK
MASK_LAST_FROM = 5
DIRECT = HALVES // 2
PIECE = 256

F32 = mybir.dt.float32
BF16 = mybir.dt.bfloat16
U32 = mybir.dt.uint32
I32 = mybir.dt.int32
U16 = mybir.dt.uint16
U8 = mybir.dt.uint8
E5M2 = mybir.dt.float8_e5m2_x4
E2M1 = mybir.dt.float4_e2m1fn_x4
ALU = mybir.AluOpType
ACT = mybir.ActivationFunctionType

FLOPS = 2 * S * N * H + 2 * 2 * S * H * K
BYTES = 4 * (N * T + 2 * H * S + S + K * T) + E * (N * H + 2 * H * K) // 2 + E * (N * H + 2 * H * K) // 32 + 2 * 128 * 256

DY = 16 * HALVES
MASKED = DY + 16
PLANES = MASKED + 16
DA = PLANES + 8
WOVEN = DA + 8


def a_place(which, h):
    return 16 * h + (0 if which == 1 else 8)


def by_lines(planes):
    return planes.rearrange("p t (c i) -> p c t i", i=4)


def woven(flat):
    return flat.rearrange("p (c i t) -> p c t i", i=4, t=X4)


def tile_moe_bdx_glu_relu_kernel(
    tc, dyT, a1, a3, w2_words, w2_scales, w1_words, w1_scales, w3_words, w3_scales, gate, offs, pos1, pos2, out
):
    nc = tc.nc
    with ExitStack() as ctx:
        held = ctx.enter_context(tc.tile_pool(name="held", bufs=1))
        arena = ctx.enter_context(tc.tile_pool(name="arena", bufs=1))
        dh_banks = ctx.enter_context(tc.psum_pool(name="dh_banks", bufs=5))
        dx_banks = ctx.enter_context(tc.psum_pool(name="dx_banks", bufs=1))

        def placed(shape, dtype, name, kib):
            return arena.tile(shape, dtype, name=name, offset=int(1024 * kib), align_bytes=64)

        offs_sb = held.tile([P, S // 16], U16, name="offs_sb")
        pos1_sb = held.tile([P, T // 16], U16, name="pos1_sb")
        pos2_sb = held.tile([P, T // 16], U16, name="pos2_sb")
        w2_sc_raw = held.tile([P, 512], U8, name="w2_sc_raw")
        spread = held.tile([P, 512], U8, name="spread")
        late_rows = held.tile([P, HALVES - DIRECT, 512], U8, name="late_rows", align_bytes=64)
        w31_rows = held.tile([P, 2, HALVES, K], U8, name="w31_rows", align_bytes=64)
        first_raw = held.tile([P, DIRECT, 512], U8, name="first_raw")
        first_rows = held.tile([P, DIRECT, 512], U8, name="first_rows", align_bytes=64)
        w1_w = held.tile([P, E * NG, 2 * K], U8, name="w1_w", align_bytes=64)
        w3_w = held.tile([P, E * NG, 2 * K], U8, name="w3_w", align_bytes=64)
        ident = held.tile([P, P], F32, name="ident")
        gate_col = held.tile([P, E, X4], F32, name="gate_col")
        gates_sb = held.tile([P, CHUNK], F32, name="gates_sb")
        nc.gpsimd.memset(first_raw[:].rearrange("p h i -> p (h i)").bitcast(I32), 0)
        nc.vector.memset(w31_rows[:].rearrange("p w h i -> p (w h i)").bitcast(I32), 0)
        nc.vector.memset(w2_sc_raw[P // 2 :, :].bitcast(I32), 0)
        nc.vector.memset(late_rows[:].rearrange("p h i -> p (h i)").bitcast(I32), 0)


        dy, dx = [], []
        w2_raw, w2_w, saved, gate_bank = {}, {}, {}, {}
        g_planes, g_woven, g_codes = {}, {}, {}
        kept = {}
        dh, dhm, step, da3, da3_codes, da1_codes, dx_bank = {}, {}, {}, {}, {}, {}, {}

        def load_dy(t):
            dy.append(placed([P, T], F32, f"dy{t}", DY + 4 * t))
            nc.sync.dma_start(dy[t][:], dyT.rearrange("(p t) s -> t p s", t=X4)[t])

        def load_w2(e):
            w2_raw[e] = held.tile([P, 2 * H], U8, name=f"w2_raw{e}")
            nc.sync.dma_start(w2_raw[e][:].bitcast(I32), w2_words[e, 0].bitcast(I32))

        def load_scales():
            by_half = w2_scales.bitcast(I32).rearrange("e s f (g i) -> g f (e s) i", g=NG)
            for g in range(NG):
                nc.sync.dma_start(w2_sc_raw[g : P // 2 : NG, :].bitcast(I32), by_half[g][:, DIRECT // NG :])

        def load_w31_scales(n):
            rows = (w3_scales, w1_scales)[n].bitcast(I32).rearrange("e s f i -> f (e s) i")
            for q in range(4):
                nc.sync.dma_start(w31_rows[32 * q : 32 * q + 4, n].bitcast(I32), rows[4 * q : 4 * q + 4])

        def load_saved(which, h, lo=0, hi=C, planes=slice(0, X4)):
            e, g = divmod(h, NG)
            if (which, h) not in saved:
                saved[which, h] = placed([P, X4, C], F32, f"a{which}_{h}", a_place(which, h))
            rows = (a1 if which == 1 else a3)[512 * g : 512 * (g + 1), C * e + lo : C * e + hi]
            nc.sync.dma_start(saved[which, h][:, planes, lo:hi], rows.rearrange("(p t) s -> p t s", t=X4)[:, planes])

        def load_w13(lo, hi):
            for w, words in ((w3_w, w3_words), (w1_w, w1_words)):
                by_pass = words.bitcast(I32).rearrange("e s p k -> p (e s) k")
                nc.sync.dma_start(w[:, lo:hi].bitcast(I32), by_pass[:, lo:hi])

        def sort_words(h):
            e, g = divmod(h, NG)
            w2_w[h] = held.tile([P, H], U8, name=f"w2_w{h}", align_bytes=64)
            nc.scalar.copy(
                w2_w[h][:].bitcast(U16).rearrange("p (t m) -> p t m", t=X4),
                w2_raw[e][:, H * g : H * (g + 1)].bitcast(U16).rearrange("p (m t) -> p t m", t=X4),
            )

        def sort_scales(engine, into, raw):
            engine.tensor_copy(into.rearrange("p (t m) -> p t m", t=X4), raw.rearrange("p (m t) -> p t m", t=X4))

        def load_first_scales():
            rows = w2_scales.bitcast(I32).rearrange("e s f i -> f (e s) i")
            for q in range(4):
                into = first_raw[32 * q : 32 * q + 4].rearrange("p (e g) i -> p e (g i)", g=NG)
                nc.sync.dma_start(into.bitcast(I32), rows[4 * q : 4 * q + 4, : DIRECT // NG])

        def deal_scales():
            sort_scales(nc.vector, spread[:], w2_sc_raw[:])
            for q in range(4):
                rows = late_rows[32 * q : 32 * q + 4].rearrange("p h i -> p (h i)")
                nc.gpsimd.dma_start(rows.bitcast(I32), spread[16 * q : 16 * (q + 1), :].bitcast(I32))

        def spread_gate(e, bank_name):
            gate_bank[e] = dx_banks.tile([P, C], F32, name=bank_name)
            for i in range(X4):
                nc.tensor.transpose(gate_bank[e][:, i:C:X4], gate_col[:, e, i : i + 1].to_broadcast([P, P]), ident[:])

        def gather(k, t, on_vector=False):
            if t == 0:
                place = MASKED + 8 + 4 * k if k < 3 else a_place(1, k - 2)
                g_planes[k] = placed([P, X4, CHUNK], F32, f"g_planes{k}", place)
            picked = dy[t][:].indirect(offs_sb[:, CHUNK * k // 16 : CHUNK * (k + 1) // 16])
            if on_vector:
                nc.vector.tensor_copy(g_planes[k][:, t, :], picked)
            else:
                nc.scalar.activation(g_planes[k][:, t, :], picked, ACT.Copy)

        def gate_chunk(engine, k, gates, lo=0, hi=CHUNK):
            start = CHUNK * (k % 2)
            by_slot = gates[:, start + lo : start + hi].rearrange("p (c i) -> p c i", i=4).unsqueeze(2)
            engine.tensor_tensor(
                woven(g_woven[k][:, X4 * lo : X4 * hi]),
                by_lines(g_planes[k][:, :, lo:hi]),
                by_slot.to_broadcast([P, (hi - lo) // 4, X4, 4]),
                ALU.mult,
            )

        def quantise(values, words, scales):
            nc.vector.quantize_mx(out=words.bitcast(E5M2), scales=scales, in_=values)

        def held_codes(name, width):
            words = held.tile([P, width], U32, name=f"{name}_words", align_bytes=64)
            scales = held.tile([P, width], U8, name=f"{name}_scales", align_bytes=64)
            return words, scales

        def placed_codes(name, width, kib):
            words = placed([P, width], U32, f"{name}_words", kib)
            scales = placed([P, width], U8, f"{name}_scales", kib + 4 * width / 1024)
            return words, scales

        def first_product(n):
            h, s = divmod(n, SB)
            e, g = divmod(h, NG)
            k, r = divmod(SB * e + s, 2)
            words, scales = g_codes[k]
            w2_rows = first_rows[:, h] if h < DIRECT else late_rows[:, h - DIRECT]
            dh[n] = dh_banks.tile([P, X4, P], F32, name="dh_bank")
            for t in range(X4):
                nc.tensor.matmul_mx(
                    out=dh[n][:, t, :],
                    lhsT=w2_w[h][:, 2 * P * t : 2 * P * (t + 1)].bitcast(E2M1),
                    lhsT_scale=w2_rows[:, P * t : P * (t + 1)],
                    rhs=words[:, P * r : P * (r + 1)].bitcast(E5M2),
                    rhs_scale=scales[:, P * r : P * (r + 1)],
                    start=True,
                    stop=True,
                )

        def relu_a1(h, lo=0, hi=C, planes=slice(0, X4)):
            if h:
                kept[h] = placed([P, X4, C], F32, f"kept{h}", a_place(1, h - 2) if h > 1 else WOVEN + 2)
            else:
                kept[h] = saved[1, h]
            nc.scalar.activation(kept[h][:, planes, lo:hi], saved[1, h][:, planes, lo:hi], ACT.Relu)

        def step_a1(h):
            step[h] = placed([P, X4 * C], BF16, f"step{h}", a_place(1, h - 4) + 4)
            nc.scalar.activation(woven(step[h][:]), by_lines(kept[h][:]), ACT.Sign)

        def start_da1(n):
            h, s = divmod(n, SB)
            slots = slice(P * s, P * (s + 1))
            if h < MASK_LAST_FROM:
                nc.vector.scalar_tensor_tensor(
                    dhm[h][:, :, slots], kept[h][:, :, slots], 0.0, dh[n][:], ALU.is_gt, ALU.mult
                )
            else:
                run = dhm[h][:, X4 * P * s : X4 * P * (s + 1)]
                nc.vector.tensor_tensor(woven(run), by_lines(dh[n][:]), by_lines(saved[3, h][:, :, slots]), ALU.mult)

        def make_da3(n):
            h, s = divmod(n, SB)
            run = da3[h][:, X4 * P * s : X4 * P * (s + 1)]
            nc.vector.tensor_tensor(
                woven(run), by_lines(dh[n][:]), by_lines(kept[h][:, :, P * s : P * (s + 1)]), ALU.mult
            )

        def make_da1(engine, h, into, run=slice(0, X4 * C)):
            if h < MASK_LAST_FROM:
                engine.tensor_tensor(woven(into), by_lines(dhm[h][:]), by_lines(saved[3, h][:]), ALU.mult)
            else:
                engine.tensor_tensor(into, dhm[h][:, run], step[h][:, run], ALU.mult)

        def second_pass(n, h, codes, opens=False, lo=0, hi=C):
            e, g = divmod(h, NG)
            words, scales = codes
            closes = g == NG - 1 and n == 1 and hi == C
            for kb in range(KB):
                if opens:
                    dx_bank[kb] = dx_banks.tile([P, C], F32, name=f"dx_bank{kb}")
                nc.tensor.matmul_mx(
                    out=dx_bank[kb][:, lo:hi],
                    lhsT=(w3_w, w1_w)[n][:, h, 2 * P * kb : 2 * P * (kb + 1)].bitcast(E2M1),
                    lhsT_scale=w31_rows[:, n, h, P * kb : P * (kb + 1)],
                    rhs=words.bitcast(E5M2),
                    rhs_scale=scales,
                    start=opens,
                    stop=closes,
                )

        def copy_dx(e):
            for kb in range(KB):
                if e == 0:
                    dx.append(placed([P, S], F32, f"dx{kb}", a_place(1, 0) if kb else PLANES))
                if e == E - 1 and kb == 1:
                    nc.vector.tensor_copy(dx[kb][:, C * e : C * (e + 1)], dx_bank[kb][:])
                else:
                    nc.scalar.copy(dx[kb][:, C * e : C * (e + 1)], dx_bank[kb][:])

        make_identity(nc, ident[:])
        nc.sync.dma_start(offs_sb[:], offs)
        load_saved(1, 0, 0, CHUNK, slice(0, 1))
        load_scales()
        load_dy(0)
        load_dy(1)
        load_first_scales()
        load_dy(2)
        nc.sync.dma_start(gate_col[:], gate[0:1, :].rearrange("o (e p i) -> p (o e) i", e=E, i=X4))
        load_dy(3)
        load_w2(0)
        load_saved(1, 0, 0, CHUNK, slice(1, X4))
        load_saved(1, 0, CHUNK, C)
        load_saved(1, 1)
        load_saved(3, 0)
        load_w2(1)
        load_w31_scales(1)
        load_saved(1, 2)
        load_w31_scales(0)
        load_w13(0, NG)
        for h in range(1, MASK_LAST_FROM):
            load_saved(3, h)
            if h in (1, 3):
                load_w2(h // 2 + 2)
            if h == 2:
                load_w13(NG, E * NG)
            if h + 2 <= MASK_LAST_FROM:
                load_saved(1, h + 2)
        for h in range(MASK_LAST_FROM, HALVES):
            if h > MASK_LAST_FROM:
                load_saved(1, h)
            load_saved(3, h)
        nc.sync.dma_start(pos1_sb[:], pos1)
        nc.sync.dma_start(pos2_sb[:], pos2)

        relu_a1(0, 0, CHUNK, slice(0, 1))
        spread_gate(0, "gate_bank")
        spread_gate(1, "dx_bank0")
        deal_scales()
        for t in range(X4 - 1):
            gather(0, t)
            gather(1, t, on_vector=True)
            gather(2, t)
            if t:
                sort_scales(nc.vector, first_rows[:, t - 1], first_raw[:, t - 1])
        for h in range(NG, DIRECT):
            sort_scales(nc.gpsimd, first_rows[:, h], first_raw[:, h])
        gather(0, X4 - 1)
        gather(1, X4 - 1, on_vector=True)
        gather(2, X4 - 1)
        sort_words(0)
        for k in range(2):
            g_woven[k] = placed([P, X4 * CHUNK], BF16, f"g_woven{k}", DA + 2 - 3 * k)
            g_codes[k] = held_codes(f"g{k}", CHUNK)
        gate_chunk(nc.vector, 0, gate_bank[0])
        gate_chunk(nc.vector, 1, gate_bank[0], 0, P)
        quantise(g_woven[0][:], g_codes[0][0][:], g_codes[0][1][:])
        gate_chunk(nc.vector, 1, gate_bank[0], P, CHUNK)
        quantise(g_woven[1][:], g_codes[1][0][:], g_codes[1][1][:])
        relu_a1(0, 0, CHUNK, slice(1, X4))
        nc.scalar.copy(gates_sb[:], gate_bank[1][:, :CHUNK])
        relu_a1(0, CHUNK, C)
        sort_words(1)
        for n in range(SB):
            first_product(n)
        g_woven[2] = placed([P, X4 * CHUNK], BF16, "g_woven2", DA)
        gate_chunk(nc.gpsimd, 2, gates_sb)

        for h in range(HALVES):
            e, g = divmod(h, NG)
            k, n = h + 2, SB * h
            more = h + 1 < HALVES
            gated = 3 <= k < CHUNKS
            if more:
                relu_a1(h + 1)
            if k + 1 < CHUNKS:
                for t in range(X4):
                    gather(k + 1, t)
            if h + 2 < HALVES:
                sort_words(h + 2)
            if MASK_LAST_FROM <= h + 1 < HALVES:
                step_a1(h + 1)
            if g == 0 and 4 <= k < CHUNKS:
                spread_gate(e + 1, "gate_bank")
            if h < MASK_LAST_FROM:
                dhm[h] = placed([P, X4, C], F32, f"dhm{h}", MASKED + 8 * (h % 2))
            else:
                dhm[h] = placed([P, X4 * C], BF16, f"dhm{h}", MASKED + 8 * (h % 2))
            if h == 0:
                da3[h] = placed([P, X4 * C], BF16, "da3_0", DA - 4)[:]
            elif k < CHUNKS:
                da = placed([P, 2 * X4 * C], BF16, f"da{h}", DA)
                da3[h], da1 = da[:, : X4 * C], da[:, X4 * C :]
            else:
                da3[h] = placed([P, X4 * C], BF16, f"da3_{h}", DA)[:]
                da1 = placed([P, X4 * C], BF16, f"da1_{h}", DA + 4)[:]
            if h:
                make_da1(nc.gpsimd, h - 1, da1)
            for place, s in enumerate((3, 0, 1, 2) if g else (1, 0, 3, 2) if h else (0, 1, 3, 2)):
                mask_first = place == 0 and h in (0, HALVES - 1)
                opening, following = (start_da1, make_da3) if mask_first else (make_da3, start_da1)
                opening(n + s)
                if place == 2 and gated:
                    g_woven[k] = placed([P, X4 * CHUNK], BF16, f"g_woven{k}", WOVEN)
                    gate_chunk(nc.vector, k, gate_bank[k // 2])
                following(n + s)
                if more and place == 0:
                    first_product(n + SB)
                if more and place < (1 if g else 3):
                    first_product(n + SB + 1 + place)
            if h == 0:
                g_codes[2] = held_codes("g2", CHUNK)
                quantise(g_woven[2][:], g_codes[2][0][:], g_codes[2][1][:])
                words, scales = placed_codes("da0", C, PLANES)
                quantise(da3[0], words[:], scales[:])
                da3_codes[0] = (words[:], scales[:])
            else:
                words, scales = placed_codes(f"da{h}", 2 * C, a_place(3, h - 1))
                if gated:
                    quantise(da[:], words[:], scales[:])
                else:
                    quantise(da1, words[:, C:], scales[:, C:])
                    quantise(da3[h], words[:, :C], scales[:, :C])
                da3_codes[h] = (words[:, :C], scales[:, :C])
                da1_codes[h - 1] = (words[:, C:], scales[:, C:])
                if gated:
                    g_codes[k] = placed_codes(f"g{k}", CHUNK, a_place(3, h - 1) + 5)
                    quantise(g_woven[k][:], g_codes[k][0][:], g_codes[k][1][:])
            if more and g:
                first_product(n + SB + 2)
                first_product(n + SB + 3)
            if g == 0:
                if h:
                    second_pass(1, h - 1, da1_codes[h - 1])
                    copy_dx(e - 1)
            else:
                first_half = [(0, da3_codes[h - 1]), (1, da1_codes[h - 1])]
                for place, (w, codes) in enumerate(first_half if e == E - 1 else first_half[::-1]):
                    second_pass(w, h - 1, codes, opens=place == 0)
                second_pass(0, h, da3_codes[h])

        last = HALVES - 1
        da1_last = placed([P, X4 * C], BF16, "da1_last", a_place(1, 4))
        words, scales = placed_codes("da1_last", C, a_place(1, 5))
        for lo in (0, CHUNK):
            run = slice(X4 * lo, X4 * (lo + CHUNK))
            make_da1(nc.vector, last, da1_last[:, run], run)
        for lo in (0, CHUNK):
            hi = lo + CHUNK
            quantise(da1_last[:, X4 * lo : X4 * hi], words[:, lo:hi], scales[:, lo:hi])
            second_pass(1, last, (words[:, lo:hi], scales[:, lo:hi]), lo=lo, hi=hi)
        copy_dx(E - 1)

        firsts = [placed([P, T], F32, f"first{kb}", DY + 4 * kb) for kb in range(KB)]
        totals = [placed([P, T], F32, f"total{kb}", DY + 8 + 4 * kb) for kb in range(KB)]
        second = placed([P, PIECE], F32, "second", a_place(1, 2))

        def entries(pos_sb, lo):
            return pos_sb[:, lo // 16 : (lo + PIECE) // 16]

        pieces = [(kb, lo) for kb in range(KB) for lo in range(0, T, PIECE)]
        nc.vector.tensor_copy(second[:], dx[1][:].indirect(entries(pos2_sb, T - PIECE)))
        for kb, lo in pieces:
            nc.scalar.activation(firsts[kb][:, lo : lo + PIECE], dx[kb][:].indirect(entries(pos1_sb, lo)), ACT.Copy)
        for kb, lo in pieces:
            hi = lo + PIECE
            other = second[:] if (kb, lo) == pieces[-1] else dx[kb][:].indirect(entries(pos2_sb, lo))
            nc.vector.tensor_tensor(totals[kb][:, lo:hi], other, firsts[kb][:, lo:hi], ALU.add)
            nc.sync.dma_start(out[P * kb : P * (kb + 1), lo:hi], totals[kb][:, lo:hi])
